import numpy as np
import ml_dtypes


def mxq(x, axis, fmt="e4m3"):
    dtype, down = {"e4m3": (ml_dtypes.float8_e4m3fn, 7), "e5m2": (ml_dtypes.float8_e5m2, 14)}[fmt]
    v = np.moveaxis(np.asarray(x, np.float32).astype(ml_dtypes.bfloat16).astype(np.float64), axis, -1)
    blocks = v.reshape(v.shape[:-1] + (-1, 32))
    amax = np.abs(blocks).max(-1, keepdims=True)
    byte = np.maximum(np.where(amax > 0, np.frexp(amax)[1] - 1 + 127, 0) - down, 1)
    scale = np.exp2(byte - 127.0)
    codes = (blocks / scale).astype(np.float32).astype(dtype).astype(np.float64)
    return np.moveaxis((codes * scale).reshape(v.shape), -1, axis)


WIDE = False


def mx_kscale(k):
    if not WIDE:
        return np.ones(k)
    levels = np.array([24, -24, 12, -12, 0])
    if k % 512:
        return np.exp2(np.random.permutation(np.resize(levels, k // 32))).repeat(32)
    a = np.empty((k // 512, 16))
    for p in range(k // 512):
        a[p, :8] = np.random.permutation(np.resize(levels, 8))
        for g in range(8):
            far = levels[np.abs(levels - a[p, g]) >= 10]
            a[p, g + 8] = far[np.random.randint(len(far))]
    return np.exp2(a.ravel()).repeat(32)


def f64(x):
    return np.asarray(x).astype(np.float64)


def striped(idx):
    return np.tile(idx.reshape(-1, 16).T, (8, 1)).astype(np.uint16)


def unstriped(offs):
    return offs[:16].T.reshape(-1).astype(np.int64)


E2M1 = np.array([0.0, 0.5, 1.0, 1.5, 2.0, 3.0, 4.0, 6.0, -0.0, -0.5, -1.0, -1.5, -2.0, -3.0, -4.0, -6.0])


def pack_weight(w, fmt):
    k, n = w.shape
    w = f64(np.asarray(w, np.float32).astype(ml_dtypes.bfloat16)).reshape(k // 32, 32, n)
    amax = np.abs(w).max(1)
    if fmt == "e4m3":
        byte = np.frexp(amax)[1] - 1 + 127 - 7
    else:
        mant, ex = np.frexp(amax / 6.0)
        byte = np.where(mant > 0.5, ex, ex - 1) + 127
    byte = np.clip(np.where(amax > 0, byte, 1), 1, 254)
    scaled = (w * np.exp2(127.0 - byte)[:, None, :]).reshape(k, n).astype(np.float32)
    by_word = np.ascontiguousarray(scaled.reshape(k // 512, 128, 4, n).transpose(0, 1, 3, 2))
    if fmt == "e4m3":
        words = by_word.astype(ml_dtypes.float8_e4m3fn).view(np.uint8)
    else:
        c = by_word.astype(ml_dtypes.float4_e2m1fn).view(np.uint8) & 0xF
        words = (c[..., 0::2] | (c[..., 1::2] << 4)).reshape(k // 512, 128, 2 * n)
    return np.ascontiguousarray(words), np.ascontiguousarray(byte.astype(np.uint8).reshape(k // 512, 16, n))


def unpack_weight(words, scales, fmt):
    g, _, n = scales.shape
    words = np.ascontiguousarray(words).reshape(g, 128, n, -1)
    if fmt == "e4m3":
        vals = words.view(ml_dtypes.float8_e4m3fn).astype(np.float64)
    else:
        nib = np.empty((g, 128, n, 4), np.uint8)
        nib[..., 0::2] = words & 0xF
        nib[..., 1::2] = words >> 4
        vals = E2M1[nib]
    vals = vals * np.repeat(np.exp2(scales.astype(np.float64) - 127.0), 8, axis=1)[..., None]
    return vals.transpose(0, 1, 3, 2).reshape(g * 512, n)


def pack_table4(v):
    words, scales = pack_weight(v, "e2m1")
    g, t = words.shape[0] // 2, v.shape[1]
    return np.ascontiguousarray(words.reshape(g, 2, 128, t, 2).transpose(0, 2, 3, 1, 4).reshape(g, 128, t, 4)), scales


def unpack_table4(words, scales):
    g, _, t, _ = words.shape
    return unpack_weight(words.reshape(g, 128, t, 2, 2).transpose(0, 3, 1, 2, 4).reshape(2 * g, 128, 2 * t), scales, "e2m1")


K, L, R, N, T, J = 1024, 512, 1024, 256, 2048, 1024


def setup_inputs():
    n = np.random.standard_normal
    s = mx_kscale(K)[:, None]
    s2 = mx_kscale(L)[:, None]
    u = mx_kscale(R)[:, None]
    p_tab = pack_table4(n((K, T)) * s)
    p_tab2 = pack_weight(n((L, T)) * s2, "e4m3")
    p_wb = pack_weight(n((L, R)) / np.sqrt(L) / s2, "e4m3")
    p_en = pack_weight(n((R, N)) / np.sqrt(R) / u, "e4m3")
    return {
        "tab_words": p_tab[0],
        "tab_scales": p_tab[1],
        "tab2_words": p_tab2[0],
        "tab2_scales": p_tab2[1],
        "wa": (n((K, R)) / np.sqrt(K) / s * u.T).astype(np.float32),
        "wb_words": p_wb[0],
        "wb_scales": p_wb[1],
        "en_words": p_en[0],
        "en_scales": p_en[1],
        "offs": striped(np.random.permutation(T)[:J]),
        "offs2": striped(np.random.permutation(T)[:J]),
    }


def reference(tab_words, tab_scales, tab2_words, tab2_scales, wa, wb_words, wb_scales, en_words, en_scales, offs, offs2):
    idx = unstriped(offs)
    idx2 = unstriped(offs2)
    tab_ = unpack_table4(tab_words, tab_scales)[:, idx]
    tab2_ = unpack_weight(tab2_words, tab2_scales, "e4m3")[:, idx2]
    wa_ = mxq(f64(wa), 0, "e4m3")
    wb_ = unpack_weight(wb_words, wb_scales, "e4m3")
    ha = wa_.T @ tab_
    hb = wb_.T @ tab2_
    h = ha * hb
    h_ = mxq(h, 0, "e4m3")
    en_ = unpack_weight(en_words, en_scales, "e4m3")
    y = en_.T @ h_
    return y

@@ -1,0 +1,265 @@
+from contextlib import ExitStack
+
+import concourse.mybir as mybir
+
+K, L, R, N, T, J = 1024, 512, 1024, 256, 2048, 1024
+FLOPS = 2 * J * R * (K + L + N)
+
+F32 = mybir.dt.float32
+BF16 = mybir.dt.bfloat16
+I32 = mybir.dt.int32
+U32 = mybir.dt.uint32
+U16 = mybir.dt.uint16
+U8 = mybir.dt.uint8
+FP8X4 = mybir.dt.float8_e4m3fn_x4
+FP4X4 = mybir.dt.float4_e2m1fn_x4
+MULT = mybir.AluOpType.mult
+
+P = 128
+PACK = 4
+PASS = P * PACK
+QUADS = 4
+HALF = J // 2
+JC = 128
+JB = 256
+CHUNKS = J // JC
+SCORE_RANGES = ((0, 512), (512, 768), (768, 896), (896, 1024))
+
+
+def as_words(dram_pass):
+    return dram_pass.rearrange("p n i -> p (n i)").bitcast(I32)
+
+
+def tile_list_kg_mul_none_kernel(
+    tc, tab_words, tab_scales, tab2_words, tab2_scales, wa, wb_words, wb_scales, en_words, en_scales, offs, offs2, out
+):
+    nc = tc.nc
+    with ExitStack() as ctx:
+        lists = ctx.enter_context(tc.tile_pool(name="lists", bufs=1))
+        keep = ctx.enter_context(tc.tile_pool(name="keep", bufs=1))
+        shared = ctx.enter_context(tc.tile_pool(name="shared", bufs=1))
+        stage = ctx.enter_context(tc.tile_pool(name="stage", bufs=2))
+        psum = ctx.enter_context(tc.psum_pool(name="psum", bufs=3))
+
+        def held(shape, dtype, name):
+            return keep.tile(shape, dtype, name=name, align_bytes=64)
+
+        list2 = lists.tile([P, J // 16], U16, name="list2")
+        list1 = lists.tile([P, J // 16], U16, name="list1")
+
+        tab2_scale_win = shared.tile([P, T], U8, name="tab2_scale_win", offset=4 * R - T // 2, align_bytes=64)
+        tab_scale_win = keep.tile([P, T], U8, name="tab_scale_win", tag="tab_scales_then_words", align_bytes=64)
+        wb_scale_raw = keep.tile([P, R], U8, name="wb_scale_raw", tag="wb_then_en_scale", align_bytes=64)
+        tab_scale = held([P, 2, J], U8, "tab_scale")
+        tab2_scale = held([P, J], U8, "tab2_scale")
+        nc.vector.memset(wb_scale_raw[:].bitcast(I32), 0)
+        nc.vector.memset(tab2_scale_win[0:96, :].bitcast(I32), 0)
+        nc.vector.memset(tab2_scale_win[96:112, :].bitcast(I32), 0)
+        for q in range(2, QUADS):
+            nc.gpsimd.memset(tab_scale_win[32 * q : 32 * q + 24, :].bitcast(I32), 0)
+        nc.gpsimd.memset(tab2_scale[:].bitcast(I32), 0)
+        nc.gpsimd.memset(tab_scale[96:128, :, :].bitcast(I32), 0)
+
+        def load_wa(b, a):
+            raw = stage.tile([P, PACK, PASS], F32, name="wa_raw")
+            rows = wa[a * PASS : (a + 1) * PASS, b * PASS : (b + 1) * PASS]
+            nc.sync.dma_start(raw[:], rows.rearrange("(p i) c -> p i c", i=PACK))
+            return raw
+
+        nc.sync.dma_start(list2[:], offs2)
+        nc.sync.dma_start(tab2_scale_win[112:128, :].bitcast(I32), tab2_scales[0].bitcast(I32))
+        wa_raw = {(0, 0): load_wa(0, 0)}
+        nc.sync.dma_start(list1[:], offs)
+        for q in range(QUADS):
+            nc.sync.dma_start(
+                tab_scale_win[32 * q + 24 : 32 * q + 32, :].bitcast(I32), tab_scales[:, 4 * q : 4 * q + 4, :].bitcast(I32)
+            )
+        wa_raw[0, 1] = load_wa(0, 1)
+        for q in range(QUADS):
+            nc.sync.dma_start(
+                wb_scale_raw[32 * q : 32 * q + 4, :].bitcast(I32), wb_scales[0, 4 * q : 4 * q + 4, :].bitcast(I32)
+            )
+
+        tab2_scale_picked = held([P, J], U8, "tab2_scale_picked")
+        nc.vector.tensor_copy(tab2_scale_picked[:], tab2_scale_win[:].indirect(list2[:]))
+        wb_raw = shared.tile([P, R], I32, name="wb_raw", offset=0, align_bytes=64)
+        nc.sync.dma_start(wb_raw[:], as_words(wb_words[0]))
+        tab2_win = shared.tile([P, T], I32, name="tab2_win", offset=4 * R, align_bytes=64)
+        nc.sync.dma_start(tab2_win[:], as_words(tab2_words[0]))
+        for q in range(QUADS):
+            nc.sync.dma_start(
+                tab2_scale[32 * q : 32 * q + 4, :].bitcast(I32),
+                tab2_scale_picked[112 + 4 * q : 116 + 4 * q, :].bitcast(I32),
+            )
+
+        for q in range(2):
+            nc.vector.memset(tab_scale_win[32 * q : 32 * q + 24, :].bitcast(I32), 0)
+        tab_scale_picked = held([P, J], U8, "tab_scale_picked")
+        nc.vector.tensor_copy(tab_scale_picked[:], tab_scale_win[:].indirect(list1[:]))
+        tab_win = keep.tile([P, T], I32, name="tab_win", tag="tab_scales_then_words", align_bytes=64)
+        nc.sync.dma_start(tab_win[:], as_words(tab_words[0]))
+        for a in range(2):
+            nc.sync.dma_start(tab_scale[0:100, a, :].bitcast(I32), tab_scale_picked[24 + 4 * a : 124 + 4 * a, :].bitcast(I32))
+
+        wa_grouped, wa_codes, wa_scale = {}, {}, {}
+
+        def round_wa(b, a):
+            grouped = held([P, PASS * PACK], BF16, "wa_grouped%d%d" % (b, a))
+            dst = grouped[:].rearrange("p (t m i) -> p m i t", t=PACK, i=PACK)
+            src = wa_raw[b, a][:].rearrange("p i (m t) -> p m i t", t=PACK)
+            for m0 in range(0, P, P // 2):
+                nc.scalar.copy(dst[:, m0 : m0 + P // 2], src[:, m0 : m0 + P // 2])
+            wa_grouped[b, a] = grouped
+
+        def quantise_wa(b, a):
+            wa_codes[b, a] = held([P, PASS], U32, "wa_codes%d%d" % (b, a))
+            wa_scale[b, a] = held([P, PASS], U8, "wa_scale%d%d" % (b, a))
+            nc.vector.quantize_mx(out=wa_codes[b, a][:].bitcast(FP8X4), scales=wa_scale[b, a][:], in_=wa_grouped[b, a][:])
+
+        round_wa(0, 0)
+        quantise_wa(0, 0)
+
+        wb_codes = held([P, R], I32, "wb_codes")
+        wb_scale = held([P, R], U8, "wb_scale")
+        nc.vector.tensor_copy(
+            wb_codes[:].rearrange("p (b t m) -> p b m t", b=2, t=PACK),
+            wb_raw[:].rearrange("p (b m t) -> p b m t", b=2, t=PACK),
+        )
+        nc.vector.tensor_copy(
+            wb_scale[:].rearrange("p (b t m) -> p b t m", b=2, t=PACK),
+            wb_scale_raw[:].rearrange("p (b m t) -> p b t m", b=2, t=PACK),
+        )
+
+        round_wa(0, 1)
+        quantise_wa(0, 1)
+
+        wa_raw[1, 0] = load_wa(1, 0)
+        wa_raw[1, 1] = load_wa(1, 1)
+        en_codes = shared.tile([P, 2, N], I32, name="en_codes", offset=0, align_bytes=64)
+        nc.sync.dma_start(en_codes[:], en_words.rearrange("a p n i -> p a (n i)").bitcast(I32))
+        en_scale = keep.tile([P, 2, N], U8, name="en_scale", tag="wb_then_en_scale", align_bytes=64)
+        nc.gpsimd.memset(en_scale[:].bitcast(I32), 0)
+        for q in range(QUADS):
+            nc.sync.dma_start(
+                en_scale[32 * q : 32 * q + 4, :, :].bitcast(I32),
+                en_scales[:, 4 * q : 4 * q + 4, :].rearrange("a r n -> r a n").bitcast(I32),
+            )
+
+        def half_list(lst, h):
+            return lst[:, h * HALF // 16 : (h + 1) * HALF // 16]
+
+        tab2_codes = []
+        for h in range(2):
+            codes = held([P, HALF], U32, "tab2_codes%d" % h)
+            nc.vector.tensor_copy(codes[:], tab2_win[:].bitcast(U32).indirect(half_list(list2, h)))
+            tab2_codes.append(codes)
+
+        hb_sb = {}
+
+        def project_b(b, g):
+            h, j0 = divmod(g * JB, HALF)
+            hb_sb[b, g] = held([P, 2, JB, 2], F32, "hb%d_%d" % (b, g))
+            for u in range(2):
+                bank = psum.tile([P, 2, JB], F32, name="hb_bank")
+                for e in range(2):
+                    t = 2 * u + e
+                    cols = slice(b * PASS + t * P, b * PASS + (t + 1) * P)
+                    nc.tensor.matmul_mx(
+                        out=bank[:, e, :],
+                        lhsT=wb_codes[:, cols].bitcast(FP8X4),
+                        lhsT_scale=wb_scale[:, cols],
+                        rhs=tab2_codes[h][:, j0 : j0 + JB].bitcast(FP8X4),
+                        rhs_scale=tab2_scale[:, g * JB : (g + 1) * JB],
+                        start=True,
+                        stop=True,
+                    )
+                nc.scalar.copy(hb_sb[b, g][:, u], bank[:].rearrange("p e j -> p j e"))
+
+        for g in range(J // JB):
+            project_b(0, g)
+
+        tab_codes = []
+        for h in range(2):
+            pairs = held([P, HALF], U32, "tab_pairs%d" % h)
+            nc.vector.tensor_copy(pairs[:], tab_win[:].bitcast(U32).indirect(half_list(list1, h)))
+            parted = held([P, 2, 2 * HALF], U8, "tab_codes%d" % h)
+            nc.vector.tensor_copy(parted[:].bitcast(U16), pairs[:].bitcast(U16).rearrange("p (j d) -> p d j", d=2))
+            tab_codes.append(parted)
+
+        h_bf16 = {(b, h): held([P, HALF, PACK], BF16, "h_bf16_%d%d" % (b, h)) for b in range(2) for h in range(2)}
+        h_codes = [held([P, J], U32, "h_codes%d" % b) for b in range(2)]
+        h_scale = [held([P, J], U8, "h_scale%d" % b) for b in range(2)]
+
+        def project_a_and_join(b, c):
+            bank = psum.tile([P, PACK, JC], F32, name="ha_bank")
+            h, j0 = divmod(c * JC, HALF)
+            for t in range(PACK):
+                cols = slice(t * P, (t + 1) * P)
+                for a in range(2):
+                    nc.tensor.matmul_mx(
+                        out=bank[:, t, :],
+                        lhsT=wa_codes[b, a][:, cols].bitcast(FP8X4),
+                        lhsT_scale=wa_scale[b, a][:, cols],
+                        rhs=tab_codes[h][:, a, 2 * j0 : 2 * (j0 + JC)].bitcast(FP4X4),
+                        rhs_scale=tab_scale[:, a, c * JC : (c + 1) * JC],
+                        start=(a == 0),
+                        stop=(a == 1),
+                    )
+            g, jb = divmod(c * JC, JB)
+            nc.vector.tensor_tensor(
+                h_bf16[b, h][:, j0 : j0 + JC, :].rearrange("p j (u e) -> p j u e", u=2),
+                bank[:].rearrange("p (u e) j -> p j u e", u=2),
+                hb_sb[b, g][:, :, jb : jb + JC, :].rearrange("p u j e -> p j u e"),
+                MULT,
+            )
+
+        def quantise_h(b, lo, hi):
+            h, j0 = divmod(lo, HALF)
+            nc.vector.quantize_mx(
+                out=h_codes[b][:, lo:hi].bitcast(FP8X4),
+                scales=h_scale[b][:, lo:hi],
+                in_=h_bf16[b, h][:, j0 : j0 + hi - lo, :].rearrange("p j t -> p (j t)"),
+            )
+
+        out_rows = out.rearrange("(u p) j -> p u j", p=P)
+
+        def score(lo, hi):
+            width = hi - lo
+            per_bank = min(2, PASS // width)
+            result = held([P, 2, width], F32, "result%d" % lo)
+            for u0 in range(0, 2, per_bank):
+                bank = psum.tile([P, per_bank, width], F32, name="y_bank", bufs=2)
+                for u in range(u0, u0 + per_bank):
+                    cols = slice(u * P, (u + 1) * P)
+                    for b in range(2):
+                        nc.tensor.matmul_mx(
+                            out=bank[:, u - u0, :],
+                            lhsT=en_codes[:, b, cols].bitcast(FP8X4),
+                            lhsT_scale=en_scale[:, b, cols],
+                            rhs=h_codes[b][:, lo:hi].bitcast(FP8X4),
+                            rhs_scale=h_scale[b][:, lo:hi],
+                            start=(b == 0),
+                            stop=(b == 1),
+                        )
+                nc.scalar.copy(result[:, u0 : u0 + per_bank, :], bank[:])
+            nc.sync.dma_start(out_rows[:, :, lo:hi], result[:])
+
+        for c in range(CHUNKS):
+            project_a_and_join(0, c)
+
+        round_wa(1, 0)
+        round_wa(1, 1)
+        quantise_wa(1, 0)
+        quantise_h(0, 0, HALF)
+        quantise_wa(1, 1)
+        quantise_h(0, HALF, J)
+        for g in range(J // JB):
+            project_b(1, g)
+
+        done = {hi // JC: (lo, hi) for lo, hi in SCORE_RANGES}
+        for c in range(CHUNKS + 1):
+            if c < CHUNKS:
+                project_a_and_join(1, c)
+            if c in done:
+                quantise_h(1, *done[c])
+                score(*done[c])

@@ -21,8 +21,8 @@ PASS = P * PACK
 QUADS = 4
 HALF = J // 2
 JC = 128
-JB = 256
 CHUNKS = J // JC
+TAB_RANGES = ((0, 256), (256, 512), (512, 1024))
 SCORE_RANGES = ((0, 512), (512, 768), (768, 896), (896, 1024))
 
 
@@ -47,18 +47,19 @@ def tile_list_kg_mul_none_kernel(
         list2 = lists.tile([P, J // 16], U16, name="list2")
         list1 = lists.tile([P, J // 16], U16, name="list1")
 
+        tab_scale_win = held([P, T], U8, "tab_scale_win")
         tab2_scale_win = shared.tile([P, T], U8, name="tab2_scale_win", offset=4 * R - T // 2, align_bytes=64)
-        tab_scale_win = keep.tile([P, T], U8, name="tab_scale_win", tag="tab_scales_then_words", align_bytes=64)
         wb_scale_raw = keep.tile([P, R], U8, name="wb_scale_raw", tag="wb_then_en_scale", align_bytes=64)
         tab_scale = held([P, 2, J], U8, "tab_scale")
         tab2_scale = held([P, J], U8, "tab2_scale")
-        nc.vector.memset(wb_scale_raw[:].bitcast(I32), 0)
-        nc.vector.memset(tab2_scale_win[0:96, :].bitcast(I32), 0)
-        nc.vector.memset(tab2_scale_win[96:112, :].bitcast(I32), 0)
-        for q in range(2, QUADS):
-            nc.gpsimd.memset(tab_scale_win[32 * q : 32 * q + 24, :].bitcast(I32), 0)
-        nc.gpsimd.memset(tab2_scale[:].bitcast(I32), 0)
         nc.gpsimd.memset(tab_scale[96:128, :, :].bitcast(I32), 0)
+        for q in range(QUADS):
+            engine = nc.vector if q < 3 else nc.gpsimd
+            engine.memset(tab_scale_win[32 * q : 32 * q + 24, :].bitcast(I32), 0)
+        nc.gpsimd.memset(tab2_scale_win[0:96, :].bitcast(I32), 0)
+        nc.gpsimd.memset(tab2_scale_win[96:112, :].bitcast(I32), 0)
+        nc.gpsimd.memset(wb_scale_raw[:].bitcast(I32), 0)
+        nc.gpsimd.memset(tab2_scale[:].bitcast(I32), 0)
 
         def load_wa(b, a):
             raw = stage.tile([P, PACK, PASS], F32, name="wa_raw")
@@ -66,19 +67,26 @@ def tile_list_kg_mul_none_kernel(
             nc.sync.dma_start(raw[:], rows.rearrange("(p i) c -> p i c", i=PACK))
             return raw
 
-        nc.sync.dma_start(list2[:], offs2)
-        nc.sync.dma_start(tab2_scale_win[112:128, :].bitcast(I32), tab2_scales[0].bitcast(I32))
-        wa_raw = {(0, 0): load_wa(0, 0)}
         nc.sync.dma_start(list1[:], offs)
         for q in range(QUADS):
             nc.sync.dma_start(
                 tab_scale_win[32 * q + 24 : 32 * q + 32, :].bitcast(I32), tab_scales[:, 4 * q : 4 * q + 4, :].bitcast(I32)
             )
+        wa_raw = {(0, 0): load_wa(0, 0)}
+        nc.sync.dma_start(list2[:], offs2)
+        nc.sync.dma_start(tab2_scale_win[112:128, :].bitcast(I32), tab2_scales[0].bitcast(I32))
         wa_raw[0, 1] = load_wa(0, 1)
+        tab_win = held([P, T], I32, "tab_win")
+        nc.sync.dma_start(tab_win[:], as_words(tab_words[0]))
         for q in range(QUADS):
             nc.sync.dma_start(
                 wb_scale_raw[32 * q : 32 * q + 4, :].bitcast(I32), wb_scales[0, 4 * q : 4 * q + 4, :].bitcast(I32)
             )
+
+        tab_scale_picked = held([P, J], U8, "tab_scale_picked")
+        nc.vector.tensor_copy(tab_scale_picked[:], tab_scale_win[:].indirect(list1[:]))
+        for a in range(2):
+            nc.sync.dma_start(tab_scale[0:100, a, :].bitcast(I32), tab_scale_picked[24 + 4 * a : 124 + 4 * a, :].bitcast(I32))
 
         tab2_scale_picked = held([P, J], U8, "tab2_scale_picked")
         nc.vector.tensor_copy(tab2_scale_picked[:], tab2_scale_win[:].indirect(list2[:]))
@@ -92,46 +100,78 @@ def tile_list_kg_mul_none_kernel(
                 tab2_scale_picked[112 + 4 * q : 116 + 4 * q, :].bitcast(I32),
             )
 
-        for q in range(2):
-            nc.vector.memset(tab_scale_win[32 * q : 32 * q + 24, :].bitcast(I32), 0)
-        tab_scale_picked = held([P, J], U8, "tab_scale_picked")
-        nc.vector.tensor_copy(tab_scale_picked[:], tab_scale_win[:].indirect(list1[:]))
-        tab_win = keep.tile([P, T], I32, name="tab_win", tag="tab_scales_then_words", align_bytes=64)
-        nc.sync.dma_start(tab_win[:], as_words(tab_words[0]))
-        for a in range(2):
-            nc.sync.dma_start(tab_scale[0:100, a, :].bitcast(I32), tab_scale_picked[24 + 4 * a : 124 + 4 * a, :].bitcast(I32))
-
         wa_grouped, wa_codes, wa_scale = {}, {}, {}
 
         def round_wa(b, a):
-            grouped = held([P, PASS * PACK], BF16, "wa_grouped%d%d" % (b, a))
+            grouped = keep.tile(
+                [P, PASS * PACK], BF16, name="wa_grouped%d%d" % (b, a), tag="bf16_%d%d" % (b, a), align_bytes=64
+            )
             dst = grouped[:].rearrange("p (t m i) -> p m i t", t=PACK, i=PACK)
             src = wa_raw[b, a][:].rearrange("p i (m t) -> p m i t", t=PACK)
-            for m0 in range(0, P, P // 2):
-                nc.scalar.copy(dst[:, m0 : m0 + P // 2], src[:, m0 : m0 + P // 2])
+            for t0 in range(0, PACK, 2):
+                nc.scalar.copy(dst[:, :, :, t0 : t0 + 2], src[:, :, :, t0 : t0 + 2])
             wa_grouped[b, a] = grouped
 
         def quantise_wa(b, a):
-            wa_codes[b, a] = held([P, PASS], U32, "wa_codes%d%d" % (b, a))
+            wa_codes[b, a] = keep.tile(
+                [P, PASS], U32, name="wa_codes%d%d" % (b, a), tag="bf16_%d%d" % (b + 1, a), align_bytes=64
+            )
             wa_scale[b, a] = held([P, PASS], U8, "wa_scale%d%d" % (b, a))
             nc.vector.quantize_mx(out=wa_codes[b, a][:].bitcast(FP8X4), scales=wa_scale[b, a][:], in_=wa_grouped[b, a][:])
 
+        def part_of(lst, lo, hi):
+            return lst[:, lo // 16 : hi // 16]
+
+        tab_codes = {}
+
+        def pick_tab(lo, hi):
+            pairs = keep.tile([P, hi - lo], U32, name="tab_pairs%d" % lo, tag="pairs%d" % lo, align_bytes=64)
+            nc.vector.tensor_copy(pairs[:], tab_win[:].bitcast(U32).indirect(part_of(list1, lo, hi)))
+            parted = held([P, 2, 2 * (hi - lo)], U8, "tab_codes%d" % lo)
+            nc.vector.tensor_copy(parted[:].bitcast(U16), pairs[:].bitcast(U16).rearrange("p (j d) -> p d j", d=2))
+            for j0 in range(lo, hi, JC):
+                tab_codes[j0 // JC] = parted[:, :, 2 * (j0 - lo) : 2 * (j0 - lo + JC)]
+
         round_wa(0, 0)
         quantise_wa(0, 0)
+        round_wa(0, 1)
+        pick_tab(*TAB_RANGES[0])
+        quantise_wa(0, 1)
+        for lo, hi in TAB_RANGES[1:]:
+            pick_tab(lo, hi)
 
-        wb_codes = held([P, R], I32, "wb_codes")
-        wb_scale = held([P, R], U8, "wb_scale")
-        nc.vector.tensor_copy(
-            wb_codes[:].rearrange("p (b t m) -> p b m t", b=2, t=PACK),
-            wb_raw[:].rearrange("p (b m t) -> p b m t", b=2, t=PACK),
-        )
+        ha_sb = {}
+
+        def project_a(b, c):
+            bank = psum.tile([P, PACK, JC], F32, name="ha_bank")
+            for t in range(PACK):
+                cols = slice(t * P, (t + 1) * P)
+                for a in range(2):
+                    nc.tensor.matmul_mx(
+                        out=bank[:, t, :],
+                        lhsT=wa_codes[b, a][:, cols].bitcast(FP8X4),
+                        lhsT_scale=wa_scale[b, a][:, cols],
+                        rhs=tab_codes[c][:, a, :].bitcast(FP4X4),
+                        rhs_scale=tab_scale[:, a, c * JC : (c + 1) * JC],
+                        start=(a == 0),
+                        stop=(a == 1),
+                    )
+            ha_sb[b, c] = held([P, JC, PACK], F32, "ha%d_%d" % (b, c))
+            nc.scalar.copy(ha_sb[b, c][:], bank[:].rearrange("p t j -> p j t"))
+
+        for c in range(CHUNKS):
+            project_a(0, c)
+
+        wb_codes = keep.tile([P, R], I32, name="wb_codes", tag="pairs512", align_bytes=64)
+        wb_scale = keep.tile([P, R], U8, name="wb_scale", tag="pairs256", align_bytes=64)
         nc.vector.tensor_copy(
             wb_scale[:].rearrange("p (b t m) -> p b t m", b=2, t=PACK),
             wb_scale_raw[:].rearrange("p (b m t) -> p b t m", b=2, t=PACK),
         )
-
-        round_wa(0, 1)
-        quantise_wa(0, 1)
+        nc.vector.tensor_copy(
+            wb_codes[:].rearrange("p (b t m) -> p b m t", b=2, t=PACK),
+            wb_raw[:].rearrange("p (b m t) -> p b m t", b=2, t=PACK),
+        )
 
         wa_raw[1, 0] = load_wa(1, 0)
         wa_raw[1, 1] = load_wa(1, 1)
@@ -145,121 +185,100 @@ def tile_list_kg_mul_none_kernel(
                 en_scales[:, 4 * q : 4 * q + 4, :].rearrange("a r n -> r a n").bitcast(I32),
             )
 
-        def half_list(lst, h):
-            return lst[:, h * HALF // 16 : (h + 1) * HALF // 16]
-
         tab2_codes = []
         for h in range(2):
             codes = held([P, HALF], U32, "tab2_codes%d" % h)
-            nc.vector.tensor_copy(codes[:], tab2_win[:].bitcast(U32).indirect(half_list(list2, h)))
+            nc.vector.tensor_copy(codes[:], tab2_win[:].bitcast(U32).indirect(part_of(list2, h * HALF, (h + 1) * HALF)))
             tab2_codes.append(codes)
 
-        hb_sb = {}
+        for a in range(2):
+            round_wa(1, a)
+            quantise_wa(1, a)
 
-        def project_b(b, g):
-            h, j0 = divmod(g * JB, HALF)
-            hb_sb[b, g] = held([P, 2, JB, 2], F32, "hb%d_%d" % (b, g))
-            for u in range(2):
-                bank = psum.tile([P, 2, JB], F32, name="hb_bank")
-                for e in range(2):
-                    t = 2 * u + e
-                    cols = slice(b * PASS + t * P, b * PASS + (t + 1) * P)
-                    nc.tensor.matmul_mx(
-                        out=bank[:, e, :],
-                        lhsT=wb_codes[:, cols].bitcast(FP8X4),
-                        lhsT_scale=wb_scale[:, cols],
-                        rhs=tab2_codes[h][:, j0 : j0 + JB].bitcast(FP8X4),
-                        rhs_scale=tab2_scale[:, g * JB : (g + 1) * JB],
-                        start=True,
-                        stop=True,
-                    )
-                nc.scalar.copy(hb_sb[b, g][:, u], bank[:].rearrange("p e j -> p j e"))
-
-        for g in range(J // JB):
-            project_b(0, g)
-
-        tab_codes = []
-        for h in range(2):
-            pairs = held([P, HALF], U32, "tab_pairs%d" % h)
-            nc.vector.tensor_copy(pairs[:], tab_win[:].bitcast(U32).indirect(half_list(list1, h)))
-            parted = held([P, 2, 2 * HALF], U8, "tab_codes%d" % h)
-            nc.vector.tensor_copy(parted[:].bitcast(U16), pairs[:].bitcast(U16).rearrange("p (j d) -> p d j", d=2))
-            tab_codes.append(parted)
-
-        h_bf16 = {(b, h): held([P, HALF, PACK], BF16, "h_bf16_%d%d" % (b, h)) for b in range(2) for h in range(2)}
         h_codes = [held([P, J], U32, "h_codes%d" % b) for b in range(2)]
         h_scale = [held([P, J], U8, "h_scale%d" % b) for b in range(2)]
+        h_bf16, h_chunk = {}, {}
 
-        def project_a_and_join(b, c):
-            bank = psum.tile([P, PACK, JC], F32, name="ha_bank")
+        def new_h(b, lo, hi, tag):
+            h_bf16[b, lo] = keep.tile([P, hi - lo, PACK], BF16, name="h_bf16_%d_%d" % (b, lo), tag=tag, align_bytes=64)
+            for j0 in range(lo, hi, JC):
+                h_chunk[b, j0 // JC] = h_bf16[b, lo][:, j0 - lo : j0 - lo + JC, :]
+
+        def join(b, c):
+            bank = psum.tile([P, PACK, JC], F32, name="hb_bank")
             h, j0 = divmod(c * JC, HALF)
             for t in range(PACK):
-                cols = slice(t * P, (t + 1) * P)
-                for a in range(2):
-                    nc.tensor.matmul_mx(
-                        out=bank[:, t, :],
-                        lhsT=wa_codes[b, a][:, cols].bitcast(FP8X4),
-                        lhsT_scale=wa_scale[b, a][:, cols],
-                        rhs=tab_codes[h][:, a, 2 * j0 : 2 * (j0 + JC)].bitcast(FP4X4),
-                        rhs_scale=tab_scale[:, a, c * JC : (c + 1) * JC],
-                        start=(a == 0),
-                        stop=(a == 1),
-                    )
-            g, jb = divmod(c * JC, JB)
-            nc.vector.tensor_tensor(
-                h_bf16[b, h][:, j0 : j0 + JC, :].rearrange("p j (u e) -> p j u e", u=2),
-                bank[:].rearrange("p (u e) j -> p j u e", u=2),
-                hb_sb[b, g][:, :, jb : jb + JC, :].rearrange("p u j e -> p j u e"),
-                MULT,
-            )
+                cols = slice(b * PASS + t * P, b * PASS + (t + 1) * P)
+                nc.tensor.matmul_mx(
+                    out=bank[:, t, :],
+                    lhsT=wb_codes[:, cols].bitcast(FP8X4),
+                    lhsT_scale=wb_scale[:, cols],
+                    rhs=tab2_codes[h][:, j0 : j0 + JC].bitcast(FP8X4),
+                    rhs_scale=tab2_scale[:, c * JC : (c + 1) * JC],
+                    start=True,
+                    stop=True,
+                )
+            nc.vector.tensor_tensor(h_chunk[b, c], bank[:].rearrange("p t j -> p j t"), ha_sb[b, c][:], MULT)
 
         def quantise_h(b, lo, hi):
-            h, j0 = divmod(lo, HALF)
             nc.vector.quantize_mx(
                 out=h_codes[b][:, lo:hi].bitcast(FP8X4),
                 scales=h_scale[b][:, lo:hi],
-                in_=h_bf16[b, h][:, j0 : j0 + hi - lo, :].rearrange("p j t -> p (j t)"),
+                in_=h_bf16[b, lo][:].rearrange("p j t -> p (j t)"),
             )
 
         out_rows = out.rearrange("(u p) j -> p u j", p=P)
 
-        def score(lo, hi):
-            width = hi - lo
-            per_bank = min(2, PASS // width)
-            result = held([P, 2, width], F32, "result%d" % lo)
-            for u0 in range(0, 2, per_bank):
-                bank = psum.tile([P, per_bank, width], F32, name="y_bank", bufs=2)
-                for u in range(u0, u0 + per_bank):
-                    cols = slice(u * P, (u + 1) * P)
-                    for b in range(2):
-                        nc.tensor.matmul_mx(
-                            out=bank[:, u - u0, :],
-                            lhsT=en_codes[:, b, cols].bitcast(FP8X4),
-                            lhsT_scale=en_scale[:, b, cols],
-                            rhs=h_codes[b][:, lo:hi].bitcast(FP8X4),
-                            rhs_scale=h_scale[b][:, lo:hi],
-                            start=(b == 0),
-                            stop=(b == 1),
-                        )
-                nc.scalar.copy(result[:, u0 : u0 + per_bank, :], bank[:])
+        def score_pass(dst, u, b, lo, hi):
+            cols = slice(u * P, (u + 1) * P)
+            nc.tensor.matmul_mx(
+                out=dst,
+                lhsT=en_codes[:, b, cols].bitcast(FP8X4),
+                lhsT_scale=en_scale[:, b, cols],
+                rhs=h_codes[b][:, lo:hi].bitcast(FP8X4),
+                rhs_scale=h_scale[b][:, lo:hi],
+                start=(b == 0),
+                stop=(b == 1),
+            )
+
+        def store(lo, hi, banks):
+            result = held([P, 2, hi - lo], F32, "result%d" % lo)
+            per_bank = 2 // len(banks)
+            for n, bank in enumerate(banks):
+                nc.scalar.copy(result[:, n * per_bank : (n + 1) * per_bank, :], bank[:])
             nc.sync.dma_start(out_rows[:, :, lo:hi], result[:])
 
-        for c in range(CHUNKS):
-            project_a_and_join(0, c)
+        quarters = [(lo, lo + J // 4) for lo in range(0, J, J // 4)]
+        wide = [psum.tile([P, 1, HALF], F32, name="y_bank", bufs=2) for u in range(2)]
+        for n, ((lo, hi), tag) in enumerate(zip(quarters, ("h00", "h01", "bf16_10", "bf16_11"))):
+            new_h(0, lo, hi, tag)
+            for c in range(lo // JC, hi // JC):
+                join(0, c)
+            if n > 0:
+                quantise_h(0, *quarters[n - 1])
+            if n == 2:
+                for u in range(2):
+                    score_pass(wide[u][:, 0, :], u, 0, 0, HALF)
 
-        round_wa(1, 0)
-        round_wa(1, 1)
-        quantise_wa(1, 0)
-        quantise_h(0, 0, HALF)
-        quantise_wa(1, 1)
-        quantise_h(0, HALF, J)
-        for g in range(J // JB):
-            project_b(1, g)
-
+        for lo, hi in SCORE_RANGES:
+            new_h(1, lo, hi, "h1_%d" % lo)
         done = {hi // JC: (lo, hi) for lo, hi in SCORE_RANGES}
         for c in range(CHUNKS + 1):
             if c < CHUNKS:
-                project_a_and_join(1, c)
+                project_a(1, c)
+                join(1, c)
+            if c == 0:
+                quantise_h(0, *quarters[-1])
             if c in done:
-                quantise_h(1, *done[c])
-                score(*done[c])
+                lo, hi = done[c]
+                quantise_h(1, lo, hi)
+                if lo == 0:
+                    for u in range(2):
+                        score_pass(wide[u][:, 0, :], u, 1, lo, hi)
+                    store(lo, hi, wide)
+                else:
+                    bank = psum.tile([P, 2, hi - lo], F32, name="y_bank", bufs=2)
+                    for u in range(2):
+                        for b in range(2):
+                            score_pass(bank[:, u, :], u, b, lo, hi)
+                    store(lo, hi, [bank])

@@ -22,6 +22,7 @@ QUADS = 4
 HALF = J // 2
 JC = 128
 CHUNKS = J // JC
+WA_BYTES = PACK * PASS * 4
 TAB_RANGES = ((0, 256), (256, 512), (512, 1024))
 SCORE_RANGES = ((0, 512), (512, 768), (768, 896), (896, 1024))
 
@@ -38,8 +39,9 @@ def tile_list_kg_mul_none_kernel(
         lists = ctx.enter_context(tc.tile_pool(name="lists", bufs=1))
         keep = ctx.enter_context(tc.tile_pool(name="keep", bufs=1))
         shared = ctx.enter_context(tc.tile_pool(name="shared", bufs=1))
-        stage = ctx.enter_context(tc.tile_pool(name="stage", bufs=2))
-        psum = ctx.enter_context(tc.psum_pool(name="psum", bufs=3))
+        late = ctx.enter_context(tc.tile_pool(name="late", bufs=1))
+        relay = ctx.enter_context(tc.tile_pool(name="relay", bufs=1))
+        psum = ctx.enter_context(tc.psum_pool(name="psum", bufs=1))
 
         def held(shape, dtype, name):
             return keep.tile(shape, dtype, name=name, align_bytes=64)
@@ -48,21 +50,21 @@ def tile_list_kg_mul_none_kernel(
         list1 = lists.tile([P, J // 16], U16, name="list1")
 
         tab_scale_win = held([P, T], U8, "tab_scale_win")
-        tab2_scale_win = shared.tile([P, T], U8, name="tab2_scale_win", offset=4 * R - T // 2, align_bytes=64)
-        wb_scale_raw = keep.tile([P, R], U8, name="wb_scale_raw", tag="wb_then_en_scale", align_bytes=64)
+        tab2_scale_win = shared.tile([P, T], U8, name="tab2_scale_win", offset=WA_BYTES - T // 2, align_bytes=64)
+        wb_scale_raw = held([P, R], U8, "wb_scale_raw")
         tab_scale = held([P, 2, J], U8, "tab_scale")
         tab2_scale = held([P, J], U8, "tab2_scale")
-        nc.gpsimd.memset(tab_scale[96:128, :, :].bitcast(I32), 0)
+        nc.gpsimd.memset(wb_scale_raw[:].bitcast(I32), 0)
         for q in range(QUADS):
             engine = nc.vector if q < 3 else nc.gpsimd
             engine.memset(tab_scale_win[32 * q : 32 * q + 24, :].bitcast(I32), 0)
+        nc.gpsimd.memset(tab_scale[96:128, :, :].bitcast(I32), 0)
         nc.gpsimd.memset(tab2_scale_win[0:96, :].bitcast(I32), 0)
         nc.gpsimd.memset(tab2_scale_win[96:112, :].bitcast(I32), 0)
-        nc.gpsimd.memset(wb_scale_raw[:].bitcast(I32), 0)
         nc.gpsimd.memset(tab2_scale[:].bitcast(I32), 0)
 
-        def load_wa(b, a):
-            raw = stage.tile([P, PACK, PASS], F32, name="wa_raw")
+        def load_wa(b, a, pool, offset):
+            raw = pool.tile([P, PACK, PASS], F32, name="wa_raw%d%d" % (b, a), offset=offset, align_bytes=64)
             rows = wa[a * PASS : (a + 1) * PASS, b * PASS : (b + 1) * PASS]
             nc.sync.dma_start(raw[:], rows.rearrange("(p i) c -> p i c", i=PACK))
             return raw
@@ -72,50 +74,52 @@ def tile_list_kg_mul_none_kernel(
             nc.sync.dma_start(
                 tab_scale_win[32 * q + 24 : 32 * q + 32, :].bitcast(I32), tab_scales[:, 4 * q : 4 * q + 4, :].bitcast(I32)
             )
-        wa_raw = {(0, 0): load_wa(0, 0)}
+        wa_raw = {(0, 0): load_wa(0, 0, keep, None)}
         nc.sync.dma_start(list2[:], offs2)
         nc.sync.dma_start(tab2_scale_win[112:128, :].bitcast(I32), tab2_scales[0].bitcast(I32))
-        wa_raw[0, 1] = load_wa(0, 1)
-        tab_win = held([P, T], I32, "tab_win")
-        nc.sync.dma_start(tab_win[:], as_words(tab_words[0]))
         for q in range(QUADS):
             nc.sync.dma_start(
                 wb_scale_raw[32 * q : 32 * q + 4, :].bitcast(I32), wb_scales[0, 4 * q : 4 * q + 4, :].bitcast(I32)
             )
+        tab_win = keep.tile([P, T], I32, name="tab_win", tag="tab_words", align_bytes=64)
+        nc.sync.dma_start(tab_win[:], as_words(tab_words[0]))
+        wa_raw[0, 1] = load_wa(0, 1, keep, None)
 
-        tab_scale_picked = held([P, J], U8, "tab_scale_picked")
+        tab_scale_picked = late.tile([P, J], U8, name="tab_scale_picked", offset=4 * T - J // 2, align_bytes=64)
         nc.vector.tensor_copy(tab_scale_picked[:], tab_scale_win[:].indirect(list1[:]))
         for a in range(2):
             nc.sync.dma_start(tab_scale[0:100, a, :].bitcast(I32), tab_scale_picked[24 + 4 * a : 124 + 4 * a, :].bitcast(I32))
 
         tab2_scale_picked = held([P, J], U8, "tab2_scale_picked")
         nc.vector.tensor_copy(tab2_scale_picked[:], tab2_scale_win[:].indirect(list2[:]))
-        wb_raw = shared.tile([P, R], I32, name="wb_raw", offset=0, align_bytes=64)
+        wa_raw[1, 0] = load_wa(1, 0, shared, 0)
+        wb_raw = shared.tile([P, R], I32, name="wb_raw", offset=WA_BYTES, align_bytes=64)
         nc.sync.dma_start(wb_raw[:], as_words(wb_words[0]))
-        tab2_win = shared.tile([P, T], I32, name="tab2_win", offset=4 * R, align_bytes=64)
-        nc.sync.dma_start(tab2_win[:], as_words(tab2_words[0]))
         for q in range(QUADS):
             nc.sync.dma_start(
                 tab2_scale[32 * q : 32 * q + 4, :].bitcast(I32),
                 tab2_scale_picked[112 + 4 * q : 116 + 4 * q, :].bitcast(I32),
             )
 
+        tab2_win = late.tile([P, T], I32, name="tab2_win", offset=0, align_bytes=64)
+        nc.sync.dma_start(tab2_win[:], as_words(tab2_words[0]))
+        wa_raw[1, 1] = load_wa(1, 1, late, 4 * T)
+
         wa_grouped, wa_codes, wa_scale = {}, {}, {}
 
-        def round_wa(b, a):
-            grouped = keep.tile(
-                [P, PASS * PACK], BF16, name="wa_grouped%d%d" % (b, a), tag="bf16_%d%d" % (b, a), align_bytes=64
-            )
+        def relay_tile(shape, dtype, name, offset=0):
+            return relay.tile(shape, dtype, name=name, offset=offset, align_bytes=64)
+
+        def round_wa(b, a, make=held):
+            grouped = make([P, PASS * PACK], BF16, "wa_grouped%d%d" % (b, a))
             dst = grouped[:].rearrange("p (t m i) -> p m i t", t=PACK, i=PACK)
             src = wa_raw[b, a][:].rearrange("p i (m t) -> p m i t", t=PACK)
             for t0 in range(0, PACK, 2):
                 nc.scalar.copy(dst[:, :, :, t0 : t0 + 2], src[:, :, :, t0 : t0 + 2])
             wa_grouped[b, a] = grouped
 
-        def quantise_wa(b, a):
-            wa_codes[b, a] = keep.tile(
-                [P, PASS], U32, name="wa_codes%d%d" % (b, a), tag="bf16_%d%d" % (b + 1, a), align_bytes=64
-            )
+        def quantise_wa(b, a, codes):
+            wa_codes[b, a] = codes
             wa_scale[b, a] = held([P, PASS], U8, "wa_scale%d%d" % (b, a))
             nc.vector.quantize_mx(out=wa_codes[b, a][:].bitcast(FP8X4), scales=wa_scale[b, a][:], in_=wa_grouped[b, a][:])
 
@@ -125,7 +129,7 @@ def tile_list_kg_mul_none_kernel(
         tab_codes = {}
 
         def pick_tab(lo, hi):
-            pairs = keep.tile([P, hi - lo], U32, name="tab_pairs%d" % lo, tag="pairs%d" % lo, align_bytes=64)
+            pairs = keep.tile([P, hi - lo], U32, name="tab_pairs%d" % lo, tag="pairs", align_bytes=64)
             nc.vector.tensor_copy(pairs[:], tab_win[:].bitcast(U32).indirect(part_of(list1, lo, hi)))
             parted = held([P, 2, 2 * (hi - lo)], U8, "tab_codes%d" % lo)
             nc.vector.tensor_copy(parted[:].bitcast(U16), pairs[:].bitcast(U16).rearrange("p (j d) -> p d j", d=2))
@@ -133,37 +137,57 @@ def tile_list_kg_mul_none_kernel(
                 tab_codes[j0 // JC] = parted[:, :, 2 * (j0 - lo) : 2 * (j0 - lo + JC)]
 
         round_wa(0, 0)
-        quantise_wa(0, 0)
-        round_wa(0, 1)
-        pick_tab(*TAB_RANGES[0])
-        quantise_wa(0, 1)
-        for lo, hi in TAB_RANGES[1:]:
+        quantise_wa(0, 0, held([P, PASS], U32, "wa_codes00"))
+        for lo, hi in TAB_RANGES:
             pick_tab(lo, hi)
+        round_wa(0, 1)
+        quantise_wa(0, 1, held([P, PASS], U32, "wa_codes01"))
 
         ha_sb = {}
 
-        def project_a(b, c):
-            bank = psum.tile([P, PACK, JC], F32, name="ha_bank")
-            for t in range(PACK):
-                cols = slice(t * P, (t + 1) * P)
-                for a in range(2):
+        def bank_tile(n):
+            return psum.tile([P, PACK, JC], F32, name="bank", tag="bank%d" % n)
+
+        def project_a(b, c, bank):
+            passes = (0, 1)
+            for a in passes:
+                for t in range(PACK):
+                    cols = slice(t * P, (t + 1) * P)
                     nc.tensor.matmul_mx(
                         out=bank[:, t, :],
                         lhsT=wa_codes[b, a][:, cols].bitcast(FP8X4),
                         lhsT_scale=wa_scale[b, a][:, cols],
                         rhs=tab_codes[c][:, a, :].bitcast(FP4X4),
                         rhs_scale=tab_scale[:, a, c * JC : (c + 1) * JC],
-                        start=(a == 0),
-                        stop=(a == 1),
+                        start=(a == passes[0] and t == 0),
+                        stop=(a == passes[1] and t == PACK - 1),
                     )
-            ha_sb[b, c] = held([P, JC, PACK], F32, "ha%d_%d" % (b, c))
+            return bank
+
+        def copy_a(b, c, bank):
+            name = "ha%d_%d" % (b, c)
+            if (b, c) == (0, 0):
+                ha_sb[b, c] = shared.tile([P, JC, PACK], F32, name=name, offset=0, align_bytes=64)
+            elif b == 0 and c >= 5:
+                ha_sb[b, c] = late.tile([P, JC, PACK], F32, name=name, offset=4 * T + J + (c - 5) * 2048, align_bytes=64)
+            else:
+                ha_sb[b, c] = held([P, JC, PACK], F32, name)
             nc.scalar.copy(ha_sb[b, c][:], bank[:].rearrange("p t j -> p j t"))
 
+        round_wa(1, 0)
+        waiting = []
         for c in range(CHUNKS):
-            project_a(0, c)
+            bank = project_a(0, c, bank_tile(c % 6))
+            if c < 5:
+                copy_a(0, c, bank)
+            else:
+                waiting.append((c, bank))
+        round_wa(1, 1, relay_tile)
+        for c, bank in waiting:
+            copy_a(0, c, bank)
 
-        wb_codes = keep.tile([P, R], I32, name="wb_codes", tag="pairs512", align_bytes=64)
-        wb_scale = keep.tile([P, R], U8, name="wb_scale", tag="pairs256", align_bytes=64)
+        wb_codes = keep.tile([P, R], I32, name="wb_codes", tag="tab_words", align_bytes=64)
+        wb_scale = held([P, R], U8, "wb_scale")
         nc.vector.tensor_copy(
             wb_scale[:].rearrange("p (b t m) -> p b t m", b=2, t=PACK),
             wb_scale_raw[:].rearrange("p (b m t) -> p b t m", b=2, t=PACK),
@@ -173,17 +197,10 @@ def tile_list_kg_mul_none_kernel(
             wb_raw[:].rearrange("p (b m t) -> p b m t", b=2, t=PACK),
         )
 
-        wa_raw[1, 0] = load_wa(1, 0)
-        wa_raw[1, 1] = load_wa(1, 1)
-        en_codes = shared.tile([P, 2, N], I32, name="en_codes", offset=0, align_bytes=64)
+        en_codes = shared.tile([P, 2, N], I32, name="en_codes", offset=WA_BYTES + 2 * R, align_bytes=64)
         nc.sync.dma_start(en_codes[:], en_words.rearrange("a p n i -> p a (n i)").bitcast(I32))
-        en_scale = keep.tile([P, 2, N], U8, name="en_scale", tag="wb_then_en_scale", align_bytes=64)
-        nc.gpsimd.memset(en_scale[:].bitcast(I32), 0)
-        for q in range(QUADS):
-            nc.sync.dma_start(
-                en_scale[32 * q : 32 * q + 4, :, :].bitcast(I32),
-                en_scales[:, 4 * q : 4 * q + 4, :].rearrange("a r n -> r a n").bitcast(I32),
-            )
+
+        quantise_wa(1, 0, shared.tile([P, PASS], U32, name="wa_codes10", offset=WA_BYTES, align_bytes=64))
 
         tab2_codes = []
         for h in range(2):
@@ -191,21 +208,28 @@ def tile_list_kg_mul_none_kernel(
             nc.vector.tensor_copy(codes[:], tab2_win[:].bitcast(U32).indirect(part_of(list2, h * HALF, (h + 1) * HALF)))
             tab2_codes.append(codes)
 
-        for a in range(2):
-            round_wa(1, a)
-            quantise_wa(1, a)
+        en_scale = late.tile([P, 2, N], U8, name="en_scale", offset=0, align_bytes=64)
+        nc.gpsimd.memset(en_scale[:].bitcast(I32), 0)
+        for q in range(QUADS):
+            nc.sync.dma_start(
+                en_scale[32 * q : 32 * q + 4, :, :].bitcast(I32),
+                en_scales[:, 4 * q : 4 * q + 4, :].rearrange("a r n -> r a n").bitcast(I32),
+            )
 
-        h_codes = [held([P, J], U32, "h_codes%d" % b) for b in range(2)]
+        quantise_wa(1, 1, held([P, PASS], U32, "wa_codes11"))
+
+        h_codes = [relay_tile([P, J], U32, "h_codes0", 2048), held([P, J], U32, "h_codes1")]
         h_scale = [held([P, J], U8, "h_scale%d" % b) for b in range(2)]
         h_bf16, h_chunk = {}, {}
 
-        def new_h(b, lo, hi, tag):
-            h_bf16[b, lo] = keep.tile([P, hi - lo, PACK], BF16, name="h_bf16_%d_%d" % (b, lo), tag=tag, align_bytes=64)
+        def new_h(b, lo, hi, offset=None):
+            shape, name = [P, hi - lo, PACK], "h_bf16_%d_%d" % (b, lo)
+            h_bf16[b, lo] = held(shape, BF16, name) if offset is None else relay_tile(shape, BF16, name, offset)
             for j0 in range(lo, hi, JC):
                 h_chunk[b, j0 // JC] = h_bf16[b, lo][:, j0 - lo : j0 - lo + JC, :]
 
         def join(b, c):
-            bank = psum.tile([P, PACK, JC], F32, name="hb_bank")
+            bank = bank_tile(2 + (b * CHUNKS + c) % 3)
             h, j0 = divmod(c * JC, HALF)
             for t in range(PACK):
                 cols = slice(b * PASS + t * P, b * PASS + (t + 1) * P)
@@ -248,37 +272,36 @@ def tile_list_kg_mul_none_kernel(
                 nc.scalar.copy(result[:, n * per_bank : (n + 1) * per_bank, :], bank[:])
             nc.sync.dma_start(out_rows[:, :, lo:hi], result[:])
 
-        quarters = [(lo, lo + J // 4) for lo in range(0, J, J // 4)]
-        wide = [psum.tile([P, 1, HALF], F32, name="y_bank", bufs=2) for u in range(2)]
-        for n, ((lo, hi), tag) in enumerate(zip(quarters, ("h00", "h01", "bf16_10", "bf16_11"))):
-            new_h(0, lo, hi, tag)
-            for c in range(lo // JC, hi // JC):
-                join(0, c)
-            if n > 0:
-                quantise_h(0, *quarters[n - 1])
-            if n == 2:
+        def finish(lo, hi):
+            if lo == 0:
+                wide = [psum.tile([P, 1, HALF], F32, name="bank", tag="bank%d" % (6 + u)) for u in range(2)]
                 for u in range(2):
-                    score_pass(wide[u][:, 0, :], u, 0, 0, HALF)
+                    for b in range(2):
+                        score_pass(wide[u][:, 0, :], u, b, lo, hi)
+                store(lo, hi, wide)
+            else:
+                last = hi // JC - 1
+                bank = psum.tile([P, 2, hi - lo], F32, name="bank", tag="bank%d" % (2 + (CHUNKS + last) % 3))
+                for u in range(2):
+                    for b in range(2):
+                        score_pass(bank[:, u, :], u, b, lo, hi)
+                store(lo, hi, [bank])
 
+        quarters = [(lo, lo + J // 4) for lo in range(0, J, J // 4)]
+        for n, (lo, hi) in enumerate(quarters):
+            new_h(0, lo, hi, (None, None, 0, None)[n])
         for lo, hi in SCORE_RANGES:
-            new_h(1, lo, hi, "h1_%d" % lo)
-        done = {hi // JC: (lo, hi) for lo, hi in SCORE_RANGES}
-        for c in range(CHUNKS + 1):
-            if c < CHUNKS:
-                project_a(1, c)
-                join(1, c)
-            if c == 0:
-                quantise_h(0, *quarters[-1])
-            if c in done:
-                lo, hi = done[c]
-                quantise_h(1, lo, hi)
-                if lo == 0:
-                    for u in range(2):
-                        score_pass(wide[u][:, 0, :], u, 1, lo, hi)
-                    store(lo, hi, wide)
-                else:
-                    bank = psum.tile([P, 2, hi - lo], F32, name="y_bank", bufs=2)
-                    for u in range(2):
-                        for b in range(2):
-                            score_pass(bank[:, u, :], u, b, lo, hi)
-                    store(lo, hi, [bank])
+            new_h(1, lo, hi)
+        ends = {hi // JC: (0, lo, hi) for lo, hi in quarters}
+        for lo, hi in SCORE_RANGES:
+            ends[CHUNKS + hi // JC] = (1, lo, hi)
+        for step in range(2 * CHUNKS + 1):
+            c = step - 5
+            if 0 <= c < CHUNKS:
+                copy_a(1, c, project_a(1, c, bank_tile((6, 7, 5, 0, 1, 5, 0, 1)[c])))
+            if step < 2 * CHUNKS:
+                join(*divmod(step, CHUNKS))
+            if step in ends:
+                quantise_h(*ends[step])
+                if step > CHUNKS:
+                    finish(*ends[step][1:])

@@ -19,12 +19,19 @@ P = 128
 PACK = 4
 PASS = P * PACK
 QUADS = 4
+LIST_GROUP = 16
 HALF = J // 2
 JC = 128
 CHUNKS = J // JC
-WA_BYTES = PACK * PASS * 4
+CHUNK_BYTES = JC * PACK * 4
 TAB_RANGES = ((0, 256), (256, 512), (512, 1024))
 SCORE_RANGES = ((0, 512), (512, 768), (768, 896), (896, 1024))
+HA0_BANKS = 6
+HB_BANKS = (2, 3, 4)
+SPARE_BANKS = (6, 7)
+HA1_BANKS = (5, 0, 1)
+COPIES_BEFORE_LAST_WA = 5
+HA1_LEAD = 3
 
 
 def as_words(dram_pass):
@@ -38,119 +45,124 @@ def tile_list_kg_mul_none_kernel(
     with ExitStack() as ctx:
         lists = ctx.enter_context(tc.tile_pool(name="lists", bufs=1))
         keep = ctx.enter_context(tc.tile_pool(name="keep", bufs=1))
-        shared = ctx.enter_context(tc.tile_pool(name="shared", bufs=1))
-        late = ctx.enter_context(tc.tile_pool(name="late", bufs=1))
+        second = ctx.enter_context(tc.tile_pool(name="second", bufs=1))
+        last_wa = ctx.enter_context(tc.tile_pool(name="last_wa", bufs=1))
+        third_wa = ctx.enter_context(tc.tile_pool(name="third_wa", bufs=1))
         relay = ctx.enter_context(tc.tile_pool(name="relay", bufs=1))
         psum = ctx.enter_context(tc.psum_pool(name="psum", bufs=1))
 
         def held(shape, dtype, name):
             return keep.tile(shape, dtype, name=name, align_bytes=64)
 
-        list2 = lists.tile([P, J // 16], U16, name="list2")
-        list1 = lists.tile([P, J // 16], U16, name="list1")
+        def placed(pool, offset):
+            return lambda shape, dtype, name: pool.tile(shape, dtype, name=name, offset=offset, align_bytes=64)
 
-        tab_scale_win = held([P, T], U8, "tab_scale_win")
-        tab2_scale_win = shared.tile([P, T], U8, name="tab2_scale_win", offset=WA_BYTES - T // 2, align_bytes=64)
+        list2 = lists.tile([P, J // LIST_GROUP], U16, name="list2")
+        list1 = lists.tile([P, J // LIST_GROUP], U16, name="list1")
+
+        wb_at = 0
+        tab2_scale_at = 4 * R
+        tab2_at = tab2_scale_at + J
+        tab_scale_win = placed(second, tab2_scale_at - T // 4)([P, T], U8, "tab_scale_win")
+        tab2_scale_win = held([P, T], U8, "tab2_scale_win")
         wb_scale_raw = held([P, R], U8, "wb_scale_raw")
-        tab_scale = held([P, 2, J], U8, "tab_scale")
-        tab2_scale = held([P, J], U8, "tab2_scale")
+        tab_scale1 = held([P, J], U8, "tab_scale1")
+        nc.gpsimd.memset(tab_scale_win[:].bitcast(I32), 0)
+        nc.vector.memset(tab2_scale_win[0:96, :].bitcast(I32), 0)
+        nc.vector.memset(tab2_scale_win[96:112, :].bitcast(I32), 0)
         nc.gpsimd.memset(wb_scale_raw[:].bitcast(I32), 0)
-        for q in range(QUADS):
-            engine = nc.vector if q < 3 else nc.gpsimd
-            engine.memset(tab_scale_win[32 * q : 32 * q + 24, :].bitcast(I32), 0)
-        nc.gpsimd.memset(tab_scale[96:128, :, :].bitcast(I32), 0)
-        nc.gpsimd.memset(tab2_scale_win[0:96, :].bitcast(I32), 0)
-        nc.gpsimd.memset(tab2_scale_win[96:112, :].bitcast(I32), 0)
-        nc.gpsimd.memset(tab2_scale[:].bitcast(I32), 0)
+        nc.gpsimd.memset(tab_scale1[96:128, :].bitcast(I32), 0)
 
-        def load_wa(b, a, pool, offset):
-            raw = pool.tile([P, PACK, PASS], F32, name="wa_raw%d%d" % (b, a), offset=offset, align_bytes=64)
+        def load_wa(b, a, make):
+            raw = make([P, PACK, PASS], F32, "wa_raw%d%d" % (b, a))
             rows = wa[a * PASS : (a + 1) * PASS, b * PASS : (b + 1) * PASS]
             nc.sync.dma_start(raw[:], rows.rearrange("(p i) c -> p i c", i=PACK))
             return raw
 
-        nc.sync.dma_start(list1[:], offs)
-        for q in range(QUADS):
-            nc.sync.dma_start(
-                tab_scale_win[32 * q + 24 : 32 * q + 32, :].bitcast(I32), tab_scales[:, 4 * q : 4 * q + 4, :].bitcast(I32)
-            )
-        wa_raw = {(0, 0): load_wa(0, 0, keep, None)}
         nc.sync.dma_start(list2[:], offs2)
         nc.sync.dma_start(tab2_scale_win[112:128, :].bitcast(I32), tab2_scales[0].bitcast(I32))
+        wa_raw = {(0, 0): load_wa(0, 0, held)}
+        nc.sync.dma_start(list1[:], offs)
+        tab_scale_rows = tab_scales.rearrange("a (q e) t -> e q a t", e=4)
+        for e in range(4):
+            nc.sync.dma_start(tab_scale_win[e:P:16, :].bitcast(I32), tab_scale_rows[e].bitcast(I32))
+        tab_win = keep.tile([P, T], I32, name="tab_win", tag="tab_then_wb", align_bytes=64)
+        nc.sync.dma_start(tab_win[:], as_words(tab_words[0]))
+        wa_raw[0, 1] = load_wa(0, 1, held)
+        wa_raw[1, 0] = load_wa(1, 0, placed(third_wa, 0))
         for q in range(QUADS):
             nc.sync.dma_start(
                 wb_scale_raw[32 * q : 32 * q + 4, :].bitcast(I32), wb_scales[0, 4 * q : 4 * q + 4, :].bitcast(I32)
             )
-        tab_win = keep.tile([P, T], I32, name="tab_win", tag="tab_words", align_bytes=64)
-        nc.sync.dma_start(tab_win[:], as_words(tab_words[0]))
-        wa_raw[0, 1] = load_wa(0, 1, keep, None)
-
-        tab_scale_picked = late.tile([P, J], U8, name="tab_scale_picked", offset=4 * T - J // 2, align_bytes=64)
-        nc.vector.tensor_copy(tab_scale_picked[:], tab_scale_win[:].indirect(list1[:]))
-        for a in range(2):
-            nc.sync.dma_start(tab_scale[0:100, a, :].bitcast(I32), tab_scale_picked[24 + 4 * a : 124 + 4 * a, :].bitcast(I32))
 
         tab2_scale_picked = held([P, J], U8, "tab2_scale_picked")
         nc.vector.tensor_copy(tab2_scale_picked[:], tab2_scale_win[:].indirect(list2[:]))
-        wa_raw[1, 0] = load_wa(1, 0, shared, 0)
-        wb_raw = shared.tile([P, R], I32, name="wb_raw", offset=WA_BYTES, align_bytes=64)
+        tab_scale0 = held([P, J], U8, "tab_scale0")
+        nc.vector.tensor_copy(tab_scale0[:], tab_scale_win[:].indirect(list1[:]))
+        nc.sync.dma_start(tab_scale1[0:112, :].bitcast(I32), tab_scale0[16:128, :].bitcast(I32))
+        tab_scale = (tab_scale0, tab_scale1)
+
+        wb_raw = placed(second, wb_at)([P, R], I32, "wb_raw")
+        tab2_win = placed(second, tab2_at)([P, T], I32, "tab2_win")
         nc.sync.dma_start(wb_raw[:], as_words(wb_words[0]))
+        nc.sync.dma_start(tab2_win[:], as_words(tab2_words[0]))
+        tab2_scale = placed(second, tab2_scale_at)([P, J], U8, "tab2_scale")
+        nc.gpsimd.memset(tab2_scale[:].bitcast(I32), 0)
         for q in range(QUADS):
             nc.sync.dma_start(
                 tab2_scale[32 * q : 32 * q + 4, :].bitcast(I32),
                 tab2_scale_picked[112 + 4 * q : 116 + 4 * q, :].bitcast(I32),
             )
 
-        tab2_win = late.tile([P, T], I32, name="tab2_win", offset=0, align_bytes=64)
-        nc.sync.dma_start(tab2_win[:], as_words(tab2_words[0]))
-        wa_raw[1, 1] = load_wa(1, 1, late, 4 * T)
+        wa_codes, wa_scale = {}, {}
 
-        wa_grouped, wa_codes, wa_scale = {}, {}, {}
+        def round_wa(b, a, dst, t0):
+            src = wa_raw[b, a][:].rearrange("p i (m t) -> p m i t", t=PACK)
+            nc.scalar.copy(dst, src[:, :, :, t0 : t0 + 2])
 
-        def relay_tile(shape, dtype, name, offset=0):
-            return relay.tile(shape, dtype, name=name, offset=offset, align_bytes=64)
-
-        def round_wa(b, a, make=held):
+        def round_wa_whole(b, a, make):
             grouped = make([P, PASS * PACK], BF16, "wa_grouped%d%d" % (b, a))
             dst = grouped[:].rearrange("p (t m i) -> p m i t", t=PACK, i=PACK)
-            src = wa_raw[b, a][:].rearrange("p i (m t) -> p m i t", t=PACK)
             for t0 in range(0, PACK, 2):
-                nc.scalar.copy(dst[:, :, :, t0 : t0 + 2], src[:, :, :, t0 : t0 + 2])
-            wa_grouped[b, a] = grouped
+                round_wa(b, a, dst[:, :, :, t0 : t0 + 2], t0)
+            return grouped
 
-        def quantise_wa(b, a, codes):
-            wa_codes[b, a] = codes
+        def quantise_wa(b, a, pieces, make):
+            wa_codes[b, a] = make([P, PASS], U32, "wa_codes%d%d" % (b, a))
             wa_scale[b, a] = held([P, PASS], U8, "wa_scale%d%d" % (b, a))
-            nc.vector.quantize_mx(out=wa_codes[b, a][:].bitcast(FP8X4), scales=wa_scale[b, a][:], in_=wa_grouped[b, a][:])
+            width = PASS // len(pieces)
+            for n, piece in enumerate(pieces):
+                cols = slice(n * width, (n + 1) * width)
+                nc.vector.quantize_mx(
+                    out=wa_codes[b, a][:, cols].bitcast(FP8X4), scales=wa_scale[b, a][:, cols], in_=piece[:]
+                )
 
         def part_of(lst, lo, hi):
-            return lst[:, lo // 16 : hi // 16]
+            return lst[:, lo // LIST_GROUP : hi // LIST_GROUP]
 
         tab_codes = {}
 
         def pick_tab(lo, hi):
-            pairs = keep.tile([P, hi - lo], U32, name="tab_pairs%d" % lo, tag="pairs", align_bytes=64)
+            pairs = keep.tile([P, hi - lo], U32, name="tab_pairs%d" % lo, tag="pairs", bufs=2, align_bytes=64)
             nc.vector.tensor_copy(pairs[:], tab_win[:].bitcast(U32).indirect(part_of(list1, lo, hi)))
             parted = held([P, 2, 2 * (hi - lo)], U8, "tab_codes%d" % lo)
             nc.vector.tensor_copy(parted[:].bitcast(U16), pairs[:].bitcast(U16).rearrange("p (j d) -> p d j", d=2))
             for j0 in range(lo, hi, JC):
                 tab_codes[j0 // JC] = parted[:, :, 2 * (j0 - lo) : 2 * (j0 - lo + JC)]
 
-        round_wa(0, 0)
-        quantise_wa(0, 0, held([P, PASS], U32, "wa_codes00"))
+        last_wa_at = PASS * PACK
+        quantise_wa(0, 0, [round_wa_whole(0, 0, placed(last_wa, 0))], held)
+        wa_raw[1, 1] = load_wa(1, 1, placed(last_wa, last_wa_at))
         for lo, hi in TAB_RANGES:
             pick_tab(lo, hi)
-        round_wa(0, 1)
-        quantise_wa(0, 1, held([P, PASS], U32, "wa_codes01"))
+        quantise_wa(0, 1, [round_wa_whole(0, 1, held)], held)
 
-        ha_sb = {}
+        def bank_tile(n, shape):
+            return psum.tile(shape, F32, name="bank", tag="bank%d" % n)
 
-        def bank_tile(n):
-            return psum.tile([P, PACK, JC], F32, name="bank", tag="bank%d" % n)
-
-        def project_a(b, c, bank):
-            passes = (0, 1)
-            for a in passes:
+        def project_a(b, c, n):
+            bank = bank_tile(n, [P, PACK, JC])
+            for a in range(2):
                 for t in range(PACK):
                     cols = slice(t * P, (t + 1) * P)
                     nc.tensor.matmul_mx(
@@ -158,35 +170,36 @@ def tile_list_kg_mul_none_kernel(
                         lhsT=wa_codes[b, a][:, cols].bitcast(FP8X4),
                         lhsT_scale=wa_scale[b, a][:, cols],
                         rhs=tab_codes[c][:, a, :].bitcast(FP4X4),
-                        rhs_scale=tab_scale[:, a, c * JC : (c + 1) * JC],
-                        start=(a == passes[0] and t == 0),
-                        stop=(a == passes[1] and t == PACK - 1),
+                        rhs_scale=tab_scale[a][:, c * JC : (c + 1) * JC],
+                        start=(a == 0 and t == 0),
+                        stop=(a == 1 and t == PACK - 1),
                     )
             return bank
 
-        def copy_a(b, c, bank):
-            name = "ha%d_%d" % (b, c)
-            if (b, c) == (0, 0):
-                ha_sb[b, c] = shared.tile([P, JC, PACK], F32, name=name, offset=0, align_bytes=64)
-            elif b == 0 and c >= 5:
-                ha_sb[b, c] = late.tile([P, JC, PACK], F32, name=name, offset=4 * T + J + (c - 5) * 2048, align_bytes=64)
-            else:
-                ha_sb[b, c] = held([P, JC, PACK], F32, name)
+        ha_sb = {}
+
+        def copy_a(b, c, bank, make):
+            ha_sb[b, c] = make([P, JC, PACK], F32, "ha%d_%d" % (b, c))
             nc.scalar.copy(ha_sb[b, c][:], bank[:].rearrange("p t j -> p j t"))
 
-        round_wa(1, 0)
-        waiting = []
+        grouped10 = round_wa_whole(1, 0, held)
+        banks = []
         for c in range(CHUNKS):
-            bank = project_a(0, c, bank_tile(c % 6))
-            if c < 5:
-                copy_a(0, c, bank)
-            else:
-                waiting.append((c, bank))
-        round_wa(1, 1, relay_tile)
-        for c, bank in waiting:
-            copy_a(0, c, bank)
+            banks.append(project_a(0, c, c % HA0_BANKS))
+            if c < COPIES_BEFORE_LAST_WA:
+                copy_a(0, c, banks[c], placed(third_wa, 0) if c == 0 else held)
+        piece_bytes = PASS * PACK
+        late_piece_at = 4 * piece_bytes
+        h_codes_at = late_piece_at + piece_bytes // 2 - 4 * J
+        h_quarter_at = late_piece_at + piece_bytes // 2
+        pieces11 = []
+        for n, offset in enumerate((0, late_piece_at)):
+            pieces11.append(placed(relay, offset)([P, 2 * PASS], BF16, "wa_grouped11_%d" % n))
+            round_wa(1, 1, pieces11[n][:].rearrange("p (t m i) -> p m i t", t=2, i=PACK), 2 * n)
+        for c in range(COPIES_BEFORE_LAST_WA, CHUNKS):
+            copy_a(0, c, banks[c], placed(last_wa, last_wa_at + (c - COPIES_BEFORE_LAST_WA) * CHUNK_BYTES))
 
-        wb_codes = keep.tile([P, R], I32, name="wb_codes", tag="tab_words", align_bytes=64)
+        wb_codes = keep.tile([P, R], I32, name="wb_codes", tag="tab_then_wb", align_bytes=64)
         wb_scale = held([P, R], U8, "wb_scale")
         nc.vector.tensor_copy(
             wb_scale[:].rearrange("p (b t m) -> p b t m", b=2, t=PACK),
@@ -197,10 +210,9 @@ def tile_list_kg_mul_none_kernel(
             wb_raw[:].rearrange("p (b m t) -> p b m t", b=2, t=PACK),
         )
 
-        en_codes = shared.tile([P, 2, N], I32, name="en_codes", offset=WA_BYTES + 2 * R, align_bytes=64)
+        en_codes = placed(second, wb_at + 2 * R)([P, 2, N], I32, "en_codes")
         nc.sync.dma_start(en_codes[:], en_words.rearrange("a p n i -> p a (n i)").bitcast(I32))
-
-        quantise_wa(1, 0, shared.tile([P, PASS], U32, name="wa_codes10", offset=WA_BYTES, align_bytes=64))
+        quantise_wa(1, 0, [grouped10], placed(second, wb_at))
 
         tab2_codes = []
         for h in range(2):
@@ -208,28 +220,30 @@ def tile_list_kg_mul_none_kernel(
             nc.vector.tensor_copy(codes[:], tab2_win[:].bitcast(U32).indirect(part_of(list2, h * HALF, (h + 1) * HALF)))
             tab2_codes.append(codes)
 
-        en_scale = late.tile([P, 2, N], U8, name="en_scale", offset=0, align_bytes=64)
+        en_scale = placed(second, 8 * R)([P, 2, N], U8, "en_scale")
         nc.gpsimd.memset(en_scale[:].bitcast(I32), 0)
         for q in range(QUADS):
             nc.sync.dma_start(
                 en_scale[32 * q : 32 * q + 4, :, :].bitcast(I32),
-                en_scales[:, 4 * q : 4 * q + 4, :].rearrange("a r n -> r a n").bitcast(I32),
+                en_scales[:, 4 * q : 4 * q + 4, :].rearrange("a e n -> e a n").bitcast(I32),
             )
 
-        quantise_wa(1, 1, held([P, PASS], U32, "wa_codes11"))
+        quantise_wa(1, 1, pieces11, held)
 
-        h_codes = [relay_tile([P, J], U32, "h_codes0", 2048), held([P, J], U32, "h_codes1")]
+        h_codes = [placed(relay, h_codes_at)([P, J], U32, "h_codes0"), held([P, J], U32, "h_codes1")]
         h_scale = [held([P, J], U8, "h_scale%d" % b) for b in range(2)]
         h_bf16, h_chunk = {}, {}
 
-        def new_h(b, lo, hi, offset=None):
-            shape, name = [P, hi - lo, PACK], "h_bf16_%d_%d" % (b, lo)
-            h_bf16[b, lo] = held(shape, BF16, name) if offset is None else relay_tile(shape, BF16, name, offset)
+        def new_h(b, lo, hi, make):
+            h_bf16[b, lo] = make([P, hi - lo, PACK], BF16, "h_bf16_%d_%d" % (b, lo))
             for j0 in range(lo, hi, JC):
                 h_chunk[b, j0 // JC] = h_bf16[b, lo][:, j0 - lo : j0 - lo + JC, :]
 
+        def hb_bank(b, c):
+            return HB_BANKS[(b * CHUNKS + c) % len(HB_BANKS)]
+
         def join(b, c):
-            bank = bank_tile(2 + (b * CHUNKS + c) % 3)
+            bank = bank_tile(hb_bank(b, c), [P, PACK, JC])
             h, j0 = divmod(c * JC, HALF)
             for t in range(PACK):
                 cols = slice(b * PASS + t * P, b * PASS + (t + 1) * P)
@@ -253,52 +267,46 @@ def tile_list_kg_mul_none_kernel(
 
         out_rows = out.rearrange("(u p) j -> p u j", p=P)
 
-        def score_pass(dst, u, b, lo, hi):
+        def score(dst, u, lo, hi):
             cols = slice(u * P, (u + 1) * P)
-            nc.tensor.matmul_mx(
-                out=dst,
-                lhsT=en_codes[:, b, cols].bitcast(FP8X4),
-                lhsT_scale=en_scale[:, b, cols],
-                rhs=h_codes[b][:, lo:hi].bitcast(FP8X4),
-                rhs_scale=h_scale[b][:, lo:hi],
-                start=(b == 0),
-                stop=(b == 1),
-            )
+            for b in range(2):
+                nc.tensor.matmul_mx(
+                    out=dst,
+                    lhsT=en_codes[:, b, cols].bitcast(FP8X4),
+                    lhsT_scale=en_scale[:, b, cols],
+                    rhs=h_codes[b][:, lo:hi].bitcast(FP8X4),
+                    rhs_scale=h_scale[b][:, lo:hi],
+                    start=(b == 0),
+                    stop=(b == 1),
+                )
 
-        def store(lo, hi, banks):
+        def finish(lo, hi):
+            if hi - lo == HALF:
+                scored = [bank_tile(n, [P, 1, HALF]) for n in SPARE_BANKS]
+            else:
+                scored = [bank_tile(hb_bank(1, hi // JC - 1), [P, 2, hi - lo])]
+            per_bank = 2 // len(scored)
+            for u in range(2):
+                score(scored[u // per_bank][:, u % per_bank, :], u, lo, hi)
             result = held([P, 2, hi - lo], F32, "result%d" % lo)
-            per_bank = 2 // len(banks)
-            for n, bank in enumerate(banks):
+            for n, bank in enumerate(scored):
                 nc.scalar.copy(result[:, n * per_bank : (n + 1) * per_bank, :], bank[:])
             nc.sync.dma_start(out_rows[:, :, lo:hi], result[:])
 
-        def finish(lo, hi):
-            if lo == 0:
-                wide = [psum.tile([P, 1, HALF], F32, name="bank", tag="bank%d" % (6 + u)) for u in range(2)]
-                for u in range(2):
-                    for b in range(2):
-                        score_pass(wide[u][:, 0, :], u, b, lo, hi)
-                store(lo, hi, wide)
-            else:
-                last = hi // JC - 1
-                bank = psum.tile([P, 2, hi - lo], F32, name="bank", tag="bank%d" % (2 + (CHUNKS + last) % 3))
-                for u in range(2):
-                    for b in range(2):
-                        score_pass(bank[:, u, :], u, b, lo, hi)
-                store(lo, hi, [bank])
-
         quarters = [(lo, lo + J // 4) for lo in range(0, J, J // 4)]
         for n, (lo, hi) in enumerate(quarters):
-            new_h(0, lo, hi, (None, None, 0, None)[n])
+            new_h(0, lo, hi, placed(relay, h_quarter_at) if n == 2 else held)
         for lo, hi in SCORE_RANGES:
-            new_h(1, lo, hi)
+            new_h(1, lo, hi, held)
         ends = {hi // JC: (0, lo, hi) for lo, hi in quarters}
         for lo, hi in SCORE_RANGES:
             ends[CHUNKS + hi // JC] = (1, lo, hi)
         for step in range(2 * CHUNKS + 1):
-            c = step - 5
+            c = step + HA1_LEAD - CHUNKS
             if 0 <= c < CHUNKS:
-                copy_a(1, c, project_a(1, c, bank_tile((6, 7, 5, 0, 1, 5, 0, 1)[c])))
+                later = c - len(SPARE_BANKS)
+                n = SPARE_BANKS[c] if later < 0 else HA1_BANKS[later % len(HA1_BANKS)]
+                copy_a(1, c, project_a(1, c, n), held)
             if step < 2 * CHUNKS:
                 join(*divmod(step, CHUNKS))
             if step in ends:

@@ -14,6 +14,7 @@ U8 = mybir.dt.uint8
 FP8X4 = mybir.dt.float8_e4m3fn_x4
 FP4X4 = mybir.dt.float4_e2m1fn_x4
 MULT = mybir.AluOpType.mult
+ADD = mybir.AluOpType.add
 
 P = 128
 PACK = 4
@@ -24,14 +25,12 @@ HALF = J // 2
 JC = 128
 CHUNKS = J // JC
 CHUNK_BYTES = JC * PACK * 4
-TAB_RANGES = ((0, 256), (256, 512), (512, 1024))
+TAB_STEP = 256
 SCORE_RANGES = ((0, 512), (512, 768), (768, 896), (896, 1024))
-HA0_BANKS = 6
-HB_BANKS = (2, 3, 4)
-SPARE_BANKS = (6, 7)
-HA1_BANKS = (5, 0, 1)
-COPIES_BEFORE_LAST_WA = 5
-HA1_LEAD = 3
+H0_RANGES = ((0, 512), (512, 768), (768, 1024))
+HB1_BANKS = (0, 1, 2)
+HA1_BANKS = (3, 4, 5, 6, 7)
+SCORE_BANKS = ((6, 7), (0,), (1,), (2,))
 
 
 def as_words(dram_pass):
@@ -46,9 +45,8 @@ def tile_list_kg_mul_none_kernel(
         lists = ctx.enter_context(tc.tile_pool(name="lists", bufs=1))
         keep = ctx.enter_context(tc.tile_pool(name="keep", bufs=1))
         second = ctx.enter_context(tc.tile_pool(name="second", bufs=1))
-        last_wa = ctx.enter_context(tc.tile_pool(name="last_wa", bufs=1))
-        third_wa = ctx.enter_context(tc.tile_pool(name="third_wa", bufs=1))
-        relay = ctx.enter_context(tc.tile_pool(name="relay", bufs=1))
+        raw0 = ctx.enter_context(tc.tile_pool(name="raw0", bufs=1))
+        raw1 = ctx.enter_context(tc.tile_pool(name="raw1", bufs=1))
         psum = ctx.enter_context(tc.psum_pool(name="psum", bufs=1))
 
         def held(shape, dtype, name):
@@ -73,23 +71,22 @@ def tile_list_kg_mul_none_kernel(
         nc.gpsimd.memset(wb_scale_raw[:].bitcast(I32), 0)
         nc.gpsimd.memset(tab_scale1[96:128, :].bitcast(I32), 0)
 
-        def load_wa(b, a, make):
-            raw = make([P, PACK, PASS], F32, "wa_raw%d%d" % (b, a))
-            rows = wa[a * PASS : (a + 1) * PASS, b * PASS : (b + 1) * PASS]
+        def load_wa(b, a, lo, hi, make):
+            raw = make([P, PACK, hi - lo], F32, "wa_raw%d%d_%d" % (b, a, lo))
+            rows = wa[a * PASS : (a + 1) * PASS, b * PASS + lo : b * PASS + hi]
             nc.sync.dma_start(raw[:], rows.rearrange("(p i) c -> p i c", i=PACK))
             return raw
 
         nc.sync.dma_start(list2[:], offs2)
         nc.sync.dma_start(tab2_scale_win[112:128, :].bitcast(I32), tab2_scales[0].bitcast(I32))
-        wa_raw = {(0, 0): load_wa(0, 0, held)}
         nc.sync.dma_start(list1[:], offs)
         tab_scale_rows = tab_scales.rearrange("a (q e) t -> e q a t", e=4)
         for e in range(4):
             nc.sync.dma_start(tab_scale_win[e:P:16, :].bitcast(I32), tab_scale_rows[e].bitcast(I32))
-        tab_win = keep.tile([P, T], I32, name="tab_win", tag="tab_then_wb", align_bytes=64)
+        tab_win = held([P, T], I32, "tab_win")
         nc.sync.dma_start(tab_win[:], as_words(tab_words[0]))
-        wa_raw[0, 1] = load_wa(0, 1, held)
-        wa_raw[1, 0] = load_wa(1, 0, placed(third_wa, 0))
+        raw00 = [load_wa(0, 0, lo, lo + PASS // 2, placed(raw0, 8 * PASS - 16 * lo)) for lo in (0, PASS // 2)]
+        raw01 = [load_wa(0, 1, lo, lo + PASS // 2, placed(raw1, 16 * lo)) for lo in (0, PASS // 2)]
         for q in range(QUADS):
             nc.sync.dma_start(
                 wb_scale_raw[32 * q : 32 * q + 4, :].bitcast(I32), wb_scales[0, 4 * q : 4 * q + 4, :].bitcast(I32)
@@ -114,21 +111,22 @@ def tile_list_kg_mul_none_kernel(
                 tab2_scale_picked[112 + 4 * q : 116 + 4 * q, :].bitcast(I32),
             )
 
-        wa_codes, wa_scale = {}, {}
-
-        def round_wa(b, a, dst, t0):
-            src = wa_raw[b, a][:].rearrange("p i (m t) -> p m i t", t=PACK)
+        def round_wa(raw, dst, t0):
+            src = raw[:].rearrange("p i (m t) -> p m i t", t=PACK)
             nc.scalar.copy(dst, src[:, :, :, t0 : t0 + 2])
 
-        def round_wa_whole(b, a, make):
-            grouped = make([P, PASS * PACK], BF16, "wa_grouped%d%d" % (b, a))
-            dst = grouped[:].rearrange("p (t m i) -> p m i t", t=PACK, i=PACK)
-            for t0 in range(0, PACK, 2):
-                round_wa(b, a, dst[:, :, :, t0 : t0 + 2], t0)
-            return grouped
+        def round_wa_pool(raw, grouped, ts, at, t0):
+            src = raw[:].rearrange("p i (m t) -> p m t i", t=PACK)
+            dst = grouped[:].rearrange("p (t m i) -> p m t i", t=ts, i=PACK)
+            nc.gpsimd.tensor_scalar(dst[:, :, at : at + 2, :], src[:, :, t0 : t0 + 2, :], 1.0, 0.0, MULT, ADD)
 
-        def quantise_wa(b, a, pieces, make):
-            wa_codes[b, a] = make([P, PASS], U32, "wa_codes%d%d" % (b, a))
+        def by_t(grouped, ts):
+            return grouped[:].rearrange("p (t m i) -> p m i t", t=ts, i=PACK)
+
+        wa_codes, wa_scale = {}, {}
+
+        def quantise_wa(b, a, pieces):
+            wa_codes[b, a] = held([P, PASS], U32, "wa_codes%d%d" % (b, a))
             wa_scale[b, a] = held([P, PASS], U8, "wa_scale%d%d" % (b, a))
             width = PASS // len(pieces)
             for n, piece in enumerate(pieces):
@@ -142,20 +140,30 @@ def tile_list_kg_mul_none_kernel(
 
         tab_codes = {}
 
-        def pick_tab(lo, hi):
-            pairs = keep.tile([P, hi - lo], U32, name="tab_pairs%d" % lo, tag="pairs", bufs=2, align_bytes=64)
+        def pick_tab(lo, pairs):
+            hi = lo + TAB_STEP
             nc.vector.tensor_copy(pairs[:], tab_win[:].bitcast(U32).indirect(part_of(list1, lo, hi)))
-            parted = held([P, 2, 2 * (hi - lo)], U8, "tab_codes%d" % lo)
+            parted = held([P, 2, 2 * TAB_STEP], U8, "tab_codes%d" % lo)
             nc.vector.tensor_copy(parted[:].bitcast(U16), pairs[:].bitcast(U16).rearrange("p (j d) -> p d j", d=2))
             for j0 in range(lo, hi, JC):
                 tab_codes[j0 // JC] = parted[:, :, 2 * (j0 - lo) : 2 * (j0 - lo + JC)]
 
-        last_wa_at = PASS * PACK
-        quantise_wa(0, 0, [round_wa_whole(0, 0, placed(last_wa, 0))], held)
-        wa_raw[1, 1] = load_wa(1, 1, placed(last_wa, last_wa_at))
-        for lo, hi in TAB_RANGES:
-            pick_tab(lo, hi)
-        quantise_wa(0, 1, [round_wa_whole(0, 1, held)], held)
+        for lo in (0, TAB_STEP):
+            pick_tab(lo, held([P, TAB_STEP], U32, "tab_pairs%d" % lo))
+        grouped00 = held([P, PASS * PACK], BF16, "wa_grouped00")
+        for n in range(2):
+            for t0 in (0, 2):
+                round_wa(raw00[n], by_t(grouped00, PACK)[:, 64 * n : 64 * n + 64, :, t0 : t0 + 2], t0)
+        quantise_wa(0, 0, [grouped00])
+        raw10 = load_wa(1, 0, 0, PASS, placed(raw0, 8 * PASS))
+        for lo in (HALF, HALF + TAB_STEP):
+            pick_tab(lo, placed(raw0, 4 * (lo - HALF))([P, TAB_STEP], U32, "tab_pairs%d" % lo))
+        grouped01 = held([P, PASS * PACK], BF16, "wa_grouped01")
+        for n in range(2):
+            for t0 in (0, 2):
+                round_wa(raw01[n], by_t(grouped01, PACK)[:, 64 * n : 64 * n + 64, :, t0 : t0 + 2], t0)
+        quantise_wa(0, 1, [grouped01])
+        raw11 = load_wa(1, 1, 0, PASS, placed(raw1, 0))
 
         def bank_tile(n, shape):
             return psum.tile(shape, F32, name="bank", tag="bank%d" % n)
@@ -176,43 +184,30 @@ def tile_list_kg_mul_none_kernel(
                     )
             return bank
 
-        ha_sb = {}
+        def by_query(bank):
+            return bank[:].rearrange("p t j -> p j t")
 
-        def copy_a(b, c, bank, make):
-            ha_sb[b, c] = make([P, JC, PACK], F32, "ha%d_%d" % (b, c))
-            nc.scalar.copy(ha_sb[b, c][:], bank[:].rearrange("p t j -> p j t"))
+        def copy_out(bank, make, name):
+            kept = make([P, JC, PACK], F32, name)
+            nc.scalar.copy(kept[:], by_query(bank))
+            return kept
 
-        grouped10 = round_wa_whole(1, 0, held)
-        banks = []
+        ha0 = []
         for c in range(CHUNKS):
-            banks.append(project_a(0, c, c % HA0_BANKS))
-            if c < COPIES_BEFORE_LAST_WA:
-                copy_a(0, c, banks[c], placed(third_wa, 0) if c == 0 else held)
-        piece_bytes = PASS * PACK
-        late_piece_at = 4 * piece_bytes
-        h_codes_at = late_piece_at + piece_bytes // 2 - 4 * J
-        h_quarter_at = late_piece_at + piece_bytes // 2
-        pieces11 = []
-        for n, offset in enumerate((0, late_piece_at)):
-            pieces11.append(placed(relay, offset)([P, 2 * PASS], BF16, "wa_grouped11_%d" % n))
-            round_wa(1, 1, pieces11[n][:].rearrange("p (t m i) -> p m i t", t=2, i=PACK), 2 * n)
-        for c in range(COPIES_BEFORE_LAST_WA, CHUNKS):
-            copy_a(0, c, banks[c], placed(last_wa, last_wa_at + (c - COPIES_BEFORE_LAST_WA) * CHUNK_BYTES))
+            ha0.append(copy_out(project_a(0, c, c), held, "ha0_%d" % c))
 
-        wb_codes = keep.tile([P, R], I32, name="wb_codes", tag="tab_then_wb", align_bytes=64)
+        wb_codes = held([P, R], I32, "wb_codes")
         wb_scale = held([P, R], U8, "wb_scale")
         nc.vector.tensor_copy(
-            wb_scale[:].rearrange("p (b t m) -> p b t m", b=2, t=PACK),
-            wb_scale_raw[:].rearrange("p (b m t) -> p b t m", b=2, t=PACK),
+            wb_codes[:].rearrange("p (b t c m) -> p b c t m", b=2, t=PACK, m=4),
+            wb_raw[:].rearrange("p (b c m t) -> p b c t m", b=2, t=PACK, m=4),
         )
         nc.vector.tensor_copy(
-            wb_codes[:].rearrange("p (b t m) -> p b m t", b=2, t=PACK),
-            wb_raw[:].rearrange("p (b m t) -> p b m t", b=2, t=PACK),
+            wb_scale[:].rearrange("p (b t c m) -> p b c t m", b=2, t=PACK, m=16),
+            wb_scale_raw[:].rearrange("p (b c m t) -> p b c t m", b=2, t=PACK, m=16),
         )
-
-        en_codes = placed(second, wb_at + 2 * R)([P, 2, N], I32, "en_codes")
+        en_codes = placed(second, wb_at)([P, 2, N], I32, "en_codes")
         nc.sync.dma_start(en_codes[:], en_words.rearrange("a p n i -> p a (n i)").bitcast(I32))
-        quantise_wa(1, 0, [grouped10], placed(second, wb_at))
 
         tab2_codes = []
         for h in range(2):
@@ -228,22 +223,8 @@ def tile_list_kg_mul_none_kernel(
                 en_scales[:, 4 * q : 4 * q + 4, :].rearrange("a e n -> e a n").bitcast(I32),
             )
 
-        quantise_wa(1, 1, pieces11, held)
-
-        h_codes = [placed(relay, h_codes_at)([P, J], U32, "h_codes0"), held([P, J], U32, "h_codes1")]
-        h_scale = [held([P, J], U8, "h_scale%d" % b) for b in range(2)]
-        h_bf16, h_chunk = {}, {}
-
-        def new_h(b, lo, hi, make):
-            h_bf16[b, lo] = make([P, hi - lo, PACK], BF16, "h_bf16_%d_%d" % (b, lo))
-            for j0 in range(lo, hi, JC):
-                h_chunk[b, j0 // JC] = h_bf16[b, lo][:, j0 - lo : j0 - lo + JC, :]
-
-        def hb_bank(b, c):
-            return HB_BANKS[(b * CHUNKS + c) % len(HB_BANKS)]
-
-        def join(b, c):
-            bank = bank_tile(hb_bank(b, c), [P, PACK, JC])
+        def project_b(b, c, n):
+            bank = bank_tile(n, [P, PACK, JC])
             h, j0 = divmod(c * JC, HALF)
             for t in range(PACK):
                 cols = slice(b * PASS + t * P, b * PASS + (t + 1) * P)
@@ -256,36 +237,75 @@ def tile_list_kg_mul_none_kernel(
                     start=True,
                     stop=True,
                 )
-            nc.vector.tensor_tensor(h_chunk[b, c], bank[:].rearrange("p t j -> p j t"), ha_sb[b, c][:], MULT)
+            return bank
+
+        h_bf16, h_chunk = {}, {}
+
+        def new_h(b, lo, hi, make):
+            h_bf16[b, lo] = make([P, hi - lo, PACK], BF16, "h_bf16_%d_%d" % (b, lo))
+            for j0 in range(lo, hi, JC):
+                h_chunk[b, j0 // JC] = h_bf16[b, lo][:, j0 - lo : j0 - lo + JC, :]
+
+        def join(b, c, bank, kept):
+            nc.vector.tensor_tensor(h_chunk[b, c], by_query(bank), kept[:], MULT)
+
+        h_scale = [held([P, J], U8, "h_scale%d" % b) for b in range(2)]
+        h_codes = {}
 
         def quantise_h(b, lo, hi):
+            codes, at = h_codes[b, lo // HALF]
             nc.vector.quantize_mx(
-                out=h_codes[b][:, lo:hi].bitcast(FP8X4),
+                out=codes[:, lo - at : hi - at].bitcast(FP8X4),
                 scales=h_scale[b][:, lo:hi],
                 in_=h_bf16[b, lo][:].rearrange("p j t -> p (j t)"),
             )
 
+        grouped10 = held([P, PASS * PACK], BF16, "wa_grouped10")
+        for t0 in (0, 2):
+            round_wa_pool(raw10, grouped10, PACK, t0, t0)
+        pieces11 = [held([P, 2 * PASS], BF16, "wa_grouped11_%d" % n) for n in range(2)]
+        for n in range(2):
+            round_wa(raw11, by_t(pieces11[n], 2), 2 * n)
+
+        new_h(0, 0, 512, held)
+        for c in range(4):
+            join(0, c, project_b(0, c, c), ha0[c])
+        quantise_wa(1, 0, [grouped10])
+        new_h(0, 512, 768, placed(raw0, 8 * PASS))
+        for c in range(4, 6):
+            join(0, c, project_b(0, c, c), ha0[c])
+        h_codes0 = placed(raw0, 12 * PASS)([P, J], U32, "h_codes0")
+        h_codes[0, 0] = (h_codes0, 0)
+        h_codes[0, 1] = (h_codes0, 0)
+        quantise_h(0, 0, 512)
+        quantise_h(0, 512, 768)
+        quantise_wa(1, 1, pieces11)
+        new_h(0, 768, 1024, placed(raw1, len(HB1_BANKS) * CHUNK_BYTES))
+        for c in range(6, CHUNKS):
+            join(0, c, project_b(0, c, c), ha0[c])
+
+        h_codes1 = held([P, J], U32, "h_codes1")
+        h_codes[1, 0] = (h_codes1, 0)
+        h_codes[1, 1] = (h_codes1, 0)
         out_rows = out.rearrange("(u p) j -> p u j", p=P)
 
         def score(dst, u, lo, hi):
             cols = slice(u * P, (u + 1) * P)
             for b in range(2):
+                codes, at = h_codes[b, lo // HALF]
                 nc.tensor.matmul_mx(
                     out=dst,
                     lhsT=en_codes[:, b, cols].bitcast(FP8X4),
                     lhsT_scale=en_scale[:, b, cols],
-                    rhs=h_codes[b][:, lo:hi].bitcast(FP8X4),
+                    rhs=codes[:, lo - at : hi - at].bitcast(FP8X4),
                     rhs_scale=h_scale[b][:, lo:hi],
                     start=(b == 0),
                     stop=(b == 1),
                 )
 
-        def finish(lo, hi):
-            if hi - lo == HALF:
-                scored = [bank_tile(n, [P, 1, HALF]) for n in SPARE_BANKS]
-            else:
-                scored = [bank_tile(hb_bank(1, hi // JC - 1), [P, 2, hi - lo])]
-            per_bank = 2 // len(scored)
+        def finish(lo, hi, banks):
+            per_bank = 2 // len(banks)
+            scored = [bank_tile(n, [P, per_bank, hi - lo]) for n in banks]
             for u in range(2):
                 score(scored[u // per_bank][:, u % per_bank, :], u, lo, hi)
             result = held([P, 2, hi - lo], F32, "result%d" % lo)
@@ -293,23 +313,24 @@ def tile_list_kg_mul_none_kernel(
                 nc.scalar.copy(result[:, n * per_bank : (n + 1) * per_bank, :], bank[:])
             nc.sync.dma_start(out_rows[:, :, lo:hi], result[:])
 
-        quarters = [(lo, lo + J // 4) for lo in range(0, J, J // 4)]
-        for n, (lo, hi) in enumerate(quarters):
-            new_h(0, lo, hi, placed(relay, h_quarter_at) if n == 2 else held)
         for lo, hi in SCORE_RANGES:
             new_h(1, lo, hi, held)
-        ends = {hi // JC: (0, lo, hi) for lo, hi in quarters}
-        for lo, hi in SCORE_RANGES:
-            ends[CHUNKS + hi // JC] = (1, lo, hi)
-        for step in range(2 * CHUNKS + 1):
-            c = step + HA1_LEAD - CHUNKS
-            if 0 <= c < CHUNKS:
-                later = c - len(SPARE_BANKS)
-                n = SPARE_BANKS[c] if later < 0 else HA1_BANKS[later % len(HA1_BANKS)]
-                copy_a(1, c, project_a(1, c, n), held)
-            if step < 2 * CHUNKS:
-                join(*divmod(step, CHUNKS))
-            if step in ends:
-                quantise_h(*ends[step])
-                if step > CHUNKS:
-                    finish(*ends[step][1:])
+        ends = {hi // JC: (n, lo, hi) for n, (lo, hi) in enumerate(SCORE_RANGES)}
+        hb1 = []
+
+        def make_hb1(c):
+            make = placed(raw1, c * CHUNK_BYTES) if c < len(HB1_BANKS) else held
+            hb1.append(copy_out(project_b(1, c, HB1_BANKS[c % len(HB1_BANKS)]), make, "hb1_%d" % c))
+
+        make_hb1(0)
+        for c in range(CHUNKS + 1):
+            if c + 1 < CHUNKS:
+                make_hb1(c + 1)
+            if c < CHUNKS:
+                join(1, c, project_a(1, c, HA1_BANKS[c % len(HA1_BANKS)]), hb1[c])
+            if c == 0:
+                quantise_h(0, 768, 1024)
+            if c in ends:
+                n, lo, hi = ends[c]
+                quantise_h(1, lo, hi)
+                finish(lo, hi, SCORE_BANKS[n])

@@ -26,11 +26,20 @@ JC = 128
 CHUNKS = J // JC
 CHUNK_BYTES = JC * PACK * 4
 TAB_STEP = 256
-SCORE_RANGES = ((0, 512), (512, 768), (768, 896), (896, 1024))
+SCORE_RANGES = ((0, 256), (256, 512), (512, 768), (768, 896), (896, 1024))
 H0_RANGES = ((0, 512), (512, 768), (768, 1024))
 HB1_BANKS = (0, 1, 2)
-HA1_BANKS = (3, 4, 5, 6, 7)
-SCORE_BANKS = ((6, 7), (0,), (1,), (2,))
+HA1_BANKS = (3, 6, 7, 4, 5)
+SCORE_BANKS = ((4,), (5,), (2,), (0,), (1,))
+BANKS = 8
+RAW00 = 6144
+RAW10 = RAW00 + 64 + 2 * J
+PAIRS = 8 * T
+H01 = RAW10 + 16 * PASS
+RAW01 = H01 + 4 * HALF + 64
+RAW11 = RAW01 - 128
+HA1_LEAD = 2
+HA0_AHEAD = 6
 
 
 def as_words(dram_pass):
@@ -45,8 +54,8 @@ def tile_list_kg_mul_none_kernel(
         lists = ctx.enter_context(tc.tile_pool(name="lists", bufs=1))
         keep = ctx.enter_context(tc.tile_pool(name="keep", bufs=1))
         second = ctx.enter_context(tc.tile_pool(name="second", bufs=1))
+        early = ctx.enter_context(tc.tile_pool(name="early", bufs=1))
         raw0 = ctx.enter_context(tc.tile_pool(name="raw0", bufs=1))
-        raw1 = ctx.enter_context(tc.tile_pool(name="raw1", bufs=1))
         psum = ctx.enter_context(tc.psum_pool(name="psum", bufs=1))
 
         def held(shape, dtype, name):
@@ -83,14 +92,13 @@ def tile_list_kg_mul_none_kernel(
         tab_scale_rows = tab_scales.rearrange("a (q e) t -> e q a t", e=4)
         for e in range(4):
             nc.sync.dma_start(tab_scale_win[e:P:16, :].bitcast(I32), tab_scale_rows[e].bitcast(I32))
-        tab_win = held([P, T], I32, "tab_win")
+        tab_win = placed(early, 0)([P, T], I32, "tab_win")
         nc.sync.dma_start(tab_win[:], as_words(tab_words[0]))
-        raw00 = [load_wa(0, 0, lo, lo + PASS // 2, placed(raw0, 8 * PASS - 16 * lo)) for lo in (0, PASS // 2)]
-        raw01 = [load_wa(0, 1, lo, lo + PASS // 2, placed(raw1, 16 * lo)) for lo in (0, PASS // 2)]
-        for q in range(QUADS):
-            nc.sync.dma_start(
-                wb_scale_raw[32 * q : 32 * q + 4, :].bitcast(I32), wb_scales[0, 4 * q : 4 * q + 4, :].bitcast(I32)
-            )
+        raw00 = load_wa(0, 0, 0, PASS, placed(raw0, RAW00))
+        raw01 = load_wa(0, 1, 0, PASS, placed(raw0, RAW01))
+        wb_scale_rows = wb_scales[0].rearrange("(q e) r -> e q r", e=4)
+        for e in range(4):
+            nc.sync.dma_start(wb_scale_raw[e:P:32, :].bitcast(I32), wb_scale_rows[e].bitcast(I32))
 
         tab2_scale_picked = held([P, J], U8, "tab2_scale_picked")
         nc.vector.tensor_copy(tab2_scale_picked[:], tab2_scale_win[:].indirect(list2[:]))
@@ -99,34 +107,29 @@ def tile_list_kg_mul_none_kernel(
         nc.sync.dma_start(tab_scale1[0:112, :].bitcast(I32), tab_scale0[16:128, :].bitcast(I32))
         tab_scale = (tab_scale0, tab_scale1)
 
-        wb_raw = placed(second, wb_at)([P, R], I32, "wb_raw")
+        wb_raw = [placed(second, 4 * PASS)([P, PASS], I32, "wb_raw0")]
         tab2_win = placed(second, tab2_at)([P, T], I32, "tab2_win")
-        nc.sync.dma_start(wb_raw[:], as_words(wb_words[0]))
+        nc.sync.dma_start(wb_raw[0][:], as_words(wb_words[0])[:, 0:PASS])
         nc.sync.dma_start(tab2_win[:], as_words(tab2_words[0]))
         tab2_scale = placed(second, tab2_scale_at)([P, J], U8, "tab2_scale")
         nc.gpsimd.memset(tab2_scale[:].bitcast(I32), 0)
-        for q in range(QUADS):
-            nc.sync.dma_start(
-                tab2_scale[32 * q : 32 * q + 4, :].bitcast(I32),
-                tab2_scale_picked[112 + 4 * q : 116 + 4 * q, :].bitcast(I32),
-            )
+        for e in range(4):
+            nc.sync.dma_start(tab2_scale[e:P:32, :].bitcast(I32), tab2_scale_picked[112 + e : P : 4, :].bitcast(I32))
 
-        def round_wa(raw, dst, t0):
+        def round_wa(raw, grouped, lo, hi):
             src = raw[:].rearrange("p i (m t) -> p m i t", t=PACK)
-            nc.scalar.copy(dst, src[:, :, :, t0 : t0 + 2])
+            dst = grouped[:].rearrange("p (t m i) -> p m i t", t=PACK, i=PACK)
+            nc.scalar.copy(dst[:, lo:hi], src)
 
-        def round_wa_pool(raw, grouped, ts, at, t0):
+        def round_wa_pool(raw, grouped, lo, hi):
             src = raw[:].rearrange("p i (m t) -> p m t i", t=PACK)
-            dst = grouped[:].rearrange("p (t m i) -> p m t i", t=ts, i=PACK)
-            nc.gpsimd.tensor_scalar(dst[:, :, at : at + 2, :], src[:, :, t0 : t0 + 2, :], 1.0, 0.0, MULT, ADD)
-
-        def by_t(grouped, ts):
-            return grouped[:].rearrange("p (t m i) -> p m i t", t=ts, i=PACK)
+            dst = grouped[:].rearrange("p (t m i) -> p m t i", t=PACK, i=PACK)
+            nc.gpsimd.tensor_scalar(dst[:, lo:hi], src, 1.0, 0.0, MULT, ADD)
 
         wa_codes, wa_scale = {}, {}
 
-        def quantise_wa(b, a, pieces):
-            wa_codes[b, a] = held([P, PASS], U32, "wa_codes%d%d" % (b, a))
+        def quantise_wa(b, a, pieces, make):
+            wa_codes[b, a] = make([P, PASS], U32, "wa_codes%d%d" % (b, a))
             wa_scale[b, a] = held([P, PASS], U8, "wa_scale%d%d" % (b, a))
             width = PASS // len(pieces)
             for n, piece in enumerate(pieces):
@@ -140,30 +143,49 @@ def tile_list_kg_mul_none_kernel(
 
         tab_codes = {}
 
-        def pick_tab(lo, pairs):
-            hi = lo + TAB_STEP
-            nc.vector.tensor_copy(pairs[:], tab_win[:].bitcast(U32).indirect(part_of(list1, lo, hi)))
-            parted = held([P, 2, 2 * TAB_STEP], U8, "tab_codes%d" % lo)
+        def gather_tab(lo):
+            pairs = (placed(early, PAIRS + 16 * (lo - HALF)) if lo >= HALF else held)([P, TAB_STEP], U32, "tab_pairs%d" % lo)
+            nc.vector.tensor_copy(pairs[:], tab_win[:].bitcast(U32).indirect(part_of(list1, lo, lo + TAB_STEP)))
+            return pairs
+
+        def part_tab(lo, pairs, make):
+            parted = make([P, 2, 2 * TAB_STEP], U8, "tab_codes%d" % lo)
             nc.vector.tensor_copy(parted[:].bitcast(U16), pairs[:].bitcast(U16).rearrange("p (j d) -> p d j", d=2))
-            for j0 in range(lo, hi, JC):
+            for j0 in range(lo, lo + TAB_STEP, JC):
                 tab_codes[j0 // JC] = parted[:, :, 2 * (j0 - lo) : 2 * (j0 - lo + JC)]
 
+        pairs = {lo: gather_tab(lo) for lo in (0, TAB_STEP)}
         for lo in (0, TAB_STEP):
-            pick_tab(lo, held([P, TAB_STEP], U32, "tab_pairs%d" % lo))
+            part_tab(lo, pairs[lo], held)
+        pairs = {lo: gather_tab(lo) for lo in (HALF, HALF + TAB_STEP)}
         grouped00 = held([P, PASS * PACK], BF16, "wa_grouped00")
-        for n in range(2):
-            for t0 in (0, 2):
-                round_wa(raw00[n], by_t(grouped00, PACK)[:, 64 * n : 64 * n + 64, :, t0 : t0 + 2], t0)
-        quantise_wa(0, 0, [grouped00])
-        raw10 = load_wa(1, 0, 0, PASS, placed(raw0, 8 * PASS))
+        round_wa(raw00, grouped00, 0, P)
+        quantise_wa(0, 0, [grouped00], placed(early, 0))
         for lo in (HALF, HALF + TAB_STEP):
-            pick_tab(lo, placed(raw0, 4 * (lo - HALF))([P, TAB_STEP], U32, "tab_pairs%d" % lo))
+            part_tab(lo, pairs[lo], placed(raw0, RAW00 + 64 + 4 * (lo - HALF)))
+        wb_raw.append(placed(raw0, RAW00 + 64 - 4 * PASS)([P, PASS], I32, "wb_raw1"))
+        nc.sync.dma_start(wb_raw[1][:], as_words(wb_words[0])[:, PASS:R])
+        raw10 = [load_wa(1, 0, lo, lo + PASS // 2, placed(raw0, RAW10 + 16 * lo)) for lo in (0, PASS // 2)]
+        wb_codes = {}
+        wb_scale = placed(early, PAIRS + 64 - R)([P, R], U8, "wb_scale")
+
+        def reorder_wb(b, make):
+            wb_codes[b] = make([P, PASS], I32, "wb_codes%d" % b)
+            nc.vector.tensor_copy(
+                wb_codes[b][:].rearrange("p (t c m) -> p c t m", t=PACK, m=4),
+                wb_raw[b][:].rearrange("p (c m t) -> p c t m", t=PACK, m=4),
+            )
+
+        reorder_wb(0, placed(early, PAIRS + 64))
+        nc.vector.tensor_copy(
+            wb_scale[:].rearrange("p (b t c m) -> p b c t m", b=2, t=PACK, m=16),
+            wb_scale_raw[:].rearrange("p (b c m t) -> p b c t m", b=2, t=PACK, m=16),
+        )
+
         grouped01 = held([P, PASS * PACK], BF16, "wa_grouped01")
-        for n in range(2):
-            for t0 in (0, 2):
-                round_wa(raw01[n], by_t(grouped01, PACK)[:, 64 * n : 64 * n + 64, :, t0 : t0 + 2], t0)
-        quantise_wa(0, 1, [grouped01])
-        raw11 = load_wa(1, 1, 0, PASS, placed(raw1, 0))
+        round_wa(raw01, grouped01, 0, P)
+        quantise_wa(0, 1, [grouped01], placed(early, PAIRS + 16 * TAB_STEP))
+        raw11 = load_wa(1, 1, 0, PASS, placed(raw0, RAW11))
 
         def bank_tile(n, shape):
             return psum.tile(shape, F32, name="bank", tag="bank%d" % n)
@@ -193,35 +215,24 @@ def tile_list_kg_mul_none_kernel(
             return kept
 
         ha0 = []
-        for c in range(CHUNKS):
-            ha0.append(copy_out(project_a(0, c, c), held, "ha0_%d" % c))
-
-        wb_codes = held([P, R], I32, "wb_codes")
-        wb_scale = held([P, R], U8, "wb_scale")
-        nc.vector.tensor_copy(
-            wb_codes[:].rearrange("p (b t c m) -> p b c t m", b=2, t=PACK, m=4),
-            wb_raw[:].rearrange("p (b c m t) -> p b c t m", b=2, t=PACK, m=4),
-        )
-        nc.vector.tensor_copy(
-            wb_scale[:].rearrange("p (b t c m) -> p b c t m", b=2, t=PACK, m=16),
-            wb_scale_raw[:].rearrange("p (b c m t) -> p b c t m", b=2, t=PACK, m=16),
-        )
-        en_codes = placed(second, wb_at)([P, 2, N], I32, "en_codes")
-        nc.sync.dma_start(en_codes[:], en_words.rearrange("a p n i -> p a (n i)").bitcast(I32))
+        for c in range(HA0_AHEAD):
+            make = {0: placed(raw0, 0), 4: placed(early, 5 * T)}.get(c, held)
+            ha0.append(copy_out(project_a(0, c, c), make, "ha0_%d" % c))
 
         tab2_codes = []
         for h in range(2):
-            codes = held([P, HALF], U32, "tab2_codes%d" % h)
+            codes = (placed(raw0, RAW11 + 16 * PASS), held)[h]([P, HALF], U32, "tab2_codes%d" % h)
             nc.vector.tensor_copy(codes[:], tab2_win[:].bitcast(U32).indirect(part_of(list2, h * HALF, (h + 1) * HALF)))
             tab2_codes.append(codes)
 
+        reorder_wb(1, held)
+        en_codes = placed(second, 8 * R + 2 * N)([P, 2, N], I32, "en_codes")
+        nc.sync.dma_start(en_codes[:], en_words.rearrange("a p n i -> p a (n i)").bitcast(I32))
         en_scale = placed(second, 8 * R)([P, 2, N], U8, "en_scale")
         nc.gpsimd.memset(en_scale[:].bitcast(I32), 0)
-        for q in range(QUADS):
-            nc.sync.dma_start(
-                en_scale[32 * q : 32 * q + 4, :, :].bitcast(I32),
-                en_scales[:, 4 * q : 4 * q + 4, :].rearrange("a e n -> e a n").bitcast(I32),
-            )
+        en_scale_rows = en_scales.rearrange("a (q e) n -> e q a n", e=4)
+        for e in range(4):
+            nc.sync.dma_start(en_scale[e:P:32, :, :].bitcast(I32), en_scale_rows[e].bitcast(I32))
 
         def project_b(b, c, n):
             bank = bank_tile(n, [P, PACK, JC])
@@ -230,7 +241,7 @@ def tile_list_kg_mul_none_kernel(
                 cols = slice(b * PASS + t * P, b * PASS + (t + 1) * P)
                 nc.tensor.matmul_mx(
                     out=bank[:, t, :],
-                    lhsT=wb_codes[:, cols].bitcast(FP8X4),
+                    lhsT=wb_codes[b][:, t * P : (t + 1) * P].bitcast(FP8X4),
                     lhsT_scale=wb_scale[:, cols],
                     rhs=tab2_codes[h][:, j0 : j0 + JC].bitcast(FP8X4),
                     rhs_scale=tab2_scale[:, c * JC : (c + 1) * JC],
@@ -249,6 +260,12 @@ def tile_list_kg_mul_none_kernel(
         def join(b, c, bank, kept):
             nc.vector.tensor_tensor(h_chunk[b, c], by_query(bank), kept[:], MULT)
 
+        def join0(c):
+            join(0, c, project_b(0, c, (c + HA0_AHEAD) % BANKS), ha0[c])
+            later = c + HA0_AHEAD
+            if later < CHUNKS:
+                ha0.append(copy_out(project_a(0, later, later), placed(raw0, RAW10 + 8 * PASS + 64 + c * CHUNK_BYTES), "ha0_%d" % later))
+
         h_scale = [held([P, J], U8, "h_scale%d" % b) for b in range(2)]
         h_codes = {}
 
@@ -260,29 +277,25 @@ def tile_list_kg_mul_none_kernel(
                 in_=h_bf16[b, lo][:].rearrange("p j t -> p (j t)"),
             )
 
-        grouped10 = held([P, PASS * PACK], BF16, "wa_grouped10")
-        for t0 in (0, 2):
-            round_wa_pool(raw10, grouped10, PACK, t0, t0)
-        pieces11 = [held([P, 2 * PASS], BF16, "wa_grouped11_%d" % n) for n in range(2)]
-        for n in range(2):
-            round_wa(raw11, by_t(pieces11[n], 2), 2 * n)
-
         new_h(0, 0, 512, held)
-        for c in range(4):
-            join(0, c, project_b(0, c, c), ha0[c])
-        quantise_wa(1, 0, [grouped10])
-        new_h(0, 512, 768, placed(raw0, 8 * PASS))
-        for c in range(4, 6):
-            join(0, c, project_b(0, c, c), ha0[c])
-        h_codes0 = placed(raw0, 12 * PASS)([P, J], U32, "h_codes0")
-        h_codes[0, 0] = (h_codes0, 0)
-        h_codes[0, 1] = (h_codes0, 0)
-        quantise_h(0, 0, 512)
-        quantise_h(0, 512, 768)
-        quantise_wa(1, 1, pieces11)
-        new_h(0, 768, 1024, placed(raw1, len(HB1_BANKS) * CHUNK_BYTES))
+        new_h(0, 512, 768, held)
+        grouped10 = placed(raw0, 128)([P, PASS * PACK], BF16, "wa_grouped10")
+        round_wa_pool(raw10[0], grouped10, 0, P // 2)
+        round_wa(raw10[1], grouped10, P // 2, P)
+        for c in range(6):
+            join0(c)
+        quantise_wa(1, 0, [grouped10], held)
+        new_h(0, 768, 1024, placed(raw0, RAW10 + 64))
         for c in range(6, CHUNKS):
-            join(0, c, project_b(0, c, c), ha0[c])
+            join0(c)
+        h_codes[0, 0] = (placed(raw0, RAW10 + 64 + 4 * PASS)([P, HALF], U32, "h_codes0_0"), 0)
+        quantise_h(0, 0, 512)
+        grouped11 = placed(early, 5 * T)([P, PASS * PACK], BF16, "wa_grouped11")
+        round_wa(raw11, grouped11, 0, P)
+        quantise_wa(1, 1, [grouped11], placed(raw0, RAW10 + 8 * PASS + 64))
+        h_codes[0, 1] = (placed(raw0, H01)([P, HALF], U32, "h_codes0_1"), HALF)
+        quantise_h(0, 512, 768)
+        quantise_h(0, 768, 1024)
 
         h_codes1 = held([P, J], U32, "h_codes1")
         h_codes[1, 0] = (h_codes1, 0)
@@ -319,18 +332,27 @@ def tile_list_kg_mul_none_kernel(
         hb1 = []
 
         def make_hb1(c):
-            make = placed(raw1, c * CHUNK_BYTES) if c < len(HB1_BANKS) else held
+            make = placed(early, 5 * T + 64 + (c - 1) * CHUNK_BYTES) if c < len(HB1_BANKS) else held
             hb1.append(copy_out(project_b(1, c, HB1_BANKS[c % len(HB1_BANKS)]), make, "hb1_%d" % c))
 
-        make_hb1(0)
-        for c in range(CHUNKS + 1):
-            if c + 1 < CHUNKS:
-                make_hb1(c + 1)
-            if c < CHUNKS:
-                join(1, c, project_a(1, c, HA1_BANKS[c % len(HA1_BANKS)]), hb1[c])
-            if c == 0:
-                quantise_h(0, 768, 1024)
-            if c in ends:
-                n, lo, hi = ends[c]
-                quantise_h(1, lo, hi)
+        ha1 = []
+
+        def make_ha1(c):
+            ha1.append(project_a(1, c, HA1_BANKS[c % len(HA1_BANKS)]))
+
+        for c in range(len(HB1_BANKS)):
+            make_hb1(c)
+        for c in range(HA1_LEAD):
+            make_ha1(c)
+        for c in range(CHUNKS + 2):
+            if c + HA1_LEAD < CHUNKS:
+                make_ha1(c + HA1_LEAD)
+            if c + len(HB1_BANKS) < CHUNKS:
+                make_hb1(c + len(HB1_BANKS))
+            if c - 1 in ends:
+                n, lo, hi = ends[c - 1]
                 finish(lo, hi, SCORE_BANKS[n])
+            if c < CHUNKS:
+                join(1, c, ha1[c], hb1[c])
+            if c in ends:
+                quantise_h(1, *ends[c][1:])

@@ -14,7 +14,6 @@ U8 = mybir.dt.uint8
 FP8X4 = mybir.dt.float8_e4m3fn_x4
 FP4X4 = mybir.dt.float4_e2m1fn_x4
 MULT = mybir.AluOpType.mult
-ADD = mybir.AluOpType.add
 
 P = 128
 PACK = 4
@@ -36,8 +35,8 @@ RAW00 = 6144
 RAW10 = RAW00 + 64 + 2 * J
 PAIRS = 8 * T
 H01 = RAW10 + 16 * PASS
-RAW01 = H01 + 4 * HALF + 64
-RAW11 = RAW01 - 128
+RAW11 = H01 + 4 * HALF - 64
+RAW01 = RAW11 + 16 * PASS
 HA1_LEAD = 2
 HA0_AHEAD = 6
 
@@ -72,7 +71,7 @@ def tile_list_kg_mul_none_kernel(
         tab2_at = tab2_scale_at + J
         tab_scale_win = placed(second, tab2_scale_at - T // 4)([P, T], U8, "tab_scale_win")
         tab2_scale_win = held([P, T], U8, "tab2_scale_win")
-        wb_scale_raw = held([P, R], U8, "wb_scale_raw")
+        wb_scale_raw = placed(raw0, RAW11 + 64)([P, R], U8, "wb_scale_raw")
         tab_scale1 = held([P, J], U8, "tab_scale1")
         nc.gpsimd.memset(tab_scale_win[:].bitcast(I32), 0)
         nc.vector.memset(tab2_scale_win[0:96, :].bitcast(I32), 0)
@@ -92,10 +91,10 @@ def tile_list_kg_mul_none_kernel(
         tab_scale_rows = tab_scales.rearrange("a (q e) t -> e q a t", e=4)
         for e in range(4):
             nc.sync.dma_start(tab_scale_win[e:P:16, :].bitcast(I32), tab_scale_rows[e].bitcast(I32))
+        raw00 = [load_wa(0, 0, lo, lo + PASS // 2, placed(raw0, RAW00 + 8 * PASS - 16 * lo)) for lo in (0, PASS // 2)]
         tab_win = placed(early, 0)([P, T], I32, "tab_win")
         nc.sync.dma_start(tab_win[:], as_words(tab_words[0]))
-        raw00 = load_wa(0, 0, 0, PASS, placed(raw0, RAW00))
-        raw01 = load_wa(0, 1, 0, PASS, placed(raw0, RAW01))
+        raw01 = load_wa(0, 1, 0, PASS, held)
         wb_scale_rows = wb_scales[0].rearrange("(q e) r -> e q r", e=4)
         for e in range(4):
             nc.sync.dma_start(wb_scale_raw[e:P:32, :].bitcast(I32), wb_scale_rows[e].bitcast(I32))
@@ -107,9 +106,9 @@ def tile_list_kg_mul_none_kernel(
         nc.sync.dma_start(tab_scale1[0:112, :].bitcast(I32), tab_scale0[16:128, :].bitcast(I32))
         tab_scale = (tab_scale0, tab_scale1)
 
-        wb_raw = [placed(second, 4 * PASS)([P, PASS], I32, "wb_raw0")]
+        wb_raw = placed(second, wb_at)([P, R], I32, "wb_raw")
         tab2_win = placed(second, tab2_at)([P, T], I32, "tab2_win")
-        nc.sync.dma_start(wb_raw[0][:], as_words(wb_words[0])[:, 0:PASS])
+        nc.sync.dma_start(wb_raw[:], as_words(wb_words[0]))
         nc.sync.dma_start(tab2_win[:], as_words(tab2_words[0]))
         tab2_scale = placed(second, tab2_scale_at)([P, J], U8, "tab2_scale")
         nc.gpsimd.memset(tab2_scale[:].bitcast(I32), 0)
@@ -122,9 +121,9 @@ def tile_list_kg_mul_none_kernel(
             nc.scalar.copy(dst[:, lo:hi], src)
 
         def round_wa_pool(raw, grouped, lo, hi):
-            src = raw[:].rearrange("p i (m t) -> p m t i", t=PACK)
-            dst = grouped[:].rearrange("p (t m i) -> p m t i", t=PACK, i=PACK)
-            nc.gpsimd.tensor_scalar(dst[:, lo:hi], src, 1.0, 0.0, MULT, ADD)
+            src = raw[:].rearrange("p i (m t) -> p t m i", t=PACK)
+            dst = grouped[:].rearrange("p (t m i) -> p t m i", t=PACK, i=PACK)
+            nc.gpsimd.tensor_copy(dst[:, :, lo:hi], src)
 
         wa_codes, wa_scale = {}, {}
 
@@ -143,48 +142,41 @@ def tile_list_kg_mul_none_kernel(
 
         tab_codes = {}
 
-        def gather_tab(lo):
-            pairs = (placed(early, PAIRS + 16 * (lo - HALF)) if lo >= HALF else held)([P, TAB_STEP], U32, "tab_pairs%d" % lo)
-            nc.vector.tensor_copy(pairs[:], tab_win[:].bitcast(U32).indirect(part_of(list1, lo, lo + TAB_STEP)))
+        def gather_tab(lo, hi, make):
+            pairs = make([P, hi - lo], U32, "tab_pairs%d" % lo)
+            nc.vector.tensor_copy(pairs[:], tab_win[:].bitcast(U32).indirect(part_of(list1, lo, hi)))
             return pairs
 
-        def part_tab(lo, pairs, make):
-            parted = make([P, 2, 2 * TAB_STEP], U8, "tab_codes%d" % lo)
+        def part_tab(lo, hi, pairs, make):
+            parted = make([P, 2, 2 * (hi - lo)], U8, "tab_codes%d" % lo)
             nc.vector.tensor_copy(parted[:].bitcast(U16), pairs[:].bitcast(U16).rearrange("p (j d) -> p d j", d=2))
-            for j0 in range(lo, lo + TAB_STEP, JC):
+            for j0 in range(lo, hi, JC):
                 tab_codes[j0 // JC] = parted[:, :, 2 * (j0 - lo) : 2 * (j0 - lo + JC)]
 
-        pairs = {lo: gather_tab(lo) for lo in (0, TAB_STEP)}
-        for lo in (0, TAB_STEP):
-            part_tab(lo, pairs[lo], held)
-        pairs = {lo: gather_tab(lo) for lo in (HALF, HALF + TAB_STEP)}
         grouped00 = held([P, PASS * PACK], BF16, "wa_grouped00")
-        round_wa(raw00, grouped00, 0, P)
-        quantise_wa(0, 0, [grouped00], placed(early, 0))
-        for lo in (HALF, HALF + TAB_STEP):
-            part_tab(lo, pairs[lo], placed(raw0, RAW00 + 64 + 4 * (lo - HALF)))
-        wb_raw.append(placed(raw0, RAW00 + 64 - 4 * PASS)([P, PASS], I32, "wb_raw1"))
-        nc.sync.dma_start(wb_raw[1][:], as_words(wb_words[0])[:, PASS:R])
+        for n in range(2):
+            round_wa(raw00[n], grouped00, n * P // 2, (n + 1) * P // 2)
+        quantise_wa(0, 0, [grouped00], held)
+        pairs0 = gather_tab(0, 256, placed(raw0, RAW00))
+        pairs1 = gather_tab(256, 512, placed(raw0, RAW00 + 64 + R))
+        part_tab(0, 256, pairs0, held)
+        part_tab(256, 512, pairs1, held)
+        pairs2 = gather_tab(512, 1024, placed(raw0, RAW00 + 64 - 4 * HALF))
         raw10 = [load_wa(1, 0, lo, lo + PASS // 2, placed(raw0, RAW10 + 16 * lo)) for lo in (0, PASS // 2)]
-        wb_codes = {}
-        wb_scale = placed(early, PAIRS + 64 - R)([P, R], U8, "wb_scale")
-
-        def reorder_wb(b, make):
-            wb_codes[b] = make([P, PASS], I32, "wb_codes%d" % b)
-            nc.vector.tensor_copy(
-                wb_codes[b][:].rearrange("p (t c m) -> p c t m", t=PACK, m=4),
-                wb_raw[b][:].rearrange("p (c m t) -> p c t m", t=PACK, m=4),
-            )
-
-        reorder_wb(0, placed(early, PAIRS + 64))
+        wb_scale = placed(raw0, RAW00 + 64)([P, R], U8, "wb_scale")
         nc.vector.tensor_copy(
             wb_scale[:].rearrange("p (b t c m) -> p b c t m", b=2, t=PACK, m=16),
             wb_scale_raw[:].rearrange("p (b c m t) -> p b c t m", b=2, t=PACK, m=16),
         )
-
+        part_tab(512, 1024, pairs2, held)
         grouped01 = held([P, PASS * PACK], BF16, "wa_grouped01")
         round_wa(raw01, grouped01, 0, P)
-        quantise_wa(0, 1, [grouped01], placed(early, PAIRS + 16 * TAB_STEP))
+        quantise_wa(0, 1, [grouped01], placed(early, 0))
+        wb_codes = placed(early, 4 * PASS)([P, R], I32, "wb_codes")
+        nc.vector.tensor_copy(
+            wb_codes[:].rearrange("p (b t c m) -> p b c t m", b=2, t=PACK, m=4),
+            wb_raw[:].rearrange("p (b c m t) -> p b c t m", b=2, t=PACK, m=4),
+        )
         raw11 = load_wa(1, 1, 0, PASS, placed(raw0, RAW11))
 
         def bank_tile(n, shape):
@@ -221,11 +213,10 @@ def tile_list_kg_mul_none_kernel(
 
         tab2_codes = []
         for h in range(2):
-            codes = (placed(raw0, RAW11 + 16 * PASS), held)[h]([P, HALF], U32, "tab2_codes%d" % h)
+            codes = placed(second, wb_at + 4 * HALF * h)([P, HALF], U32, "tab2_codes%d" % h)
             nc.vector.tensor_copy(codes[:], tab2_win[:].bitcast(U32).indirect(part_of(list2, h * HALF, (h + 1) * HALF)))
             tab2_codes.append(codes)
 
-        reorder_wb(1, held)
         en_codes = placed(second, 8 * R + 2 * N)([P, 2, N], I32, "en_codes")
         nc.sync.dma_start(en_codes[:], en_words.rearrange("a p n i -> p a (n i)").bitcast(I32))
         en_scale = placed(second, 8 * R)([P, 2, N], U8, "en_scale")
@@ -241,7 +232,7 @@ def tile_list_kg_mul_none_kernel(
                 cols = slice(b * PASS + t * P, b * PASS + (t + 1) * P)
                 nc.tensor.matmul_mx(
                     out=bank[:, t, :],
-                    lhsT=wb_codes[b][:, t * P : (t + 1) * P].bitcast(FP8X4),
+                    lhsT=wb_codes[:, cols].bitcast(FP8X4),
                     lhsT_scale=wb_scale[:, cols],
                     rhs=tab2_codes[h][:, j0 : j0 + JC].bitcast(FP8X4),
                     rhs_scale=tab2_scale[:, c * JC : (c + 1) * JC],

@@ -27,16 +27,14 @@ CHUNK_BYTES = JC * PACK * 4
 TAB_STEP = 256
 SCORE_RANGES = ((0, 256), (256, 512), (512, 768), (768, 896), (896, 1024))
 H0_RANGES = ((0, 512), (512, 768), (768, 1024))
-HB1_BANKS = (0, 1, 2)
-HA1_BANKS = (3, 6, 7, 4, 5)
-SCORE_BANKS = ((4,), (5,), (2,), (0,), (1,))
+HB1_BANKS = (3, 4, 5)
+HA1_BANKS = (0, 1, 2, 6, 7)
+SCORE_BANKS = ((6,), (7,), (5,), (3,), (4,))
 BANKS = 8
 RAW00 = 6144
 RAW10 = RAW00 + 64 + 2 * J
 PAIRS = 8 * T
-H01 = RAW10 + 16 * PASS
-RAW11 = H01 + 4 * HALF - 64
-RAW01 = RAW11 + 16 * PASS
+RAW11 = RAW10 + 20 * PASS
 HA1_LEAD = 2
 HA0_AHEAD = 6
 
@@ -94,7 +92,7 @@ def tile_list_kg_mul_none_kernel(
         raw00 = [load_wa(0, 0, lo, lo + PASS // 2, placed(raw0, RAW00 + 8 * PASS - 16 * lo)) for lo in (0, PASS // 2)]
         tab_win = placed(early, 0)([P, T], I32, "tab_win")
         nc.sync.dma_start(tab_win[:], as_words(tab_words[0]))
-        raw01 = load_wa(0, 1, 0, PASS, held)
+        raw01 = [load_wa(0, 1, lo, lo + PASS // 2, held) for lo in (0, PASS // 2)]
         wb_scale_rows = wb_scales[0].rearrange("(q e) r -> e q r", e=4)
         for e in range(4):
             nc.sync.dma_start(wb_scale_raw[e:P:32, :].bitcast(I32), wb_scale_rows[e].bitcast(I32))
@@ -119,11 +117,6 @@ def tile_list_kg_mul_none_kernel(
             src = raw[:].rearrange("p i (m t) -> p m i t", t=PACK)
             dst = grouped[:].rearrange("p (t m i) -> p m i t", t=PACK, i=PACK)
             nc.scalar.copy(dst[:, lo:hi], src)
-
-        def round_wa_pool(raw, grouped, lo, hi):
-            src = raw[:].rearrange("p i (m t) -> p t m i", t=PACK)
-            dst = grouped[:].rearrange("p (t m i) -> p t m i", t=PACK, i=PACK)
-            nc.gpsimd.tensor_copy(dst[:, :, lo:hi], src)
 
         wa_codes, wa_scale = {}, {}
 
@@ -162,16 +155,17 @@ def tile_list_kg_mul_none_kernel(
         part_tab(0, 256, pairs0, held)
         part_tab(256, 512, pairs1, held)
         pairs2 = gather_tab(512, 1024, placed(raw0, RAW00 + 64 - 4 * HALF))
-        raw10 = [load_wa(1, 0, lo, lo + PASS // 2, placed(raw0, RAW10 + 16 * lo)) for lo in (0, PASS // 2)]
+        raw10 = load_wa(1, 0, 0, PASS, placed(raw0, RAW10))
         wb_scale = placed(raw0, RAW00 + 64)([P, R], U8, "wb_scale")
         nc.vector.tensor_copy(
             wb_scale[:].rearrange("p (b t c m) -> p b c t m", b=2, t=PACK, m=16),
             wb_scale_raw[:].rearrange("p (b c m t) -> p b c t m", b=2, t=PACK, m=16),
         )
-        part_tab(512, 1024, pairs2, held)
         grouped01 = held([P, PASS * PACK], BF16, "wa_grouped01")
-        round_wa(raw01, grouped01, 0, P)
+        for n in range(2):
+            round_wa(raw01[n], grouped01, n * P // 2, (n + 1) * P // 2)
         quantise_wa(0, 1, [grouped01], placed(early, 0))
+        part_tab(512, 1024, pairs2, held)
         wb_codes = placed(early, 4 * PASS)([P, R], I32, "wb_codes")
         nc.vector.tensor_copy(
             wb_codes[:].rearrange("p (b t c m) -> p b c t m", b=2, t=PACK, m=4),
@@ -207,8 +201,8 @@ def tile_list_kg_mul_none_kernel(
             return kept
 
         ha0 = []
-        for c in range(HA0_AHEAD):
-            make = {0: placed(raw0, 0), 4: placed(early, 5 * T)}.get(c, held)
+        for c in range(CHUNKS):
+            make = placed(early, 5 * T) if c == 4 else held
             ha0.append(copy_out(project_a(0, c, c), make, "ha0_%d" % c))
 
         tab2_codes = []
@@ -252,16 +246,18 @@ def tile_list_kg_mul_none_kernel(
             nc.vector.tensor_tensor(h_chunk[b, c], by_query(bank), kept[:], MULT)
 
         def join0(c):
-            join(0, c, project_b(0, c, (c + HA0_AHEAD) % BANKS), ha0[c])
-            later = c + HA0_AHEAD
-            if later < CHUNKS:
-                ha0.append(copy_out(project_a(0, later, later), placed(raw0, RAW10 + 8 * PASS + 64 + c * CHUNK_BYTES), "ha0_%d" % later))
+            join(0, c, project_b(0, c, c), ha0[c])
 
         h_scale = [held([P, J], U8, "h_scale%d" % b) for b in range(2)]
         h_codes = {}
 
+        def new_codes(b, lo, hi, make):
+            codes = make([P, hi - lo], U32, "h_codes%d_%d" % (b, lo))
+            for j0 in range(lo, hi, JC):
+                h_codes[b, j0] = (codes, lo)
+
         def quantise_h(b, lo, hi):
-            codes, at = h_codes[b, lo // HALF]
+            codes, at = h_codes[b, lo]
             nc.vector.quantize_mx(
                 out=codes[:, lo - at : hi - at].bitcast(FP8X4),
                 scales=h_scale[b][:, lo:hi],
@@ -270,33 +266,28 @@ def tile_list_kg_mul_none_kernel(
 
         new_h(0, 0, 512, held)
         new_h(0, 512, 768, held)
-        grouped10 = placed(raw0, 128)([P, PASS * PACK], BF16, "wa_grouped10")
-        round_wa_pool(raw10[0], grouped10, 0, P // 2)
-        round_wa(raw10[1], grouped10, P // 2, P)
+        grouped10 = placed(second, 8 * R + 2 * N + 8 * N)([P, PASS * PACK], BF16, "wa_grouped10")
+        round_wa(raw10, grouped10, 0, P)
         for c in range(6):
             join0(c)
-        quantise_wa(1, 0, [grouped10], held)
-        new_h(0, 768, 1024, placed(raw0, RAW10 + 64))
+        quantise_wa(1, 0, [grouped10], placed(early, 5 * T))
+        new_h(0, 768, 1024, placed(raw0, RAW10))
         for c in range(6, CHUNKS):
             join0(c)
-        h_codes[0, 0] = (placed(raw0, RAW10 + 64 + 4 * PASS)([P, HALF], U32, "h_codes0_0"), 0)
-        quantise_h(0, 0, 512)
-        grouped11 = placed(early, 5 * T)([P, PASS * PACK], BF16, "wa_grouped11")
+        grouped11 = placed(raw0, RAW10 + 2 * CHUNK_BYTES)([P, PASS * PACK], BF16, "wa_grouped11")
         round_wa(raw11, grouped11, 0, P)
-        quantise_wa(1, 1, [grouped11], placed(raw0, RAW10 + 8 * PASS + 64))
-        h_codes[0, 1] = (placed(raw0, H01)([P, HALF], U32, "h_codes0_1"), HALF)
-        quantise_h(0, 512, 768)
-        quantise_h(0, 768, 1024)
+        quantise_wa(1, 1, [grouped11], held)
+        new_codes(0, 0, J, placed(raw0, RAW11))
+        for lo, hi in H0_RANGES:
+            quantise_h(0, lo, hi)
+        new_codes(1, 0, J, held)
 
-        h_codes1 = held([P, J], U32, "h_codes1")
-        h_codes[1, 0] = (h_codes1, 0)
-        h_codes[1, 1] = (h_codes1, 0)
         out_rows = out.rearrange("(u p) j -> p u j", p=P)
 
         def score(dst, u, lo, hi):
             cols = slice(u * P, (u + 1) * P)
             for b in range(2):
-                codes, at = h_codes[b, lo // HALF]
+                codes, at = h_codes[b, lo]
                 nc.tensor.matmul_mx(
                     out=dst,
                     lhsT=en_codes[:, b, cols].bitcast(FP8X4),
@@ -323,7 +314,7 @@ def tile_list_kg_mul_none_kernel(
         hb1 = []
 
         def make_hb1(c):
-            make = placed(early, 5 * T + 64 + (c - 1) * CHUNK_BYTES) if c < len(HB1_BANKS) else held
+            make = placed(raw0, RAW10 + 64 + (c + 1) * CHUNK_BYTES) if c < len(HB1_BANKS) else held
             hb1.append(copy_out(project_b(1, c, HB1_BANKS[c % len(HB1_BANKS)]), make, "hb1_%d" % c))
 
         ha1 = []

@@ -30,7 +30,7 @@ H0_RANGES = ((0, 512), (512, 768), (768, 1024))
 HB1_BANKS = (3, 4, 5)
 HA1_BANKS = (0, 1, 2, 6, 7)
 SCORE_BANKS = ((6,), (7,), (5,), (3,), (4,))
-BANKS = 8
+SHARE = 32
 RAW00 = 6144
 RAW10 = RAW00 + 64 + 2 * J
 PAIRS = 8 * T
@@ -64,10 +64,11 @@ def tile_list_kg_mul_none_kernel(
         list2 = lists.tile([P, J // LIST_GROUP], U16, name="list2")
         list1 = lists.tile([P, J // LIST_GROUP], U16, name="list1")
 
-        wb_at = 0
-        tab2_scale_at = 4 * R
+        win_at = 4 * R
+        wb_at = win_at + 64 - 4 * PASS
+        tab2_scale_at = win_at + 128
         tab2_at = tab2_scale_at + J
-        tab_scale_win = placed(second, tab2_scale_at - T // 4)([P, T], U8, "tab_scale_win")
+        tab_scale_win = placed(second, win_at)([P, T], U8, "tab_scale_win")
         tab2_scale_win = held([P, T], U8, "tab2_scale_win")
         wb_scale_raw = placed(raw0, RAW11 + 64)([P, R], U8, "wb_scale_raw")
         tab_scale1 = held([P, J], U8, "tab_scale1")
@@ -89,7 +90,7 @@ def tile_list_kg_mul_none_kernel(
         tab_scale_rows = tab_scales.rearrange("a (q e) t -> e q a t", e=4)
         for e in range(4):
             nc.sync.dma_start(tab_scale_win[e:P:16, :].bitcast(I32), tab_scale_rows[e].bitcast(I32))
-        raw00 = [load_wa(0, 0, lo, lo + PASS // 2, placed(raw0, RAW00 + 8 * PASS - 16 * lo)) for lo in (0, PASS // 2)]
+        raw00 = [load_wa(0, 0, 0, PASS // 2, placed(early, 8 * T)), load_wa(0, 0, PASS // 2, PASS, placed(raw0, RAW00))]
         tab_win = placed(early, 0)([P, T], I32, "tab_win")
         nc.sync.dma_start(tab_win[:], as_words(tab_words[0]))
         raw01 = [load_wa(0, 1, lo, lo + PASS // 2, held) for lo in (0, PASS // 2)]
@@ -104,9 +105,9 @@ def tile_list_kg_mul_none_kernel(
         nc.sync.dma_start(tab_scale1[0:112, :].bitcast(I32), tab_scale0[16:128, :].bitcast(I32))
         tab_scale = (tab_scale0, tab_scale1)
 
-        wb_raw = placed(second, wb_at)([P, R], I32, "wb_raw")
+        wb_raw = [placed(second, wb_at)([P, PASS], I32, "wb_raw0")]
         tab2_win = placed(second, tab2_at)([P, T], I32, "tab2_win")
-        nc.sync.dma_start(wb_raw[:], as_words(wb_words[0]))
+        nc.sync.dma_start(wb_raw[0][:], as_words(wb_words[0])[:, 0:PASS])
         nc.sync.dma_start(tab2_win[:], as_words(tab2_words[0]))
         tab2_scale = placed(second, tab2_scale_at)([P, J], U8, "tab2_scale")
         nc.gpsimd.memset(tab2_scale[:].bitcast(I32), 0)
@@ -114,7 +115,7 @@ def tile_list_kg_mul_none_kernel(
             nc.sync.dma_start(tab2_scale[e:P:32, :].bitcast(I32), tab2_scale_picked[112 + e : P : 4, :].bitcast(I32))
 
         def round_wa(raw, grouped, lo, hi):
-            src = raw[:].rearrange("p i (m t) -> p m i t", t=PACK)
+            src = raw.rearrange("p i (m t) -> p m i t", t=PACK)
             dst = grouped[:].rearrange("p (t m i) -> p m i t", t=PACK, i=PACK)
             nc.scalar.copy(dst[:, lo:hi], src)
 
@@ -148,29 +149,38 @@ def tile_list_kg_mul_none_kernel(
 
         grouped00 = held([P, PASS * PACK], BF16, "wa_grouped00")
         for n in range(2):
-            round_wa(raw00[n], grouped00, n * P // 2, (n + 1) * P // 2)
+            round_wa(raw00[n][:], grouped00, n * P // 2, (n + 1) * P // 2)
         quantise_wa(0, 0, [grouped00], held)
         pairs0 = gather_tab(0, 256, placed(raw0, RAW00))
         pairs1 = gather_tab(256, 512, placed(raw0, RAW00 + 64 + R))
         part_tab(0, 256, pairs0, held)
         part_tab(256, 512, pairs1, held)
-        pairs2 = gather_tab(512, 1024, placed(raw0, RAW00 + 64 - 4 * HALF))
+        wb_raw.append(placed(early, 8 * T)([P, PASS], I32, "wb_raw1"))
+        nc.sync.dma_start(wb_raw[1][:], as_words(wb_words[0])[:, PASS:R])
+        pairs2 = gather_tab(512, 768, placed(raw0, RAW00 + 64 - J))
+        pairs3 = gather_tab(768, 1024, placed(raw0, RAW00 + 64))
         raw10 = load_wa(1, 0, 0, PASS, placed(raw0, RAW10))
-        wb_scale = placed(raw0, RAW00 + 64)([P, R], U8, "wb_scale")
+        part_tab(512, 768, pairs2, held)
+        grouped01 = held([P, PASS * PACK], BF16, "wa_grouped01")
+        for n in range(2):
+            round_wa(raw01[n][:], grouped01, n * P // 2, (n + 1) * P // 2)
+        part_tab(768, 1024, pairs3, held)
+        quantise_wa(0, 1, [grouped01], placed(early, 0))
+        wb_scale = placed(early, 4 * PASS)([P, R], U8, "wb_scale")
         nc.vector.tensor_copy(
             wb_scale[:].rearrange("p (b t c m) -> p b c t m", b=2, t=PACK, m=16),
             wb_scale_raw[:].rearrange("p (b c m t) -> p b c t m", b=2, t=PACK, m=16),
         )
-        grouped01 = held([P, PASS * PACK], BF16, "wa_grouped01")
-        for n in range(2):
-            round_wa(raw01[n], grouped01, n * P // 2, (n + 1) * P // 2)
-        quantise_wa(0, 1, [grouped01], placed(early, 0))
-        part_tab(512, 1024, pairs2, held)
-        wb_codes = placed(early, 4 * PASS)([P, R], I32, "wb_codes")
-        nc.vector.tensor_copy(
-            wb_codes[:].rearrange("p (b t c m) -> p b c t m", b=2, t=PACK, m=4),
-            wb_raw[:].rearrange("p (b c m t) -> p b c t m", b=2, t=PACK, m=4),
-        )
+        wb_codes = {}
+
+        def reorder_wb(engine, b, make):
+            wb_codes[b] = make([P, PASS], I32, "wb_codes%d" % b)
+            engine.tensor_copy(
+                wb_codes[b][:].rearrange("p (t c m) -> p c t m", t=PACK, m=4),
+                wb_raw[b][:].rearrange("p (c m t) -> p c t m", t=PACK, m=4),
+            )
+
+        reorder_wb(nc.vector, 0, placed(early, 8 * PASS))
         raw11 = load_wa(1, 1, 0, PASS, placed(raw0, RAW11))
 
         def bank_tile(n, shape):
@@ -202,15 +212,16 @@ def tile_list_kg_mul_none_kernel(
 
         ha0 = []
         for c in range(CHUNKS):
-            make = placed(early, 5 * T) if c == 4 else held
+            make = {1: placed(early, 16 * T), 4: placed(early, 5 * T)}.get(c, held)
             ha0.append(copy_out(project_a(0, c, c), make, "ha0_%d" % c))
 
         tab2_codes = []
         for h in range(2):
-            codes = placed(second, wb_at + 4 * HALF * h)([P, HALF], U32, "tab2_codes%d" % h)
+            codes = placed(second, wb_at + 64 + 4 * HALF * (h - 1))([P, HALF], U32, "tab2_codes%d" % h)
             nc.vector.tensor_copy(codes[:], tab2_win[:].bitcast(U32).indirect(part_of(list2, h * HALF, (h + 1) * HALF)))
             tab2_codes.append(codes)
 
+        reorder_wb(nc.gpsimd, 1, placed(second, tab2_at))
         en_codes = placed(second, 8 * R + 2 * N)([P, 2, N], I32, "en_codes")
         nc.sync.dma_start(en_codes[:], en_words.rearrange("a p n i -> p a (n i)").bitcast(I32))
         en_scale = placed(second, 8 * R)([P, 2, N], U8, "en_scale")
@@ -226,7 +237,7 @@ def tile_list_kg_mul_none_kernel(
                 cols = slice(b * PASS + t * P, b * PASS + (t + 1) * P)
                 nc.tensor.matmul_mx(
                     out=bank[:, t, :],
-                    lhsT=wb_codes[:, cols].bitcast(FP8X4),
+                    lhsT=wb_codes[b][:, t * P : (t + 1) * P].bitcast(FP8X4),
                     lhsT_scale=wb_scale[:, cols],
                     rhs=tab2_codes[h][:, j0 : j0 + JC].bitcast(FP8X4),
                     rhs_scale=tab2_scale[:, c * JC : (c + 1) * JC],
@@ -266,19 +277,28 @@ def tile_list_kg_mul_none_kernel(
 
         new_h(0, 0, 512, held)
         new_h(0, 512, 768, held)
-        grouped10 = placed(second, 8 * R + 2 * N + 8 * N)([P, PASS * PACK], BF16, "wa_grouped10")
-        round_wa(raw10, grouped10, 0, P)
-        for c in range(6):
+        for c in range(2):
             join0(c)
-        quantise_wa(1, 0, [grouped10], placed(early, 5 * T))
+        grouped10 = placed(early, 16 * T)([P, PASS * PACK], BF16, "wa_grouped10")
+        round_wa(raw10[:, :, PACK * SHARE : PASS], grouped10, SHARE, P)
+        for c in range(2, 5):
+            join0(c)
+        nc.vector.tensor_copy(
+            grouped10[:].rearrange("p (t m i) -> p m t i", t=PACK, i=PACK)[:, 0:SHARE],
+            raw10[:].rearrange("p i (m t) -> p m t i", t=PACK)[:, 0:SHARE],
+        )
+        join0(5)
+        quantise_wa(1, 0, [grouped10], held)
         new_h(0, 768, 1024, placed(raw0, RAW10))
         for c in range(6, CHUNKS):
             join0(c)
-        grouped11 = placed(raw0, RAW10 + 2 * CHUNK_BYTES)([P, PASS * PACK], BF16, "wa_grouped11")
-        round_wa(raw11, grouped11, 0, P)
+        new_codes(0, 0, HALF, placed(raw0, RAW10 + CHUNK_BYTES))
+        quantise_h(0, 0, HALF)
+        grouped11 = placed(early, 5 * T)([P, PASS * PACK], BF16, "wa_grouped11")
+        round_wa(raw11[:], grouped11, 0, P)
         quantise_wa(1, 1, [grouped11], held)
-        new_codes(0, 0, J, placed(raw0, RAW11))
-        for lo, hi in H0_RANGES:
+        new_codes(0, HALF, J, placed(raw0, RAW11))
+        for lo, hi in H0_RANGES[1:]:
             quantise_h(0, lo, hi)
         new_codes(1, 0, J, held)
 
@@ -314,7 +334,7 @@ def tile_list_kg_mul_none_kernel(
         hb1 = []
 
         def make_hb1(c):
-            make = placed(raw0, RAW10 + 64 + (c + 1) * CHUNK_BYTES) if c < len(HB1_BANKS) else held
+            make = placed(early, 5 * T + 64 + (c - 1) * CHUNK_BYTES) if c < len(HB1_BANKS) else held
             hb1.append(copy_out(project_b(1, c, HB1_BANKS[c % len(HB1_BANKS)]), make, "hb1_%d" % c))
 
         ha1 = []

@@ -27,15 +27,20 @@ CHUNK_BYTES = JC * PACK * 4
 TAB_STEP = 256
 SCORE_RANGES = ((0, 256), (256, 512), (512, 768), (768, 896), (896, 1024))
 H0_RANGES = ((0, 512), (512, 768), (768, 1024))
-HB1_BANKS = (3, 4, 5)
-HA1_BANKS = (0, 1, 2, 6, 7)
-SCORE_BANKS = ((6,), (7,), (5,), (3,), (4,))
-SHARE = 32
+BANKS = 8
+HB1_BANKS = (0, 1, 2)
+HA1_BANKS = (3, 6, 7, 4, 5)
+SCORE_BANKS = ((4,), (5,), (2,), (0,), (1,))
+SHARE10 = 32
+SHARE11 = 64
 RAW00 = 6144
 RAW10 = RAW00 + 64 + 2 * J
 PAIRS = 8 * T
-RAW11 = RAW10 + 20 * PASS
+RAW11 = RAW10 + 20 * PASS + 128
+FIRST = 80
 HA1_LEAD = 2
+HB1_LEAD = 4
+AFTER10 = 6
 HA0_AHEAD = 6
 
 
@@ -90,10 +95,11 @@ def tile_list_kg_mul_none_kernel(
         tab_scale_rows = tab_scales.rearrange("a (q e) t -> e q a t", e=4)
         for e in range(4):
             nc.sync.dma_start(tab_scale_win[e:P:16, :].bitcast(I32), tab_scale_rows[e].bitcast(I32))
-        raw00 = [load_wa(0, 0, 0, PASS // 2, placed(early, 8 * T)), load_wa(0, 0, PASS // 2, PASS, placed(raw0, RAW00))]
+        raw00 = [load_wa(0, 0, 0, PACK * FIRST, placed(early, 8 * T))]
         tab_win = placed(early, 0)([P, T], I32, "tab_win")
         nc.sync.dma_start(tab_win[:], as_words(tab_words[0]))
-        raw01 = [load_wa(0, 1, lo, lo + PASS // 2, held) for lo in (0, PASS // 2)]
+        raw00.append(load_wa(0, 0, PACK * FIRST, PASS, placed(raw0, RAW00)))
+        raw01 = [load_wa(0, 1, 0, PASS // 2, held), load_wa(0, 1, PASS // 2, PASS, placed(early, 12 * T))]
         wb_scale_rows = wb_scales[0].rearrange("(q e) r -> e q r", e=4)
         for e in range(4):
             nc.sync.dma_start(wb_scale_raw[e:P:32, :].bitcast(I32), wb_scale_rows[e].bitcast(I32))
@@ -147,30 +153,23 @@ def tile_list_kg_mul_none_kernel(
             for j0 in range(lo, hi, JC):
                 tab_codes[j0 // JC] = parted[:, :, 2 * (j0 - lo) : 2 * (j0 - lo + JC)]
 
-        grouped00 = held([P, PASS * PACK], BF16, "wa_grouped00")
+        pairs = [gather_tab(lo, lo + TAB_STEP, held) for lo in (0, TAB_STEP)]
         for n in range(2):
-            round_wa(raw00[n][:], grouped00, n * P // 2, (n + 1) * P // 2)
+            part_tab(n * TAB_STEP, (n + 1) * TAB_STEP, pairs[n], held)
+        grouped00 = held([P, PASS * PACK], BF16, "wa_grouped00")
+        round_wa(raw00[0][:], grouped00, 0, FIRST)
+        round_wa(raw00[1][:], grouped00, FIRST, P)
         quantise_wa(0, 0, [grouped00], held)
-        pairs0 = gather_tab(0, 256, placed(raw0, RAW00))
-        pairs1 = gather_tab(256, 512, placed(raw0, RAW00 + 64 + R))
-        part_tab(0, 256, pairs0, held)
-        part_tab(256, 512, pairs1, held)
         wb_raw.append(placed(early, 8 * T)([P, PASS], I32, "wb_raw1"))
         nc.sync.dma_start(wb_raw[1][:], as_words(wb_words[0])[:, PASS:R])
-        pairs2 = gather_tab(512, 768, placed(raw0, RAW00 + 64 - J))
-        pairs3 = gather_tab(768, 1024, placed(raw0, RAW00 + 64))
+        pairs2 = gather_tab(512, 768, placed(raw0, RAW00))
+        pairs3 = gather_tab(768, 1024, placed(raw0, RAW00 + J))
         raw10 = load_wa(1, 0, 0, PASS, placed(raw0, RAW10))
         part_tab(512, 768, pairs2, held)
         grouped01 = held([P, PASS * PACK], BF16, "wa_grouped01")
         for n in range(2):
             round_wa(raw01[n][:], grouped01, n * P // 2, (n + 1) * P // 2)
         part_tab(768, 1024, pairs3, held)
-        quantise_wa(0, 1, [grouped01], placed(early, 0))
-        wb_scale = placed(early, 4 * PASS)([P, R], U8, "wb_scale")
-        nc.vector.tensor_copy(
-            wb_scale[:].rearrange("p (b t c m) -> p b c t m", b=2, t=PACK, m=16),
-            wb_scale_raw[:].rearrange("p (b c m t) -> p b c t m", b=2, t=PACK, m=16),
-        )
         wb_codes = {}
 
         def reorder_wb(engine, b, make):
@@ -181,6 +180,12 @@ def tile_list_kg_mul_none_kernel(
             )
 
         reorder_wb(nc.vector, 0, placed(early, 8 * PASS))
+        quantise_wa(0, 1, [grouped01], placed(early, 0))
+        wb_scale = placed(early, 12 * T)([P, R], U8, "wb_scale")
+        nc.vector.tensor_copy(
+            wb_scale[:].rearrange("p (b t c m) -> p b c t m", b=2, t=PACK, m=16),
+            wb_scale_raw[:].rearrange("p (b c m t) -> p b c t m", b=2, t=PACK, m=16),
+        )
         raw11 = load_wa(1, 1, 0, PASS, placed(raw0, RAW11))
 
         def bank_tile(n, shape):
@@ -211,8 +216,8 @@ def tile_list_kg_mul_none_kernel(
             return kept
 
         ha0 = []
-        for c in range(CHUNKS):
-            make = {1: placed(early, 16 * T), 4: placed(early, 5 * T)}.get(c, held)
+        for c in range(HA0_AHEAD):
+            make = {0: placed(early, 16 * T), AFTER10 - 2: placed(early, 5 * T)}.get(c, held)
             ha0.append(copy_out(project_a(0, c, c), make, "ha0_%d" % c))
 
         tab2_codes = []
@@ -257,7 +262,10 @@ def tile_list_kg_mul_none_kernel(
             nc.vector.tensor_tensor(h_chunk[b, c], by_query(bank), kept[:], MULT)
 
         def join0(c):
-            join(0, c, project_b(0, c, c), ha0[c])
+            join(0, c, project_b(0, c, (c + HA0_AHEAD) % BANKS), ha0[c])
+
+        def late_ha0(c):
+            ha0.append(copy_out(project_a(0, c, c), placed(raw0, RAW10 + (c - HA0_AHEAD + 1) * CHUNK_BYTES), "ha0_%d" % c))
 
         h_scale = [held([P, J], U8, "h_scale%d" % b) for b in range(2)]
         h_codes = {}
@@ -277,28 +285,31 @@ def tile_list_kg_mul_none_kernel(
 
         new_h(0, 0, 512, held)
         new_h(0, 512, 768, held)
+        def round_share(engine, walk, raw, grouped, lo, hi):
+            src = raw[:, :, PACK * lo : PACK * hi].rearrange("p i (m t) -> p " + walk, t=PACK)
+            dst = grouped[:].rearrange("p (t m i) -> p t m i", t=PACK, i=PACK)[:, :, lo:hi]
+            engine.tensor_copy(dst.rearrange("p t m i -> p " + walk), src)
+
         for c in range(2):
             join0(c)
         grouped10 = placed(early, 16 * T)([P, PASS * PACK], BF16, "wa_grouped10")
-        round_wa(raw10[:, :, PACK * SHARE : PASS], grouped10, SHARE, P)
-        for c in range(2, 5):
+        round_wa(raw10[:, :, PACK * SHARE10 : PASS], grouped10, SHARE10, P)
+        for c in range(2, AFTER10 - 1):
             join0(c)
-        nc.vector.tensor_copy(
-            grouped10[:].rearrange("p (t m i) -> p m t i", t=PACK, i=PACK)[:, 0:SHARE],
-            raw10[:].rearrange("p i (m t) -> p m t i", t=PACK)[:, 0:SHARE],
-        )
-        join0(5)
-        quantise_wa(1, 0, [grouped10], held)
+        round_share(nc.vector, "m t i", raw10, grouped10, 0, SHARE10)
+        for c in range(HA0_AHEAD, CHUNKS):
+            late_ha0(c)
+        join0(AFTER10 - 1)
+        quantise_wa(1, 0, [grouped10], placed(early, 5 * T))
+        grouped11 = placed(raw0, RAW10 + 3 * CHUNK_BYTES)([P, PASS * PACK], BF16, "wa_grouped11")
+        round_share(nc.vector, "m t i", raw11, grouped11, 0, SHARE11)
+        round_wa(raw11[:, :, PACK * SHARE11 : PASS], grouped11, SHARE11, P)
         new_h(0, 768, 1024, placed(raw0, RAW10))
-        for c in range(6, CHUNKS):
+        for c in range(AFTER10, CHUNKS):
             join0(c)
-        new_codes(0, 0, HALF, placed(raw0, RAW10 + CHUNK_BYTES))
-        quantise_h(0, 0, HALF)
-        grouped11 = placed(early, 5 * T)([P, PASS * PACK], BF16, "wa_grouped11")
-        round_wa(raw11[:], grouped11, 0, P)
         quantise_wa(1, 1, [grouped11], held)
-        new_codes(0, HALF, J, placed(raw0, RAW11))
-        for lo, hi in H0_RANGES[1:]:
+        new_codes(0, 0, J, placed(raw0, RAW11))
+        for lo, hi in H0_RANGES:
             quantise_h(0, lo, hi)
         new_codes(1, 0, J, held)
 
@@ -334,7 +345,7 @@ def tile_list_kg_mul_none_kernel(
         hb1 = []
 
         def make_hb1(c):
-            make = placed(early, 5 * T + 64 + (c - 1) * CHUNK_BYTES) if c < len(HB1_BANKS) else held
+            make = placed(raw0, RAW10 + 64 + (c + 2) * CHUNK_BYTES) if c < len(HB1_BANKS) else held
             hb1.append(copy_out(project_b(1, c, HB1_BANKS[c % len(HB1_BANKS)]), make, "hb1_%d" % c))
 
         ha1 = []
@@ -346,11 +357,13 @@ def tile_list_kg_mul_none_kernel(
             make_hb1(c)
         for c in range(HA1_LEAD):
             make_ha1(c)
+        for c in range(len(HB1_BANKS), HB1_LEAD):
+            make_hb1(c)
         for c in range(CHUNKS + 2):
             if c + HA1_LEAD < CHUNKS:
                 make_ha1(c + HA1_LEAD)
-            if c + len(HB1_BANKS) < CHUNKS:
-                make_hb1(c + len(HB1_BANKS))
+            if c + HB1_LEAD < CHUNKS:
+                make_hb1(c + HB1_LEAD)
             if c - 1 in ends:
                 n, lo, hi = ends[c - 1]
                 finish(lo, hi, SCORE_BANKS[n])

@@ -285,10 +285,10 @@ def tile_list_kg_mul_none_kernel(
 
         new_h(0, 0, 512, held)
         new_h(0, 512, 768, held)
-        def round_share(engine, walk, raw, grouped, lo, hi):
-            src = raw[:, :, PACK * lo : PACK * hi].rearrange("p i (m t) -> p " + walk, t=PACK)
-            dst = grouped[:].rearrange("p (t m i) -> p t m i", t=PACK, i=PACK)[:, :, lo:hi]
-            engine.tensor_copy(dst.rearrange("p t m i -> p " + walk), src)
+        def round_share(raw, grouped, share):
+            src = raw[:, :, 0 : PACK * share].rearrange("p i (m h l) -> p h m i l", h=2, l=2)
+            dst = grouped[:].rearrange("p (h l m i) -> p h m i l", h=2, l=2, i=PACK)
+            nc.vector.tensor_copy(dst[:, :, 0:share], src)
 
         for c in range(2):
             join0(c)
@@ -296,13 +296,13 @@ def tile_list_kg_mul_none_kernel(
         round_wa(raw10[:, :, PACK * SHARE10 : PASS], grouped10, SHARE10, P)
         for c in range(2, AFTER10 - 1):
             join0(c)
-        round_share(nc.vector, "m t i", raw10, grouped10, 0, SHARE10)
+        round_share(raw10, grouped10, SHARE10)
         for c in range(HA0_AHEAD, CHUNKS):
             late_ha0(c)
         join0(AFTER10 - 1)
         quantise_wa(1, 0, [grouped10], placed(early, 5 * T))
         grouped11 = placed(raw0, RAW10 + 3 * CHUNK_BYTES)([P, PASS * PACK], BF16, "wa_grouped11")
-        round_share(nc.vector, "m t i", raw11, grouped11, 0, SHARE11)
+        round_share(raw11, grouped11, SHARE11)
         round_wa(raw11[:, :, PACK * SHARE11 : PASS], grouped11, SHARE11, P)
         new_h(0, 768, 1024, placed(raw0, RAW10))
         for c in range(AFTER10, CHUNKS):

@@ -31,7 +31,6 @@ BANKS = 8
 HB1_BANKS = (0, 1, 2)
 HA1_BANKS = (3, 6, 7, 4, 5)
 SCORE_BANKS = ((4,), (5,), (2,), (0,), (1,))
-SHARE10 = 32
 SHARE11 = 64
 RAW00 = 6144
 RAW10 = RAW00 + 64 + 2 * J
@@ -75,7 +74,7 @@ def tile_list_kg_mul_none_kernel(
         tab2_at = tab2_scale_at + J
         tab_scale_win = placed(second, win_at)([P, T], U8, "tab_scale_win")
         tab2_scale_win = held([P, T], U8, "tab2_scale_win")
-        wb_scale_raw = placed(raw0, RAW11 + 64)([P, R], U8, "wb_scale_raw")
+        wb_scale_raw = held([P, R], U8, "wb_scale_raw")
         tab_scale1 = held([P, J], U8, "tab_scale1")
         nc.gpsimd.memset(tab_scale_win[:].bitcast(I32), 0)
         nc.vector.memset(tab2_scale_win[0:96, :].bitcast(I32), 0)
@@ -99,7 +98,7 @@ def tile_list_kg_mul_none_kernel(
         tab_win = placed(early, 0)([P, T], I32, "tab_win")
         nc.sync.dma_start(tab_win[:], as_words(tab_words[0]))
         raw00.append(load_wa(0, 0, PACK * FIRST, PASS, placed(raw0, RAW00)))
-        raw01 = [load_wa(0, 1, 0, PASS // 2, held), load_wa(0, 1, PASS // 2, PASS, placed(early, 12 * T))]
+        raw01 = [load_wa(0, 1, 0, PASS // 2, placed(raw0, RAW11)), load_wa(0, 1, PASS // 2, PASS, placed(early, 12 * T))]
         wb_scale_rows = wb_scales[0].rearrange("(q e) r -> e q r", e=4)
         for e in range(4):
             nc.sync.dma_start(wb_scale_raw[e:P:32, :].bitcast(I32), wb_scale_rows[e].bitcast(I32))
@@ -181,11 +180,16 @@ def tile_list_kg_mul_none_kernel(
 
         reorder_wb(nc.vector, 0, placed(early, 8 * PASS))
         quantise_wa(0, 1, [grouped01], placed(early, 0))
-        wb_scale = placed(early, 12 * T)([P, R], U8, "wb_scale")
-        nc.vector.tensor_copy(
-            wb_scale[:].rearrange("p (b t c m) -> p b c t m", b=2, t=PACK, m=16),
-            wb_scale_raw[:].rearrange("p (b c m t) -> p b c t m", b=2, t=PACK, m=16),
-        )
+        wb_scale = {}
+
+        def reorder_wb_scale(engine, b, make):
+            wb_scale[b] = make([P, PASS], U8, "wb_scale%d" % b)
+            engine.tensor_copy(
+                wb_scale[b][:].rearrange("p (t c m) -> p c t m", t=PACK, m=16),
+                wb_scale_raw[:, b * PASS : (b + 1) * PASS].rearrange("p (c m t) -> p c t m", t=PACK, m=16),
+            )
+
+        reorder_wb_scale(nc.vector, 0, placed(early, 12 * T))
         raw11 = load_wa(1, 1, 0, PASS, placed(raw0, RAW11))
 
         def bank_tile(n, shape):
@@ -217,7 +221,7 @@ def tile_list_kg_mul_none_kernel(
 
         ha0 = []
         for c in range(HA0_AHEAD):
-            make = {0: placed(early, 16 * T), AFTER10 - 2: placed(early, 5 * T)}.get(c, held)
+            make = placed(early, 5 * T) if c == AFTER10 - 2 else held
             ha0.append(copy_out(project_a(0, c, c), make, "ha0_%d" % c))
 
         tab2_codes = []
@@ -227,6 +231,7 @@ def tile_list_kg_mul_none_kernel(
             tab2_codes.append(codes)
 
         reorder_wb(nc.gpsimd, 1, placed(second, tab2_at))
+        reorder_wb_scale(nc.gpsimd, 1, placed(second, tab2_at + 4 * PASS))
         en_codes = placed(second, 8 * R + 2 * N)([P, 2, N], I32, "en_codes")
         nc.sync.dma_start(en_codes[:], en_words.rearrange("a p n i -> p a (n i)").bitcast(I32))
         en_scale = placed(second, 8 * R)([P, 2, N], U8, "en_scale")
@@ -243,7 +248,7 @@ def tile_list_kg_mul_none_kernel(
                 nc.tensor.matmul_mx(
                     out=bank[:, t, :],
                     lhsT=wb_codes[b][:, t * P : (t + 1) * P].bitcast(FP8X4),
-                    lhsT_scale=wb_scale[:, cols],
+                    lhsT_scale=wb_scale[b][:, t * P : (t + 1) * P],
                     rhs=tab2_codes[h][:, j0 : j0 + JC].bitcast(FP8X4),
                     rhs_scale=tab2_scale[:, c * JC : (c + 1) * JC],
                     start=True,
@@ -292,11 +297,10 @@ def tile_list_kg_mul_none_kernel(
 
         for c in range(2):
             join0(c)
-        grouped10 = placed(early, 16 * T)([P, PASS * PACK], BF16, "wa_grouped10")
-        round_wa(raw10[:, :, PACK * SHARE10 : PASS], grouped10, SHARE10, P)
+        grouped10 = placed(second, 8 * R + 2 * N + 8 * N)([P, PASS * PACK], BF16, "wa_grouped10")
+        round_wa(raw10[:], grouped10, 0, P)
         for c in range(2, AFTER10 - 1):
             join0(c)
-        round_share(raw10, grouped10, SHARE10)
         for c in range(HA0_AHEAD, CHUNKS):
             late_ha0(c)
         join0(AFTER10 - 1)

@@ -36,7 +36,7 @@ RAW00 = 6144
 RAW10 = RAW00 + 64 + 2 * J
 PAIRS = 8 * T
 RAW11 = RAW10 + 20 * PASS + 128
-FIRST = 80
+FIRST = 64
 HA1_LEAD = 2
 HB1_LEAD = 4
 AFTER10 = 6
@@ -90,14 +90,14 @@ def tile_list_kg_mul_none_kernel(
 
         nc.sync.dma_start(list2[:], offs2)
         nc.sync.dma_start(tab2_scale_win[112:128, :].bitcast(I32), tab2_scales[0].bitcast(I32))
+        raw00 = [load_wa(0, 0, 0, PACK * FIRST, placed(early, 8 * T))]
         nc.sync.dma_start(list1[:], offs)
         tab_scale_rows = tab_scales.rearrange("a (q e) t -> e q a t", e=4)
         for e in range(4):
             nc.sync.dma_start(tab_scale_win[e:P:16, :].bitcast(I32), tab_scale_rows[e].bitcast(I32))
-        raw00 = [load_wa(0, 0, 0, PACK * FIRST, placed(early, 8 * T))]
+        raw00.append(load_wa(0, 0, PACK * FIRST, PASS, placed(raw0, RAW00)))
         tab_win = placed(early, 0)([P, T], I32, "tab_win")
         nc.sync.dma_start(tab_win[:], as_words(tab_words[0]))
-        raw00.append(load_wa(0, 0, PACK * FIRST, PASS, placed(raw0, RAW00)))
         raw01 = [load_wa(0, 1, 0, PASS // 2, placed(raw0, RAW11)), load_wa(0, 1, PASS // 2, PASS, placed(early, 12 * T))]
         wb_scale_rows = wb_scales[0].rearrange("(q e) r -> e q r", e=4)
         for e in range(4):
@@ -152,7 +152,7 @@ def tile_list_kg_mul_none_kernel(
             for j0 in range(lo, hi, JC):
                 tab_codes[j0 // JC] = parted[:, :, 2 * (j0 - lo) : 2 * (j0 - lo + JC)]
 
-        pairs = [gather_tab(lo, lo + TAB_STEP, held) for lo in (0, TAB_STEP)]
+        pairs = [gather_tab(lo, lo + TAB_STEP, placed(raw0, 4 * lo)) for lo in (0, TAB_STEP)]
         for n in range(2):
             part_tab(n * TAB_STEP, (n + 1) * TAB_STEP, pairs[n], held)
         grouped00 = held([P, PASS * PACK], BF16, "wa_grouped00")
@@ -161,8 +161,8 @@ def tile_list_kg_mul_none_kernel(
         quantise_wa(0, 0, [grouped00], held)
         wb_raw.append(placed(early, 8 * T)([P, PASS], I32, "wb_raw1"))
         nc.sync.dma_start(wb_raw[1][:], as_words(wb_words[0])[:, PASS:R])
-        pairs2 = gather_tab(512, 768, placed(raw0, RAW00))
-        pairs3 = gather_tab(768, 1024, placed(raw0, RAW00 + J))
+        pairs2 = gather_tab(512, 768, placed(raw0, 0))
+        pairs3 = gather_tab(768, 1024, placed(raw0, 4 * TAB_STEP))
         raw10 = load_wa(1, 0, 0, PASS, placed(raw0, RAW10))
         part_tab(512, 768, pairs2, held)
         grouped01 = held([P, PASS * PACK], BF16, "wa_grouped01")

@@ -28,9 +28,11 @@ TAB_STEP = 256
 SCORE_RANGES = ((0, 256), (256, 512), (512, 768), (768, 896), (896, 1024))
 H0_RANGES = ((0, 512), (512, 768), (768, 1024))
 BANKS = 8
-HB1_BANKS = (0, 1, 2)
-HA1_BANKS = (3, 6, 7, 4, 5)
-SCORE_BANKS = ((4,), (5,), (2,), (0,), (1,))
+HA0_BANKS = (0, 1, 2, 3, 0, 1, 6, 7)
+HB0_BANKS = (6, 7, 2, 3, 0, 1, 4, 5)
+HB1_BANKS = (2, 3, 0)
+HA1_BANKS = (1, 6, 7, 4, 5)
+SCORE_BANKS = (4, 5, 0, 2, 3)
 SHARE11 = 64
 RAW00 = 6144
 RAW10 = RAW00 + 64 + 2 * J
@@ -98,10 +100,14 @@ def tile_list_kg_mul_none_kernel(
         raw00.append(load_wa(0, 0, PACK * FIRST, PASS, placed(raw0, RAW00)))
         tab_win = placed(early, 0)([P, T], I32, "tab_win")
         nc.sync.dma_start(tab_win[:], as_words(tab_words[0]))
-        raw01 = [load_wa(0, 1, 0, PASS // 2, placed(raw0, RAW11)), load_wa(0, 1, PASS // 2, PASS, placed(early, 12 * T))]
         wb_scale_rows = wb_scales[0].rearrange("(q e) r -> e q r", e=4)
         for e in range(4):
             nc.sync.dma_start(wb_scale_raw[e:P:32, :].bitcast(I32), wb_scale_rows[e].bitcast(I32))
+        raw01 = [
+            load_wa(0, 1, 0, PACK * 32, placed(raw0, RAW11)),
+            load_wa(0, 1, PACK * 32, PACK * 80, held),
+            load_wa(0, 1, PACK * 80, PASS, placed(early, 12 * T)),
+        ]
 
         tab2_scale_picked = held([P, J], U8, "tab2_scale_picked")
         nc.vector.tensor_copy(tab2_scale_picked[:], tab2_scale_win[:].indirect(list2[:]))
@@ -159,26 +165,27 @@ def tile_list_kg_mul_none_kernel(
         round_wa(raw00[0][:], grouped00, 0, FIRST)
         round_wa(raw00[1][:], grouped00, FIRST, P)
         quantise_wa(0, 0, [grouped00], held)
-        wb_raw.append(placed(early, 8 * T)([P, PASS], I32, "wb_raw1"))
-        nc.sync.dma_start(wb_raw[1][:], as_words(wb_words[0])[:, PASS:R])
         pairs2 = gather_tab(512, 768, placed(raw0, 0))
         pairs3 = gather_tab(768, 1024, placed(raw0, 4 * TAB_STEP))
-        raw10 = load_wa(1, 0, 0, PASS, placed(raw0, RAW10))
+        raw10 = [load_wa(1, 0, 0, PASS // 2, placed(raw0, RAW10))]
+        wb_raw.append(placed(early, 8 * T)([P, PASS], I32, "wb_raw1"))
+        nc.sync.dma_start(wb_raw[1][:], as_words(wb_words[0])[:, PASS:R])
+        raw10.append(load_wa(1, 0, PASS // 2, PASS, placed(raw0, RAW10 + 2 * CHUNK_BYTES)))
         part_tab(512, 768, pairs2, held)
         grouped01 = held([P, PASS * PACK], BF16, "wa_grouped01")
-        for n in range(2):
-            round_wa(raw01[n][:], grouped01, n * P // 2, (n + 1) * P // 2)
+        for raw, lo, hi in zip(raw01, (0, 32, 80), (32, 80, P)):
+            round_wa(raw[:], grouped01, lo, hi)
         part_tab(768, 1024, pairs3, held)
         wb_codes = {}
 
-        def reorder_wb(engine, b, make):
-            wb_codes[b] = make([P, PASS], I32, "wb_codes%d" % b)
-            engine.tensor_copy(
+        def reorder_wb(copy, b, make):
+            wb_codes[b] = make([P, PASS], U32, "wb_codes%d" % b)
+            copy(
                 wb_codes[b][:].rearrange("p (t c m) -> p c t m", t=PACK, m=4),
-                wb_raw[b][:].rearrange("p (c m t) -> p c t m", t=PACK, m=4),
+                wb_raw[b][:].bitcast(U32).rearrange("p (c m t) -> p c t m", t=PACK, m=4),
             )
 
-        reorder_wb(nc.vector, 0, placed(early, 8 * PASS))
+        reorder_wb(nc.scalar.copy, 0, held)
         quantise_wa(0, 1, [grouped01], placed(early, 0))
         wb_scale = {}
 
@@ -222,15 +229,15 @@ def tile_list_kg_mul_none_kernel(
         ha0 = []
         for c in range(HA0_AHEAD):
             make = placed(early, 5 * T) if c == AFTER10 - 2 else held
-            ha0.append(copy_out(project_a(0, c, c), make, "ha0_%d" % c))
+            ha0.append(copy_out(project_a(0, c, HA0_BANKS[c]), make, "ha0_%d" % c))
 
         tab2_codes = []
         for h in range(2):
-            codes = placed(second, wb_at + 64 + 4 * HALF * (h - 1))([P, HALF], U32, "tab2_codes%d" % h)
+            codes = held([P, HALF], U32, "tab2_codes%d" % h)
             nc.vector.tensor_copy(codes[:], tab2_win[:].bitcast(U32).indirect(part_of(list2, h * HALF, (h + 1) * HALF)))
             tab2_codes.append(codes)
 
-        reorder_wb(nc.gpsimd, 1, placed(second, tab2_at))
+        reorder_wb(nc.gpsimd.tensor_copy, 1, placed(second, tab2_at))
         reorder_wb_scale(nc.gpsimd, 1, placed(second, tab2_at + 4 * PASS))
         en_codes = placed(second, 8 * R + 2 * N)([P, 2, N], I32, "en_codes")
         nc.sync.dma_start(en_codes[:], en_words.rearrange("a p n i -> p a (n i)").bitcast(I32))
@@ -267,10 +274,10 @@ def tile_list_kg_mul_none_kernel(
             nc.vector.tensor_tensor(h_chunk[b, c], by_query(bank), kept[:], MULT)
 
         def join0(c):
-            join(0, c, project_b(0, c, (c + HA0_AHEAD) % BANKS), ha0[c])
+            join(0, c, project_b(0, c, HB0_BANKS[c]), ha0[c])
 
         def late_ha0(c):
-            ha0.append(copy_out(project_a(0, c, c), placed(raw0, RAW10 + (c - HA0_AHEAD + 1) * CHUNK_BYTES), "ha0_%d" % c))
+            ha0.append(copy_out(project_a(0, c, HA0_BANKS[c]), placed(raw0, RAW10 + 64 + (c - HA0_AHEAD + 1) * CHUNK_BYTES), "ha0_%d" % c))
 
         h_scale = [held([P, J], U8, "h_scale%d" % b) for b in range(2)]
         h_codes = {}
@@ -298,14 +305,15 @@ def tile_list_kg_mul_none_kernel(
         for c in range(2):
             join0(c)
         grouped10 = placed(second, 8 * R + 2 * N + 8 * N)([P, PASS * PACK], BF16, "wa_grouped10")
-        round_wa(raw10[:], grouped10, 0, P)
+        for n in range(2):
+            round_wa(raw10[n][:], grouped10, n * P // 2, (n + 1) * P // 2)
         for c in range(2, AFTER10 - 1):
             join0(c)
         for c in range(HA0_AHEAD, CHUNKS):
             late_ha0(c)
         join0(AFTER10 - 1)
         quantise_wa(1, 0, [grouped10], placed(early, 5 * T))
-        grouped11 = placed(raw0, RAW10 + 3 * CHUNK_BYTES)([P, PASS * PACK], BF16, "wa_grouped11")
+        grouped11 = placed(raw0, RAW10 + 64 + 3 * CHUNK_BYTES)([P, PASS * PACK], BF16, "wa_grouped11")
         round_share(raw11, grouped11, SHARE11)
         round_wa(raw11[:, :, PACK * SHARE11 : PASS], grouped11, SHARE11, P)
         new_h(0, 768, 1024, placed(raw0, RAW10))
@@ -319,28 +327,23 @@ def tile_list_kg_mul_none_kernel(
 
         out_rows = out.rearrange("(u p) j -> p u j", p=P)
 
-        def score(dst, u, lo, hi):
-            cols = slice(u * P, (u + 1) * P)
+        def finish(lo, hi, n):
+            bank = bank_tile(n, [P, 2, hi - lo])
             for b in range(2):
                 codes, at = h_codes[b, lo]
-                nc.tensor.matmul_mx(
-                    out=dst,
-                    lhsT=en_codes[:, b, cols].bitcast(FP8X4),
-                    lhsT_scale=en_scale[:, b, cols],
-                    rhs=codes[:, lo - at : hi - at].bitcast(FP8X4),
-                    rhs_scale=h_scale[b][:, lo:hi],
-                    start=(b == 0),
-                    stop=(b == 1),
-                )
-
-        def finish(lo, hi, banks):
-            per_bank = 2 // len(banks)
-            scored = [bank_tile(n, [P, per_bank, hi - lo]) for n in banks]
-            for u in range(2):
-                score(scored[u // per_bank][:, u % per_bank, :], u, lo, hi)
+                for u in range(2):
+                    cols = slice(u * P, (u + 1) * P)
+                    nc.tensor.matmul_mx(
+                        out=bank[:, u, :],
+                        lhsT=en_codes[:, b, cols].bitcast(FP8X4),
+                        lhsT_scale=en_scale[:, b, cols],
+                        rhs=codes[:, lo - at : hi - at].bitcast(FP8X4),
+                        rhs_scale=h_scale[b][:, lo:hi],
+                        start=(b == 0 and u == 0),
+                        stop=(b == 1 and u == 1),
+                    )
             result = held([P, 2, hi - lo], F32, "result%d" % lo)
-            for n, bank in enumerate(scored):
-                nc.scalar.copy(result[:, n * per_bank : (n + 1) * per_bank, :], bank[:])
+            nc.scalar.copy(result[:], bank[:])
             nc.sync.dma_start(out_rows[:, :, lo:hi], result[:])
 
         for lo, hi in SCORE_RANGES:
@@ -349,7 +352,7 @@ def tile_list_kg_mul_none_kernel(
         hb1 = []
 
         def make_hb1(c):
-            make = placed(raw0, RAW10 + 64 + (c + 2) * CHUNK_BYTES) if c < len(HB1_BANKS) else held
+            make = placed(raw0, RAW10 + 128 + (c + 2) * CHUNK_BYTES) if c < len(HB1_BANKS) else held
             hb1.append(copy_out(project_b(1, c, HB1_BANKS[c % len(HB1_BANKS)]), make, "hb1_%d" % c))
 
         ha1 = []

@@ -27,22 +27,22 @@ CHUNK_BYTES = JC * PACK * 4
 TAB_STEP = 256
 SCORE_RANGES = ((0, 256), (256, 512), (512, 768), (768, 896), (896, 1024))
 H0_RANGES = ((0, 512), (512, 768), (768, 1024))
-BANKS = 8
-HA0_BANKS = (0, 1, 2, 3, 0, 1, 6, 7)
-HB0_BANKS = (6, 7, 2, 3, 0, 1, 4, 5)
-HB1_BANKS = (2, 3, 0)
-HA1_BANKS = (1, 6, 7, 4, 5)
-SCORE_BANKS = (4, 5, 0, 2, 3)
-SHARE11 = 64
-RAW00 = 6144
-RAW10 = RAW00 + 64 + 2 * J
-PAIRS = 8 * T
-RAW11 = RAW10 + 20 * PASS + 128
-FIRST = 64
+HB1_BANKS = (0, 1, 2)
+HA1_BANKS = (3, 4, 5, 6, 7)
+SCORE_BANKS = (6, 7, 2, 0, 1)
+GROUPS = 128
+WA01_CUTS = (0, 48, 96, GROUPS)
+SHARE11 = 32
 HA1_LEAD = 2
 HB1_LEAD = 4
 AFTER10 = 6
-HA0_AHEAD = 6
+EDGE = 64
+PAIRS_AT = 0
+LAST01_AT = 3 * CHUNK_BYTES
+HB0_4_AT = LAST01_AT - CHUNK_BYTES + EDGE
+RAW10_AT = LAST01_AT + 4 * CHUNK_BYTES
+RAW11_AT = RAW10_AT + 5 * CHUNK_BYTES + 2 * EDGE
+WIN_AT = RAW11_AT + 4 * CHUNK_BYTES
 
 
 def as_words(dram_pass):
@@ -56,74 +56,104 @@ def tile_list_kg_mul_none_kernel(
     with ExitStack() as ctx:
         lists = ctx.enter_context(tc.tile_pool(name="lists", bufs=1))
         keep = ctx.enter_context(tc.tile_pool(name="keep", bufs=1))
-        second = ctx.enter_context(tc.tile_pool(name="second", bufs=1))
-        early = ctx.enter_context(tc.tile_pool(name="early", bufs=1))
-        raw0 = ctx.enter_context(tc.tile_pool(name="raw0", bufs=1))
+        shared = ctx.enter_context(tc.tile_pool(name="shared", bufs=1))
         psum = ctx.enter_context(tc.psum_pool(name="psum", bufs=1))
 
         def held(shape, dtype, name):
             return keep.tile(shape, dtype, name=name, align_bytes=64)
 
-        def placed(pool, offset):
-            return lambda shape, dtype, name: pool.tile(shape, dtype, name=name, offset=offset, align_bytes=64)
+        def placed(offset):
+            return lambda shape, dtype, name: shared.tile(shape, dtype, name=name, offset=offset, align_bytes=64)
 
         list2 = lists.tile([P, J // LIST_GROUP], U16, name="list2")
         list1 = lists.tile([P, J // LIST_GROUP], U16, name="list1")
-
-        win_at = 4 * R
-        wb_at = win_at + 64 - 4 * PASS
-        tab2_scale_at = win_at + 128
-        tab2_at = tab2_scale_at + J
-        tab_scale_win = placed(second, win_at)([P, T], U8, "tab_scale_win")
+        tab_scale_win = placed(WIN_AT)([P, T], U8, "tab_scale_win")
         tab2_scale_win = held([P, T], U8, "tab2_scale_win")
         wb_scale_raw = held([P, R], U8, "wb_scale_raw")
         tab_scale1 = held([P, J], U8, "tab_scale1")
+        tab2_scale = held([P, J], U8, "tab2_scale")
+        en_scale = held([P, 2, N], U8, "en_scale")
         nc.gpsimd.memset(tab_scale_win[:].bitcast(I32), 0)
+        nc.vector.memset(wb_scale_raw[:].bitcast(I32), 0)
         nc.vector.memset(tab2_scale_win[0:96, :].bitcast(I32), 0)
         nc.vector.memset(tab2_scale_win[96:112, :].bitcast(I32), 0)
-        nc.gpsimd.memset(wb_scale_raw[:].bitcast(I32), 0)
+        nc.gpsimd.memset(tab2_scale[:].bitcast(I32), 0)
         nc.gpsimd.memset(tab_scale1[96:128, :].bitcast(I32), 0)
+        nc.gpsimd.memset(en_scale[:].bitcast(I32), 0)
 
         def load_wa(b, a, lo, hi, make):
-            raw = make([P, PACK, hi - lo], F32, "wa_raw%d%d_%d" % (b, a, lo))
-            rows = wa[a * PASS : (a + 1) * PASS, b * PASS + lo : b * PASS + hi]
+            raw = make([P, PACK, PACK * (hi - lo)], F32, "wa_raw%d%d_%d" % (b, a, lo))
+            rows = wa[a * PASS : (a + 1) * PASS, b * PASS + PACK * lo : b * PASS + PACK * hi]
             nc.sync.dma_start(raw[:], rows.rearrange("(p i) c -> p i c", i=PACK))
+            return raw
+
+        def load_wb(b):
+            raw = held([P, PASS], I32, "wb_raw%d" % b)
+            nc.sync.dma_start(raw[:], as_words(wb_words[0])[:, b * PASS : (b + 1) * PASS])
             return raw
 
         nc.sync.dma_start(list2[:], offs2)
         nc.sync.dma_start(tab2_scale_win[112:128, :].bitcast(I32), tab2_scales[0].bitcast(I32))
-        raw00 = [load_wa(0, 0, 0, PACK * FIRST, placed(early, 8 * T))]
         nc.sync.dma_start(list1[:], offs)
-        tab_scale_rows = tab_scales.rearrange("a (q e) t -> e q a t", e=4)
-        for e in range(4):
-            nc.sync.dma_start(tab_scale_win[e:P:16, :].bitcast(I32), tab_scale_rows[e].bitcast(I32))
-        raw00.append(load_wa(0, 0, PACK * FIRST, PASS, placed(raw0, RAW00)))
-        tab_win = placed(early, 0)([P, T], I32, "tab_win")
-        nc.sync.dma_start(tab_win[:], as_words(tab_words[0]))
+        tab2_win = held([P, T], I32, "tab2_win")
+        nc.sync.dma_start(tab2_win[:], as_words(tab2_words[0]))
+        wb_raw = [load_wb(0)]
         wb_scale_rows = wb_scales[0].rearrange("(q e) r -> e q r", e=4)
         for e in range(4):
             nc.sync.dma_start(wb_scale_raw[e:P:32, :].bitcast(I32), wb_scale_rows[e].bitcast(I32))
-        raw01 = [
-            load_wa(0, 1, 0, PACK * 32, placed(raw0, RAW11)),
-            load_wa(0, 1, PACK * 32, PACK * 80, held),
-            load_wa(0, 1, PACK * 80, PASS, placed(early, 12 * T)),
-        ]
-
+        halves = ((0, GROUPS // 2), (GROUPS // 2, GROUPS))
+        raw00 = [load_wa(0, 0, *halves[0], held)]
+        tab_scale_rows = tab_scales.rearrange("a (q e) t -> e q a t", e=4)
+        for e in range(4):
+            nc.sync.dma_start(tab_scale_win[e:P:16, :].bitcast(I32), tab_scale_rows[e].bitcast(I32))
+        raw00.append(load_wa(0, 0, *halves[1], held))
         tab2_scale_picked = held([P, J], U8, "tab2_scale_picked")
         nc.vector.tensor_copy(tab2_scale_picked[:], tab2_scale_win[:].indirect(list2[:]))
+        for e in range(4):
+            nc.sync.dma_start(tab2_scale[e:P:32, :].bitcast(I32), tab2_scale_picked[112 + e : P : 4, :].bitcast(I32))
+        tab_win = held([P, T], I32, "tab_win")
+        nc.sync.dma_start(tab_win[:], as_words(tab_words[0]))
+        cuts01 = list(zip(WA01_CUTS, WA01_CUTS[1:]))
+        raw01 = [load_wa(0, 1, lo, hi, placed(LAST01_AT) if hi == GROUPS else held) for lo, hi in cuts01]
+        wb_raw.append(load_wb(1))
+
+        wb_codes, wb_scale = {}, {}
+
+        def reorder_wb(copy, b, make):
+            wb_codes[b] = make([P, PASS], U32, "wb_codes%d" % b)
+            copy(
+                wb_codes[b][:].rearrange("p (t c m) -> p c t m", t=PACK, m=4),
+                wb_raw[b][:].bitcast(U32).rearrange("p (c m t) -> p c t m", t=PACK, m=4),
+            )
+
+        def reorder_wb_scale(engine, b, make):
+            wb_scale[b] = make([P, PASS], U8, "wb_scale%d" % b)
+            engine.tensor_copy(
+                wb_scale[b][:].rearrange("p (t c m) -> p c t m", t=PACK, m=16),
+                wb_scale_raw[:, b * PASS : (b + 1) * PASS].rearrange("p (c m t) -> p c t m", t=PACK, m=16),
+            )
+
+        def part_of(lst, lo, hi):
+            return lst[:, lo // LIST_GROUP : hi // LIST_GROUP]
+
+        reorder_wb(nc.scalar.copy, 0, held)
+        tab2_codes = []
+        for h in range(2):
+            codes = held([P, HALF], U32, "tab2_codes%d" % h)
+            nc.vector.tensor_copy(codes[:], tab2_win[:].bitcast(U32).indirect(part_of(list2, h * HALF, (h + 1) * HALF)))
+            tab2_codes.append(codes)
+        reorder_wb_scale(nc.vector, 0, held)
         tab_scale0 = held([P, J], U8, "tab_scale0")
         nc.vector.tensor_copy(tab_scale0[:], tab_scale_win[:].indirect(list1[:]))
         nc.sync.dma_start(tab_scale1[0:112, :].bitcast(I32), tab_scale0[16:128, :].bitcast(I32))
         tab_scale = (tab_scale0, tab_scale1)
-
-        wb_raw = [placed(second, wb_at)([P, PASS], I32, "wb_raw0")]
-        tab2_win = placed(second, tab2_at)([P, T], I32, "tab2_win")
-        nc.sync.dma_start(wb_raw[0][:], as_words(wb_words[0])[:, 0:PASS])
-        nc.sync.dma_start(tab2_win[:], as_words(tab2_words[0]))
-        tab2_scale = placed(second, tab2_scale_at)([P, J], U8, "tab2_scale")
-        nc.gpsimd.memset(tab2_scale[:].bitcast(I32), 0)
+        raw10 = load_wa(1, 0, 0, GROUPS, placed(RAW10_AT))
+        raw11 = load_wa(1, 1, 0, GROUPS, placed(RAW11_AT))
+        en_codes = held([P, 2, N], I32, "en_codes")
+        nc.sync.dma_start(en_codes[:], en_words.rearrange("a p n i -> p a (n i)").bitcast(I32))
+        en_scale_rows = en_scales.rearrange("a (q e) n -> e q a n", e=4)
         for e in range(4):
-            nc.sync.dma_start(tab2_scale[e:P:32, :].bitcast(I32), tab2_scale_picked[112 + e : P : 4, :].bitcast(I32))
+            nc.sync.dma_start(en_scale[e:P:32, :, :].bitcast(I32), en_scale_rows[e].bitcast(I32))
 
         def round_wa(raw, grouped, lo, hi):
             src = raw.rearrange("p i (m t) -> p m i t", t=PACK)
@@ -142,9 +172,6 @@ def tile_list_kg_mul_none_kernel(
                     out=wa_codes[b, a][:, cols].bitcast(FP8X4), scales=wa_scale[b, a][:, cols], in_=piece[:]
                 )
 
-        def part_of(lst, lo, hi):
-            return lst[:, lo // LIST_GROUP : hi // LIST_GROUP]
-
         tab_codes = {}
 
         def gather_tab(lo, hi, make):
@@ -157,47 +184,6 @@ def tile_list_kg_mul_none_kernel(
             nc.vector.tensor_copy(parted[:].bitcast(U16), pairs[:].bitcast(U16).rearrange("p (j d) -> p d j", d=2))
             for j0 in range(lo, hi, JC):
                 tab_codes[j0 // JC] = parted[:, :, 2 * (j0 - lo) : 2 * (j0 - lo + JC)]
-
-        pairs = [gather_tab(lo, lo + TAB_STEP, placed(raw0, 4 * lo)) for lo in (0, TAB_STEP)]
-        for n in range(2):
-            part_tab(n * TAB_STEP, (n + 1) * TAB_STEP, pairs[n], held)
-        grouped00 = held([P, PASS * PACK], BF16, "wa_grouped00")
-        round_wa(raw00[0][:], grouped00, 0, FIRST)
-        round_wa(raw00[1][:], grouped00, FIRST, P)
-        quantise_wa(0, 0, [grouped00], held)
-        pairs2 = gather_tab(512, 768, placed(raw0, 0))
-        pairs3 = gather_tab(768, 1024, placed(raw0, 4 * TAB_STEP))
-        raw10 = [load_wa(1, 0, 0, PASS // 2, placed(raw0, RAW10))]
-        wb_raw.append(placed(early, 8 * T)([P, PASS], I32, "wb_raw1"))
-        nc.sync.dma_start(wb_raw[1][:], as_words(wb_words[0])[:, PASS:R])
-        raw10.append(load_wa(1, 0, PASS // 2, PASS, placed(raw0, RAW10 + 2 * CHUNK_BYTES)))
-        part_tab(512, 768, pairs2, held)
-        grouped01 = held([P, PASS * PACK], BF16, "wa_grouped01")
-        for raw, lo, hi in zip(raw01, (0, 32, 80), (32, 80, P)):
-            round_wa(raw[:], grouped01, lo, hi)
-        part_tab(768, 1024, pairs3, held)
-        wb_codes = {}
-
-        def reorder_wb(copy, b, make):
-            wb_codes[b] = make([P, PASS], U32, "wb_codes%d" % b)
-            copy(
-                wb_codes[b][:].rearrange("p (t c m) -> p c t m", t=PACK, m=4),
-                wb_raw[b][:].bitcast(U32).rearrange("p (c m t) -> p c t m", t=PACK, m=4),
-            )
-
-        reorder_wb(nc.scalar.copy, 0, held)
-        quantise_wa(0, 1, [grouped01], placed(early, 0))
-        wb_scale = {}
-
-        def reorder_wb_scale(engine, b, make):
-            wb_scale[b] = make([P, PASS], U8, "wb_scale%d" % b)
-            engine.tensor_copy(
-                wb_scale[b][:].rearrange("p (t c m) -> p c t m", t=PACK, m=16),
-                wb_scale_raw[:, b * PASS : (b + 1) * PASS].rearrange("p (c m t) -> p c t m", t=PACK, m=16),
-            )
-
-        reorder_wb_scale(nc.vector, 0, placed(early, 12 * T))
-        raw11 = load_wa(1, 1, 0, PASS, placed(raw0, RAW11))
 
         def bank_tile(n, shape):
             return psum.tile(shape, F32, name="bank", tag="bank%d" % n)
@@ -221,31 +207,12 @@ def tile_list_kg_mul_none_kernel(
         def by_query(bank):
             return bank[:].rearrange("p t j -> p j t")
 
-        def copy_out(bank, make, name):
-            kept = make([P, JC, PACK], F32, name)
-            nc.scalar.copy(kept[:], by_query(bank))
+        def copy_into(bank, kept):
+            nc.scalar.copy(kept, by_query(bank))
             return kept
 
-        ha0 = []
-        for c in range(HA0_AHEAD):
-            make = placed(early, 5 * T) if c == AFTER10 - 2 else held
-            ha0.append(copy_out(project_a(0, c, HA0_BANKS[c]), make, "ha0_%d" % c))
-
-        tab2_codes = []
-        for h in range(2):
-            codes = held([P, HALF], U32, "tab2_codes%d" % h)
-            nc.vector.tensor_copy(codes[:], tab2_win[:].bitcast(U32).indirect(part_of(list2, h * HALF, (h + 1) * HALF)))
-            tab2_codes.append(codes)
-
-        reorder_wb(nc.gpsimd.tensor_copy, 1, placed(second, tab2_at))
-        reorder_wb_scale(nc.gpsimd, 1, placed(second, tab2_at + 4 * PASS))
-        en_codes = placed(second, 8 * R + 2 * N)([P, 2, N], I32, "en_codes")
-        nc.sync.dma_start(en_codes[:], en_words.rearrange("a p n i -> p a (n i)").bitcast(I32))
-        en_scale = placed(second, 8 * R)([P, 2, N], U8, "en_scale")
-        nc.gpsimd.memset(en_scale[:].bitcast(I32), 0)
-        en_scale_rows = en_scales.rearrange("a (q e) n -> e q a n", e=4)
-        for e in range(4):
-            nc.sync.dma_start(en_scale[e:P:32, :, :].bitcast(I32), en_scale_rows[e].bitcast(I32))
+        def copy_out(bank, make, name):
+            return copy_into(bank, make([P, JC, PACK], F32, name)[:])
 
         def project_b(b, c, n):
             bank = bank_tile(n, [P, PACK, JC])
@@ -263,6 +230,29 @@ def tile_list_kg_mul_none_kernel(
                 )
             return bank
 
+        grouped00 = held([P, PASS * PACK], BF16, "wa_grouped00")
+        for raw, (lo, hi) in zip(raw00, halves):
+            round_wa(raw[:], grouped00, lo, hi)
+        quantise_wa(0, 0, [grouped00], held)
+        hb0_banks = [project_b(0, c, c) for c in range(CHUNKS)]
+        hb0 = [copy_out(hb0_banks[c], held, "hb0_%d" % c) for c in range(4)]
+        pairs = [gather_tab(lo, lo + TAB_STEP, placed(PAIRS_AT + 4 * lo)) for lo in (0, TAB_STEP)]
+        for n in range(2):
+            part_tab(n * TAB_STEP, (n + 1) * TAB_STEP, pairs[n], held)
+        pairs = [gather_tab(HALF + lo, HALF + lo + TAB_STEP, placed(PAIRS_AT + 4 * lo)) for lo in (0, TAB_STEP)]
+        part_tab(HALF, HALF + TAB_STEP, pairs[0], held)
+        grouped01 = held([P, PASS * PACK], BF16, "wa_grouped01")
+        for raw, (lo, hi) in zip(raw01, cuts01):
+            round_wa(raw[:], grouped01, lo, hi)
+        quantise_wa(0, 1, [grouped01], held)
+        part_tab(HALF + TAB_STEP, J, pairs[1], placed(LAST01_AT + EDGE))
+        hb0.append(copy_out(hb0_banks[4], placed(HB0_4_AT), "hb0_4"))
+        last_hb0 = placed(LAST01_AT + CHUNK_BYTES - EDGE)([P, 3, JC, PACK], F32, "hb0_last")
+        for c in range(5, CHUNKS):
+            hb0.append(copy_into(hb0_banks[c], last_hb0[:, c - 5]))
+        reorder_wb(nc.gpsimd.tensor_copy, 1, placed(PAIRS_AT + 8 * TAB_STEP - EDGE))
+        reorder_wb_scale(nc.gpsimd, 1, placed(PAIRS_AT + 4 * TAB_STEP))
+
         h_bf16, h_chunk = {}, {}
 
         def new_h(b, lo, hi, make):
@@ -271,13 +261,10 @@ def tile_list_kg_mul_none_kernel(
                 h_chunk[b, j0 // JC] = h_bf16[b, lo][:, j0 - lo : j0 - lo + JC, :]
 
         def join(b, c, bank, kept):
-            nc.vector.tensor_tensor(h_chunk[b, c], by_query(bank), kept[:], MULT)
+            nc.vector.tensor_tensor(h_chunk[b, c], by_query(bank), kept, MULT)
 
         def join0(c):
-            join(0, c, project_b(0, c, HB0_BANKS[c]), ha0[c])
-
-        def late_ha0(c):
-            ha0.append(copy_out(project_a(0, c, HA0_BANKS[c]), placed(raw0, RAW10 + 64 + (c - HA0_AHEAD + 1) * CHUNK_BYTES), "ha0_%d" % c))
+            join(0, c, project_a(0, c, c), hb0[c])
 
         h_scale = [held([P, J], U8, "h_scale%d" % b) for b in range(2)]
         h_codes = {}
@@ -302,25 +289,19 @@ def tile_list_kg_mul_none_kernel(
             dst = grouped[:].rearrange("p (h l m i) -> p h m i l", h=2, l=2, i=PACK)
             nc.vector.tensor_copy(dst[:, :, 0:share], src)
 
-        for c in range(2):
+        for c in range(AFTER10):
             join0(c)
-        grouped10 = placed(second, 8 * R + 2 * N + 8 * N)([P, PASS * PACK], BF16, "wa_grouped10")
-        for n in range(2):
-            round_wa(raw10[n][:], grouped10, n * P // 2, (n + 1) * P // 2)
-        for c in range(2, AFTER10 - 1):
-            join0(c)
-        for c in range(HA0_AHEAD, CHUNKS):
-            late_ha0(c)
-        join0(AFTER10 - 1)
-        quantise_wa(1, 0, [grouped10], placed(early, 5 * T))
-        grouped11 = placed(raw0, RAW10 + 64 + 3 * CHUNK_BYTES)([P, PASS * PACK], BF16, "wa_grouped11")
+        grouped10 = held([P, PASS * PACK], BF16, "wa_grouped10")
+        round_wa(raw10[:], grouped10, 0, P)
+        quantise_wa(1, 0, [grouped10], placed(HB0_4_AT))
+        grouped11 = placed(RAW10_AT + 3 * CHUNK_BYTES)([P, PASS * PACK], BF16, "wa_grouped11")
         round_share(raw11, grouped11, SHARE11)
         round_wa(raw11[:, :, PACK * SHARE11 : PASS], grouped11, SHARE11, P)
-        new_h(0, 768, 1024, placed(raw0, RAW10))
+        new_h(0, 768, 1024, placed(RAW10_AT))
         for c in range(AFTER10, CHUNKS):
             join0(c)
         quantise_wa(1, 1, [grouped11], held)
-        new_codes(0, 0, J, placed(raw0, RAW11))
+        new_codes(0, 0, J, placed(RAW11_AT))
         for lo, hi in H0_RANGES:
             quantise_h(0, lo, hi)
         new_codes(1, 0, J, held)
@@ -352,7 +333,7 @@ def tile_list_kg_mul_none_kernel(
         hb1 = []
 
         def make_hb1(c):
-            make = placed(raw0, RAW10 + 128 + (c + 2) * CHUNK_BYTES) if c < len(HB1_BANKS) else held
+            make = placed(RAW10_AT + EDGE + (c + 2) * CHUNK_BYTES) if c < len(HB1_BANKS) else held
             hb1.append(copy_out(project_b(1, c, HB1_BANKS[c % len(HB1_BANKS)]), make, "hb1_%d" % c))
 
         ha1 = []

@@ -18,31 +18,31 @@ MULT = mybir.AluOpType.mult
 P = 128
 PACK = 4
 PASS = P * PACK
-QUADS = 4
+QUAD = 32
+ROWS = 16
 LIST_GROUP = 16
 HALF = J // 2
 JC = 128
 CHUNKS = J // JC
-CHUNK_BYTES = JC * PACK * 4
+GROUPS = PASS // PACK
 TAB_STEP = 256
+TAB2_ROW = 4
+WB_ROW = 8
+HB0_EARLY = 6
+SHARE01 = 48
+SHARE11 = 40
 SCORE_RANGES = ((0, 256), (256, 512), (512, 768), (768, 896), (896, 1024))
-H0_RANGES = ((0, 512), (512, 768), (768, 1024))
-HB1_BANKS = (0, 1, 2)
-HA1_BANKS = (3, 4, 5, 6, 7)
-SCORE_BANKS = (6, 7, 2, 0, 1)
-GROUPS = 128
-WA01_CUTS = (0, 48, 96, GROUPS)
-SHARE11 = 32
-HA1_LEAD = 2
-HB1_LEAD = 4
-AFTER10 = 6
-EDGE = 64
-PAIRS_AT = 0
-LAST01_AT = 3 * CHUNK_BYTES
-HB0_4_AT = LAST01_AT - CHUNK_BYTES + EDGE
-RAW10_AT = LAST01_AT + 4 * CHUNK_BYTES
-RAW11_AT = RAW10_AT + 5 * CHUNK_BYTES + 2 * EDGE
-WIN_AT = RAW11_AT + 4 * CHUNK_BYTES
+HB_BANKS = ((0, 1, 2, 3, 4, 5, 6, 7), (6, 7, 2, 3, 4, 5, 0, 1))
+HA_BANKS = ((0, 1, 2, 3, 4, 5, 0, 1), HB_BANKS[1])
+SCORE_BANKS = tuple(HB_BANKS[1][c] for c in (0, 2, 4, 5, 6))
+KIB = 1024
+RAW01_AT = 0
+GROUPED01_AT = 8 * KIB
+RAW11_AT = 12 * KIB
+RAW10_AT = 32 * KIB
+WB0_AT = 40 * KIB
+JOINS_BEFORE_WA10 = 6
+HA1_LEAD = 3
 
 
 def as_words(dram_pass):
@@ -65,57 +65,76 @@ def tile_list_kg_mul_none_kernel(
         def placed(offset):
             return lambda shape, dtype, name: shared.tile(shape, dtype, name=name, offset=offset, align_bytes=64)
 
-        list2 = lists.tile([P, J // LIST_GROUP], U16, name="list2")
         list1 = lists.tile([P, J // LIST_GROUP], U16, name="list1")
-        tab_scale_win = placed(WIN_AT)([P, T], U8, "tab_scale_win")
+        list2 = lists.tile([P, J // LIST_GROUP], U16, name="list2")
+        tab_scale_win = held([P, T], U8, "tab_scale_win")
         tab2_scale_win = held([P, T], U8, "tab2_scale_win")
         wb_scale_raw = held([P, R], U8, "wb_scale_raw")
-        tab_scale1 = held([P, J], U8, "tab_scale1")
         tab2_scale = held([P, J], U8, "tab2_scale")
+        tab_scale = [held([P, J], U8, "tab_scale%d" % a) for a in range(2)]
         en_scale = held([P, 2, N], U8, "en_scale")
-        nc.gpsimd.memset(tab_scale_win[:].bitcast(I32), 0)
-        nc.vector.memset(wb_scale_raw[:].bitcast(I32), 0)
         nc.vector.memset(tab2_scale_win[0:96, :].bitcast(I32), 0)
         nc.vector.memset(tab2_scale_win[96:112, :].bitcast(I32), 0)
+        nc.vector.memset(tab_scale_win[0:96, :].bitcast(I32), 0)
+        nc.gpsimd.memset(wb_scale_raw[:].bitcast(I32), 0)
         nc.gpsimd.memset(tab2_scale[:].bitcast(I32), 0)
-        nc.gpsimd.memset(tab_scale1[96:128, :].bitcast(I32), 0)
+        for a in range(2):
+            nc.gpsimd.memset(tab_scale[a][:].bitcast(I32), 0)
         nc.gpsimd.memset(en_scale[:].bitcast(I32), 0)
 
-        def load_wa(b, a, lo, hi, make):
-            raw = make([P, PACK, PACK * (hi - lo)], F32, "wa_raw%d%d_%d" % (b, a, lo))
-            rows = wa[a * PASS : (a + 1) * PASS, b * PASS + PACK * lo : b * PASS + PACK * hi]
+        def load_wa(b, a, make):
+            raw = make([P, PACK, PASS], F32, "wa_raw%d%d" % (b, a))
+            rows = wa[a * PASS : (a + 1) * PASS, b * PASS : (b + 1) * PASS]
             nc.sync.dma_start(raw[:], rows.rearrange("(p i) c -> p i c", i=PACK))
             return raw
 
-        def load_wb(b):
-            raw = held([P, PASS], I32, "wb_raw%d" % b)
+        def load_wb(b, make):
+            raw = make([P, PASS], I32, "wb_raw%d" % b)
             nc.sync.dma_start(raw[:], as_words(wb_words[0])[:, b * PASS : (b + 1) * PASS])
             return raw
 
+        def move_rows(plane, first_row, picked, at):
+            for e in range(4):
+                nc.sync.dma_start(
+                    plane[first_row + e : P : QUAD, :].bitcast(I32), picked[at + e : at + ROWS : 4, :].bitcast(I32)
+                )
+
+        def part_of(lst, lo, hi):
+            return lst[:, lo // LIST_GROUP : hi // LIST_GROUP]
+
         nc.sync.dma_start(list2[:], offs2)
-        nc.sync.dma_start(tab2_scale_win[112:128, :].bitcast(I32), tab2_scales[0].bitcast(I32))
+        nc.sync.dma_start(tab2_scale_win[P - ROWS : P, :].bitcast(I32), tab2_scales[0].bitcast(I32))
         nc.sync.dma_start(list1[:], offs)
-        tab2_win = held([P, T], I32, "tab2_win")
-        nc.sync.dma_start(tab2_win[:], as_words(tab2_words[0]))
-        wb_raw = [load_wb(0)]
+        nc.sync.dma_start(
+            tab_scale_win[P - 2 * ROWS : P, :].bitcast(I32), tab_scales.rearrange("a g t -> (a g) t").bitcast(I32)
+        )
+        raw00 = load_wa(0, 0, held)
         wb_scale_rows = wb_scales[0].rearrange("(q e) r -> e q r", e=4)
         for e in range(4):
-            nc.sync.dma_start(wb_scale_raw[e:P:32, :].bitcast(I32), wb_scale_rows[e].bitcast(I32))
-        halves = ((0, GROUPS // 2), (GROUPS // 2, GROUPS))
-        raw00 = [load_wa(0, 0, *halves[0], held)]
-        tab_scale_rows = tab_scales.rearrange("a (q e) t -> e q a t", e=4)
-        for e in range(4):
-            nc.sync.dma_start(tab_scale_win[e:P:16, :].bitcast(I32), tab_scale_rows[e].bitcast(I32))
-        raw00.append(load_wa(0, 0, *halves[1], held))
+            nc.sync.dma_start(wb_scale_raw[WB_ROW + e : P : QUAD, :].bitcast(I32), wb_scale_rows[e].bitcast(I32))
+        tab2_win = held([P, T], I32, "tab2_win")
+        nc.sync.dma_start(tab2_win[:], as_words(tab2_words[0]))
+        wb_raw = [load_wb(0, placed(WB0_AT))]
+
         tab2_scale_picked = held([P, J], U8, "tab2_scale_picked")
         nc.vector.tensor_copy(tab2_scale_picked[:], tab2_scale_win[:].indirect(list2[:]))
-        for e in range(4):
-            nc.sync.dma_start(tab2_scale[e:P:32, :].bitcast(I32), tab2_scale_picked[112 + e : P : 4, :].bitcast(I32))
+        tab_scale_picked = held([P, J], U8, "tab_scale_picked")
+        nc.vector.tensor_copy(tab_scale_picked[:], tab_scale_win[:].indirect(list1[:]))
+
+        move_rows(tab2_scale, TAB2_ROW, tab2_scale_picked, P - ROWS)
         tab_win = held([P, T], I32, "tab_win")
         nc.sync.dma_start(tab_win[:], as_words(tab_words[0]))
-        cuts01 = list(zip(WA01_CUTS, WA01_CUTS[1:]))
-        raw01 = [load_wa(0, 1, lo, hi, placed(LAST01_AT) if hi == GROUPS else held) for lo, hi in cuts01]
-        wb_raw.append(load_wb(1))
+        move_rows(tab_scale[0], 0, tab_scale_picked, P - 2 * ROWS)
+        raw01 = load_wa(0, 1, placed(RAW01_AT))
+        move_rows(tab_scale[1], 0, tab_scale_picked, P - ROWS)
+        wb_raw.append(load_wb(1, held))
+        raw10 = load_wa(1, 0, placed(RAW10_AT))
+        raw11 = load_wa(1, 1, placed(RAW11_AT))
+        en_codes = held([P, 2, N], I32, "en_codes")
+        nc.sync.dma_start(en_codes[:], en_words.rearrange("a p n i -> p a (n i)").bitcast(I32))
+        en_scale_rows = en_scales.rearrange("a (q e) n -> e q a n", e=4)
+        for e in range(4):
+            nc.sync.dma_start(en_scale[e:P:QUAD, :, :].bitcast(I32), en_scale_rows[e].bitcast(I32))
 
         wb_codes, wb_scale = {}, {}
 
@@ -133,63 +152,48 @@ def tile_list_kg_mul_none_kernel(
                 wb_scale_raw[:, b * PASS : (b + 1) * PASS].rearrange("p (c m t) -> p c t m", t=PACK, m=16),
             )
 
-        def part_of(lst, lo, hi):
-            return lst[:, lo // LIST_GROUP : hi // LIST_GROUP]
-
-        reorder_wb(nc.scalar.copy, 0, held)
-        tab2_codes = []
-        for h in range(2):
-            codes = held([P, HALF], U32, "tab2_codes%d" % h)
-            nc.vector.tensor_copy(codes[:], tab2_win[:].bitcast(U32).indirect(part_of(list2, h * HALF, (h + 1) * HALF)))
-            tab2_codes.append(codes)
-        reorder_wb_scale(nc.vector, 0, held)
-        tab_scale0 = held([P, J], U8, "tab_scale0")
-        nc.vector.tensor_copy(tab_scale0[:], tab_scale_win[:].indirect(list1[:]))
-        nc.sync.dma_start(tab_scale1[0:112, :].bitcast(I32), tab_scale0[16:128, :].bitcast(I32))
-        tab_scale = (tab_scale0, tab_scale1)
-        raw10 = load_wa(1, 0, 0, GROUPS, placed(RAW10_AT))
-        raw11 = load_wa(1, 1, 0, GROUPS, placed(RAW11_AT))
-        en_codes = held([P, 2, N], I32, "en_codes")
-        nc.sync.dma_start(en_codes[:], en_words.rearrange("a p n i -> p a (n i)").bitcast(I32))
-        en_scale_rows = en_scales.rearrange("a (q e) n -> e q a n", e=4)
-        for e in range(4):
-            nc.sync.dma_start(en_scale[e:P:32, :, :].bitcast(I32), en_scale_rows[e].bitcast(I32))
-
-        def round_wa(raw, grouped, lo, hi):
-            src = raw.rearrange("p i (m t) -> p m i t", t=PACK)
+        def round_on_scalar(raw, grouped, lo):
+            src = raw[:].rearrange("p i (m t) -> p m i t", t=PACK)
             dst = grouped[:].rearrange("p (t m i) -> p m i t", t=PACK, i=PACK)
-            nc.scalar.copy(dst[:, lo:hi], src)
+            nc.scalar.copy(dst[:, lo:GROUPS], src[:, lo:GROUPS])
+
+        def round_on_vector(raw, grouped, hi):
+            src = raw[:].rearrange("p i (m h l) -> p h m i l", h=2, l=2)
+            dst = grouped[:].rearrange("p (h l m i) -> p h m i l", h=2, l=2, i=PACK)
+            nc.vector.tensor_copy(dst[:, :, 0:hi], src[:, :, 0:hi])
 
         wa_codes, wa_scale = {}, {}
 
-        def quantise_wa(b, a, pieces, make):
+        def quantise_wa(b, a, grouped, make):
             wa_codes[b, a] = make([P, PASS], U32, "wa_codes%d%d" % (b, a))
             wa_scale[b, a] = held([P, PASS], U8, "wa_scale%d%d" % (b, a))
-            width = PASS // len(pieces)
-            for n, piece in enumerate(pieces):
-                cols = slice(n * width, (n + 1) * width)
-                nc.vector.quantize_mx(
-                    out=wa_codes[b, a][:, cols].bitcast(FP8X4), scales=wa_scale[b, a][:, cols], in_=piece[:]
-                )
+            nc.vector.quantize_mx(out=wa_codes[b, a][:].bitcast(FP8X4), scales=wa_scale[b, a][:], in_=grouped[:])
+
+        def new_grouped(b, a, make):
+            return make([P, PASS * PACK], BF16, "wa_grouped%d%d" % (b, a))
 
         tab_codes = {}
 
-        def gather_tab(lo, hi, make):
-            pairs = make([P, hi - lo], U32, "tab_pairs%d" % lo)
-            nc.vector.tensor_copy(pairs[:], tab_win[:].bitcast(U32).indirect(part_of(list1, lo, hi)))
+        def gather_tab(n):
+            pairs = held([P, TAB_STEP], U32, "tab_pairs%d" % n)
+            lo = n * TAB_STEP
+            nc.vector.tensor_copy(pairs[:], tab_win[:].bitcast(U32).indirect(part_of(list1, lo, lo + TAB_STEP)))
             return pairs
 
-        def part_tab(lo, hi, pairs, make):
-            parted = make([P, 2, 2 * (hi - lo)], U8, "tab_codes%d" % lo)
+        def part_tab(n, pairs):
+            parted = held([P, 2, 2 * TAB_STEP], U8, "tab_codes%d" % n)
             nc.vector.tensor_copy(parted[:].bitcast(U16), pairs[:].bitcast(U16).rearrange("p (j d) -> p d j", d=2))
-            for j0 in range(lo, hi, JC):
-                tab_codes[j0 // JC] = parted[:, :, 2 * (j0 - lo) : 2 * (j0 - lo + JC)]
+            for j0 in range(0, TAB_STEP, JC):
+                tab_codes[(n * TAB_STEP + j0) // JC] = parted[:, :, 2 * j0 : 2 * (j0 + JC)]
 
         def bank_tile(n, shape):
             return psum.tile(shape, F32, name="bank", tag="bank%d" % n)
 
-        def project_a(b, c, n):
-            bank = bank_tile(n, [P, PACK, JC])
+        def by_query(bank):
+            return bank[:].rearrange("p t j -> p j t")
+
+        def project_a(b, c):
+            bank = bank_tile(HA_BANKS[b][c], [P, PACK, JC])
             for a in range(2):
                 for t in range(PACK):
                     cols = slice(t * P, (t + 1) * P)
@@ -204,158 +208,136 @@ def tile_list_kg_mul_none_kernel(
                     )
             return bank
 
-        def by_query(bank):
-            return bank[:].rearrange("p t j -> p j t")
+        tab2_codes = []
 
-        def copy_into(bank, kept):
-            nc.scalar.copy(kept, by_query(bank))
-            return kept
-
-        def copy_out(bank, make, name):
-            return copy_into(bank, make([P, JC, PACK], F32, name)[:])
-
-        def project_b(b, c, n):
-            bank = bank_tile(n, [P, PACK, JC])
+        def project_b(b, c):
+            bank = bank_tile(HB_BANKS[b][c], [P, PACK, JC])
             h, j0 = divmod(c * JC, HALF)
             for t in range(PACK):
-                cols = slice(b * PASS + t * P, b * PASS + (t + 1) * P)
+                cols = slice(t * P, (t + 1) * P)
                 nc.tensor.matmul_mx(
                     out=bank[:, t, :],
-                    lhsT=wb_codes[b][:, t * P : (t + 1) * P].bitcast(FP8X4),
-                    lhsT_scale=wb_scale[b][:, t * P : (t + 1) * P],
+                    lhsT=wb_codes[b][:, cols].bitcast(FP8X4),
+                    lhsT_scale=wb_scale[b][WB_ROW:P, cols],
                     rhs=tab2_codes[h][:, j0 : j0 + JC].bitcast(FP8X4),
-                    rhs_scale=tab2_scale[:, c * JC : (c + 1) * JC],
+                    rhs_scale=tab2_scale[TAB2_ROW:P, c * JC : (c + 1) * JC],
                     start=True,
                     stop=True,
                 )
             return bank
 
-        grouped00 = held([P, PASS * PACK], BF16, "wa_grouped00")
-        for raw, (lo, hi) in zip(raw00, halves):
-            round_wa(raw[:], grouped00, lo, hi)
-        quantise_wa(0, 0, [grouped00], held)
-        hb0_banks = [project_b(0, c, c) for c in range(CHUNKS)]
-        hb0 = [copy_out(hb0_banks[c], held, "hb0_%d" % c) for c in range(4)]
-        pairs = [gather_tab(lo, lo + TAB_STEP, placed(PAIRS_AT + 4 * lo)) for lo in (0, TAB_STEP)]
-        for n in range(2):
-            part_tab(n * TAB_STEP, (n + 1) * TAB_STEP, pairs[n], held)
-        pairs = [gather_tab(HALF + lo, HALF + lo + TAB_STEP, placed(PAIRS_AT + 4 * lo)) for lo in (0, TAB_STEP)]
-        part_tab(HALF, HALF + TAB_STEP, pairs[0], held)
-        grouped01 = held([P, PASS * PACK], BF16, "wa_grouped01")
-        for raw, (lo, hi) in zip(raw01, cuts01):
-            round_wa(raw[:], grouped01, lo, hi)
-        quantise_wa(0, 1, [grouped01], held)
-        part_tab(HALF + TAB_STEP, J, pairs[1], placed(LAST01_AT + EDGE))
-        hb0.append(copy_out(hb0_banks[4], placed(HB0_4_AT), "hb0_4"))
-        last_hb0 = placed(LAST01_AT + CHUNK_BYTES - EDGE)([P, 3, JC, PACK], F32, "hb0_last")
-        for c in range(5, CHUNKS):
-            hb0.append(copy_into(hb0_banks[c], last_hb0[:, c - 5]))
-        reorder_wb(nc.gpsimd.tensor_copy, 1, placed(PAIRS_AT + 8 * TAB_STEP - EDGE))
-        reorder_wb_scale(nc.gpsimd, 1, placed(PAIRS_AT + 4 * TAB_STEP))
+        def copy_out(bank, kept):
+            nc.scalar.copy(kept, by_query(bank))
+            return kept
 
-        h_bf16, h_chunk = {}, {}
+        grouped00 = new_grouped(0, 0, held)
+        round_on_scalar(raw00, grouped00, 0)
+        reorder_wb_scale(nc.vector, 0, held)
+        reorder_wb(nc.scalar.copy, 0, held)
+        for h in range(2):
+            codes = held([P, HALF], U32, "tab2_codes%d" % h)
+            nc.vector.tensor_copy(codes[:], tab2_win[:].bitcast(U32).indirect(part_of(list2, h * HALF, (h + 1) * HALF)))
+            tab2_codes.append(codes)
+        quantise_wa(0, 0, grouped00, placed(WB0_AT))
+
+        hb_banks = [project_b(0, c) for c in range(CHUNKS)]
+        hb_early = held([P, HB0_EARLY, JC, PACK], F32, "hb0_early")
+        hb = [copy_out(hb_banks[c], hb_early[:, c]) for c in range(HB0_EARLY)]
+
+        steps = J // TAB_STEP
+        pairs = [gather_tab(0)]
+        for n in range(steps):
+            if n + 1 < steps:
+                pairs.append(gather_tab(n + 1))
+            part_tab(n, pairs[n])
+
+        grouped01 = new_grouped(0, 1, placed(GROUPED01_AT))
+        round_on_vector(raw01, grouped01, SHARE01)
+        round_on_scalar(raw01, grouped01, SHARE01)
+        quantise_wa(0, 1, grouped01, held)
+        hb_late = placed(RAW01_AT)([P, CHUNKS - HB0_EARLY, JC, PACK], F32, "hb0_late")
+        for c in range(HB0_EARLY, CHUNKS):
+            hb.append(copy_out(hb_banks[c], hb_late[:, c - HB0_EARLY]))
+        reorder_wb(nc.gpsimd.tensor_copy, 1, placed(GROUPED01_AT))
+        reorder_wb_scale(nc.gpsimd, 1, placed(GROUPED01_AT + 2 * KIB))
+
+        h_bf16 = {}
 
         def new_h(b, lo, hi, make):
-            h_bf16[b, lo] = make([P, hi - lo, PACK], BF16, "h_bf16_%d_%d" % (b, lo))
+            tile = make([P, hi - lo, PACK], BF16, "h_bf16_%d_%d" % (b, lo))
             for j0 in range(lo, hi, JC):
-                h_chunk[b, j0 // JC] = h_bf16[b, lo][:, j0 - lo : j0 - lo + JC, :]
+                h_bf16[b, j0] = (tile, lo)
 
-        def join(b, c, bank, kept):
-            nc.vector.tensor_tensor(h_chunk[b, c], by_query(bank), kept, MULT)
-
-        def join0(c):
-            join(0, c, project_a(0, c, c), hb0[c])
+        def h_cols(b, lo, hi):
+            tile, at = h_bf16[b, lo]
+            return tile[:, lo - at : hi - at, :]
 
         h_scale = [held([P, J], U8, "h_scale%d" % b) for b in range(2)]
         h_codes = {}
 
-        def new_codes(b, lo, hi, make):
-            codes = make([P, hi - lo], U32, "h_codes%d_%d" % (b, lo))
-            for j0 in range(lo, hi, JC):
-                h_codes[b, j0] = (codes, lo)
+        def join(b, c, bank, kept):
+            nc.vector.tensor_tensor(h_cols(b, c * JC, (c + 1) * JC), by_query(bank), kept, MULT)
 
         def quantise_h(b, lo, hi):
-            codes, at = h_codes[b, lo]
             nc.vector.quantize_mx(
-                out=codes[:, lo - at : hi - at].bitcast(FP8X4),
+                out=h_codes[b][:, lo:hi].bitcast(FP8X4),
                 scales=h_scale[b][:, lo:hi],
-                in_=h_bf16[b, lo][:].rearrange("p j t -> p (j t)"),
+                in_=h_cols(b, lo, hi).rearrange("p j t -> p (j t)"),
             )
 
-        new_h(0, 0, 512, held)
-        new_h(0, 512, 768, held)
-        def round_share(raw, grouped, share):
-            src = raw[:, :, 0 : PACK * share].rearrange("p i (m h l) -> p h m i l", h=2, l=2)
-            dst = grouped[:].rearrange("p (h l m i) -> p h m i l", h=2, l=2, i=PACK)
-            nc.vector.tensor_copy(dst[:, :, 0:share], src)
+        split = JOINS_BEFORE_WA10 * JC
+        new_h(0, 0, split, held)
+        for c in range(JOINS_BEFORE_WA10):
+            join(0, c, project_a(0, c), hb[c])
 
-        for c in range(AFTER10):
-            join0(c)
-        grouped10 = held([P, PASS * PACK], BF16, "wa_grouped10")
-        round_wa(raw10[:], grouped10, 0, P)
-        quantise_wa(1, 0, [grouped10], placed(HB0_4_AT))
-        grouped11 = placed(RAW10_AT + 3 * CHUNK_BYTES)([P, PASS * PACK], BF16, "wa_grouped11")
-        round_share(raw11, grouped11, SHARE11)
-        round_wa(raw11[:, :, PACK * SHARE11 : PASS], grouped11, SHARE11, P)
-        new_h(0, 768, 1024, placed(RAW10_AT))
-        for c in range(AFTER10, CHUNKS):
-            join0(c)
-        quantise_wa(1, 1, [grouped11], held)
-        new_codes(0, 0, J, placed(RAW11_AT))
-        for lo, hi in H0_RANGES:
+        grouped10 = new_grouped(1, 0, held)
+        round_on_scalar(raw10, grouped10, 0)
+        quantise_wa(1, 0, grouped10, held)
+        grouped11 = new_grouped(1, 1, held)
+        round_on_vector(raw11, grouped11, SHARE11)
+        round_on_scalar(raw11, grouped11, SHARE11)
+        new_h(0, split, J, placed(RAW10_AT))
+        for c in range(JOINS_BEFORE_WA10, CHUNKS):
+            join(0, c, project_a(0, c), hb[c])
+        quantise_wa(1, 1, grouped11, held)
+        new_h(1, 0, J, held)
+        h_codes[0] = placed(RAW11_AT)([P, J], U32, "h_codes0")
+        h_codes[1] = held([P, J], U32, "h_codes1")
+        for lo, hi in ((0, HALF), (HALF, split), (split, J)):
             quantise_h(0, lo, hi)
-        new_codes(1, 0, J, held)
+
+        hb_banks = [project_b(1, c) for c in range(CHUNKS)]
+        hb1 = placed(RAW11_AT + 4 * KIB)([P, CHUNKS, JC, PACK], F32, "hb1")
+        hb = [copy_out(hb_banks[c], hb1[:, c]) for c in range(CHUNKS)]
+        ha = [project_a(1, c) for c in range(HA1_LEAD)]
 
         out_rows = out.rearrange("(u p) j -> p u j", p=P)
 
-        def finish(lo, hi, n):
-            bank = bank_tile(n, [P, 2, hi - lo])
+        def finish(n):
+            lo, hi = SCORE_RANGES[n]
+            bank = bank_tile(SCORE_BANKS[n], [P, 2, hi - lo])
             for b in range(2):
-                codes, at = h_codes[b, lo]
                 for u in range(2):
                     cols = slice(u * P, (u + 1) * P)
                     nc.tensor.matmul_mx(
                         out=bank[:, u, :],
                         lhsT=en_codes[:, b, cols].bitcast(FP8X4),
                         lhsT_scale=en_scale[:, b, cols],
-                        rhs=codes[:, lo - at : hi - at].bitcast(FP8X4),
+                        rhs=h_codes[b][:, lo:hi].bitcast(FP8X4),
                         rhs_scale=h_scale[b][:, lo:hi],
                         start=(b == 0 and u == 0),
                         stop=(b == 1 and u == 1),
                     )
-            result = held([P, 2, hi - lo], F32, "result%d" % lo)
+            result = held([P, 2, hi - lo], F32, "result%d" % n)
             nc.scalar.copy(result[:], bank[:])
             nc.sync.dma_start(out_rows[:, :, lo:hi], result[:])
 
-        for lo, hi in SCORE_RANGES:
-            new_h(1, lo, hi, held)
-        ends = {hi // JC: (n, lo, hi) for n, (lo, hi) in enumerate(SCORE_RANGES)}
-        hb1 = []
-
-        def make_hb1(c):
-            make = placed(RAW10_AT + EDGE + (c + 2) * CHUNK_BYTES) if c < len(HB1_BANKS) else held
-            hb1.append(copy_out(project_b(1, c, HB1_BANKS[c % len(HB1_BANKS)]), make, "hb1_%d" % c))
-
-        ha1 = []
-
-        def make_ha1(c):
-            ha1.append(project_a(1, c, HA1_BANKS[c % len(HA1_BANKS)]))
-
-        for c in range(len(HB1_BANKS)):
-            make_hb1(c)
-        for c in range(HA1_LEAD):
-            make_ha1(c)
-        for c in range(len(HB1_BANKS), HB1_LEAD):
-            make_hb1(c)
-        for c in range(CHUNKS + 2):
+        ends = {hi // JC: n for n, (lo, hi) in enumerate(SCORE_RANGES)}
+        for c in range(CHUNKS + 1):
             if c + HA1_LEAD < CHUNKS:
-                make_ha1(c + HA1_LEAD)
-            if c + HB1_LEAD < CHUNKS:
-                make_hb1(c + HB1_LEAD)
-            if c - 1 in ends:
-                n, lo, hi = ends[c - 1]
-                finish(lo, hi, SCORE_BANKS[n])
+                ha.append(project_a(1, c + HA1_LEAD))
             if c < CHUNKS:
-                join(1, c, ha1[c], hb1[c])
+                join(1, c, ha[c], hb[c])
             if c in ends:
-                quantise_h(1, *ends[c][1:])
+                quantise_h(1, *SCORE_RANGES[ends[c]])
+                finish(ends[c])

@@ -14,6 +14,7 @@ U8 = mybir.dt.uint8
 FP8X4 = mybir.dt.float8_e4m3fn_x4
 FP4X4 = mybir.dt.float4_e2m1fn_x4
 MULT = mybir.AluOpType.mult
+ADD = mybir.AluOpType.add
 
 P = 128
 PACK = 4
@@ -162,6 +163,11 @@ def tile_list_kg_mul_none_kernel(
             dst = grouped[:].rearrange("p (h l m i) -> p h m i l", h=2, l=2, i=PACK)
             nc.vector.tensor_copy(dst[:, :, 0:hi], src[:, :, 0:hi])
 
+        def round_on_gpsimd(raw, grouped, lo, hi):
+            src = raw[:].rearrange("p i (m t) -> p t m i", t=PACK)
+            dst = grouped[:].rearrange("p (t m i) -> p t m i", t=PACK, i=PACK)
+            nc.gpsimd.tensor_scalar(dst[:, :, lo:hi], src[:, :, lo:hi], 1.0, 0.0, MULT, ADD)
+
         wa_codes, wa_scale = {}, {}
 
         def quantise_wa(b, a, grouped, make):
@@ -231,8 +237,8 @@ def tile_list_kg_mul_none_kernel(
             return kept
 
         grouped00 = new_grouped(0, 0, held)
-        round_on_scalar(raw00, grouped00, 0)
-        reorder_wb_scale(nc.vector, 0, held)
+        reorder_wb_scale(nc.gpsimd, 0, held)
+        round_on_gpsimd(raw00, grouped00, 0, GROUPS)
         reorder_wb(nc.scalar.copy, 0, held)
         for h in range(2):
             codes = held([P, HALF], U32, "tab2_codes%d" % h)

@@ -29,20 +29,21 @@ GROUPS = PASS // PACK
 TAB_STEP = 256
 TAB2_ROW = 4
 WB_ROW = 8
-HB0_EARLY = 6
-SHARE01 = 48
-SHARE11 = 40
+HB0_EARLY = 4
+GPSIMD00 = 72
+GPSIMD10 = 72
 SCORE_RANGES = ((0, 256), (256, 512), (512, 768), (768, 896), (896, 1024))
-HB_BANKS = ((0, 1, 2, 3, 4, 5, 6, 7), (6, 7, 2, 3, 4, 5, 0, 1))
-HA_BANKS = ((0, 1, 2, 3, 4, 5, 0, 1), HB_BANKS[1])
+HB_BANKS = ((0, 1, 2, 3, 4, 5, 6, 7), (4, 5, 6, 7, 0, 1, 2, 3))
+HA_BANKS = ((0, 1, 2, 3, 0, 1, 2, 3), HB_BANKS[1])
 SCORE_BANKS = tuple(HB_BANKS[1][c] for c in (0, 2, 4, 5, 6))
 KIB = 1024
 RAW01_AT = 0
-GROUPED01_AT = 8 * KIB
-RAW11_AT = 12 * KIB
-RAW10_AT = 32 * KIB
-WB0_AT = 40 * KIB
-JOINS_BEFORE_WA10 = 6
+GROUPED01_AT = 12 * KIB
+RAW11_AT = 56 * KIB
+WB0_AT = 8 * KIB
+RAW10_GPSIMD_AT = 20 * KIB
+RAW00_GPSIMD_AT = 32 * KIB
+RAW00_AT = 40 * KIB
 HA1_LEAD = 3
 
 
@@ -71,21 +72,18 @@ def tile_list_kg_mul_none_kernel(
         tab_scale_win = held([P, T], U8, "tab_scale_win")
         tab2_scale_win = held([P, T], U8, "tab2_scale_win")
         wb_scale_raw = held([P, R], U8, "wb_scale_raw")
-        tab2_scale = held([P, J], U8, "tab2_scale")
         tab_scale = [held([P, J], U8, "tab_scale%d" % a) for a in range(2)]
         en_scale = held([P, 2, N], U8, "en_scale")
-        nc.vector.memset(tab2_scale_win[0:96, :].bitcast(I32), 0)
-        nc.vector.memset(tab2_scale_win[96:112, :].bitcast(I32), 0)
-        nc.vector.memset(tab_scale_win[0:96, :].bitcast(I32), 0)
-        nc.gpsimd.memset(wb_scale_raw[:].bitcast(I32), 0)
-        nc.gpsimd.memset(tab2_scale[:].bitcast(I32), 0)
+        nc.gpsimd.memset(tab2_scale_win[:].bitcast(I32), 0)
+        nc.vector.memset(wb_scale_raw[:].bitcast(I32), 0)
+        nc.vector.memset(tab_scale_win[0 : P - 2 * ROWS, :].bitcast(I32), 0)
         for a in range(2):
-            nc.gpsimd.memset(tab_scale[a][:].bitcast(I32), 0)
+            nc.vector.memset(tab_scale[a][:].bitcast(I32), 0)
         nc.gpsimd.memset(en_scale[:].bitcast(I32), 0)
 
-        def load_wa(b, a, make):
-            raw = make([P, PACK, PASS], F32, "wa_raw%d%d" % (b, a))
-            rows = wa[a * PASS : (a + 1) * PASS, b * PASS : (b + 1) * PASS]
+        def load_wa(b, a, lo, hi, make):
+            raw = make([P, PACK, PACK * (hi - lo)], F32, "wa_raw%d%d_%d" % (b, a, lo))
+            rows = wa[a * PASS : (a + 1) * PASS, b * PASS + PACK * lo : b * PASS + PACK * hi]
             nc.sync.dma_start(raw[:], rows.rearrange("(p i) c -> p i c", i=PACK))
             return raw
 
@@ -94,48 +92,27 @@ def tile_list_kg_mul_none_kernel(
             nc.sync.dma_start(raw[:], as_words(wb_words[0])[:, b * PASS : (b + 1) * PASS])
             return raw
 
-        def move_rows(plane, first_row, picked, at):
+        def load_scale_rows(plane, first_row, step, rows):
             for e in range(4):
-                nc.sync.dma_start(
-                    plane[first_row + e : P : QUAD, :].bitcast(I32), picked[at + e : at + ROWS : 4, :].bitcast(I32)
-                )
+                nc.sync.dma_start(plane[first_row + e : P : step].bitcast(I32), rows[e].bitcast(I32))
 
         def part_of(lst, lo, hi):
             return lst[:, lo // LIST_GROUP : hi // LIST_GROUP]
 
         nc.sync.dma_start(list2[:], offs2)
-        nc.sync.dma_start(tab2_scale_win[P - ROWS : P, :].bitcast(I32), tab2_scales[0].bitcast(I32))
         nc.sync.dma_start(list1[:], offs)
+        load_scale_rows(tab2_scale_win, TAB2_ROW, QUAD, tab2_scales[0].rearrange("(q e) t -> e q t", e=4))
+        tab2_win = held([P, T], I32, "tab2_win")
+        nc.sync.dma_start(tab2_win[:], as_words(tab2_words[0]))
         nc.sync.dma_start(
             tab_scale_win[P - 2 * ROWS : P, :].bitcast(I32), tab_scales.rearrange("a g t -> (a g) t").bitcast(I32)
         )
-        raw00 = load_wa(0, 0, held)
-        wb_scale_rows = wb_scales[0].rearrange("(q e) r -> e q r", e=4)
-        for e in range(4):
-            nc.sync.dma_start(wb_scale_raw[WB_ROW + e : P : QUAD, :].bitcast(I32), wb_scale_rows[e].bitcast(I32))
-        tab2_win = held([P, T], I32, "tab2_win")
-        nc.sync.dma_start(tab2_win[:], as_words(tab2_words[0]))
         wb_raw = [load_wb(0, placed(WB0_AT))]
-
-        tab2_scale_picked = held([P, J], U8, "tab2_scale_picked")
-        nc.vector.tensor_copy(tab2_scale_picked[:], tab2_scale_win[:].indirect(list2[:]))
-        tab_scale_picked = held([P, J], U8, "tab_scale_picked")
-        nc.vector.tensor_copy(tab_scale_picked[:], tab_scale_win[:].indirect(list1[:]))
-
-        move_rows(tab2_scale, TAB2_ROW, tab2_scale_picked, P - ROWS)
+        load_scale_rows(wb_scale_raw, WB_ROW, QUAD, wb_scales[0].rearrange("(q e) r -> e q r", e=4))
+        raw00 = [load_wa(0, 0, 0, GPSIMD00, placed(RAW00_GPSIMD_AT)), load_wa(0, 0, GPSIMD00, GROUPS, placed(RAW00_AT))]
         tab_win = held([P, T], I32, "tab_win")
         nc.sync.dma_start(tab_win[:], as_words(tab_words[0]))
-        move_rows(tab_scale[0], 0, tab_scale_picked, P - 2 * ROWS)
-        raw01 = load_wa(0, 1, placed(RAW01_AT))
-        move_rows(tab_scale[1], 0, tab_scale_picked, P - ROWS)
-        wb_raw.append(load_wb(1, held))
-        raw10 = load_wa(1, 0, placed(RAW10_AT))
-        raw11 = load_wa(1, 1, placed(RAW11_AT))
-        en_codes = held([P, 2, N], I32, "en_codes")
-        nc.sync.dma_start(en_codes[:], en_words.rearrange("a p n i -> p a (n i)").bitcast(I32))
-        en_scale_rows = en_scales.rearrange("a (q e) n -> e q a n", e=4)
-        for e in range(4):
-            nc.sync.dma_start(en_scale[e:P:QUAD, :, :].bitcast(I32), en_scale_rows[e].bitcast(I32))
+        raw01 = [load_wa(0, 1, 0, GROUPS // 2, held)]
 
         wb_codes, wb_scale = {}, {}
 
@@ -146,6 +123,36 @@ def tile_list_kg_mul_none_kernel(
                 wb_raw[b][:].bitcast(U32).rearrange("p (c m t) -> p c t m", t=PACK, m=4),
             )
 
+        tab2_codes = []
+
+        def gather_tab2(h, make):
+            codes = make([P, HALF], U32, "tab2_codes%d" % h)
+            nc.vector.tensor_copy(codes[:], tab2_win[:].bitcast(U32).indirect(part_of(list2, h * HALF, (h + 1) * HALF)))
+            tab2_codes.append(codes)
+
+        tab2_scale = held([P, J], U8, "tab2_scale")
+        nc.vector.tensor_copy(tab2_scale[:], tab2_scale_win[:].indirect(list2[:]))
+        gather_tab2(0, held)
+        tab_scale_picked = placed(GROUPED01_AT - KIB)([P, J], U8, "tab_scale_picked")
+        nc.vector.tensor_copy(tab_scale_picked[:], tab_scale_win[:].indirect(list1[:]))
+        reorder_wb(nc.scalar.copy, 0, held)
+        gather_tab2(1, placed(WB0_AT))
+
+        def move_tab_rows(a):
+            first = P - 2 * ROWS + a * ROWS
+            load_scale_rows(tab_scale[a], 0, QUAD, [tab_scale_picked[first + e : first + ROWS : 4, :] for e in range(4)])
+
+        move_tab_rows(0)
+        raw01.append(load_wa(0, 1, GROUPS // 2, GROUPS, placed(RAW01_AT)))
+        wb_raw.append(load_wb(1, placed(GROUPED01_AT + 5 * KIB)))
+        raw10 = [load_wa(1, 0, 0, GPSIMD10, placed(RAW10_GPSIMD_AT))]
+        move_tab_rows(1)
+        raw10.append(load_wa(1, 0, GPSIMD10, GROUPS, held))
+        raw11 = load_wa(1, 1, 0, GROUPS, placed(RAW11_AT))
+        en_codes = held([P, 2, N], I32, "en_codes")
+        nc.sync.dma_start(en_codes[:], en_words.rearrange("a p n i -> p a (n i)").bitcast(I32))
+        load_scale_rows(en_scale, 0, QUAD, en_scales.rearrange("a (q e) n -> e q a n", e=4))
+
         def reorder_wb_scale(engine, b, make):
             wb_scale[b] = make([P, PASS], U8, "wb_scale%d" % b)
             engine.tensor_copy(
@@ -153,15 +160,10 @@ def tile_list_kg_mul_none_kernel(
                 wb_scale_raw[:, b * PASS : (b + 1) * PASS].rearrange("p (c m t) -> p c t m", t=PACK, m=16),
             )
 
-        def round_on_scalar(raw, grouped, lo):
+        def round_on_scalar(raw, at, grouped, lo, hi):
             src = raw[:].rearrange("p i (m t) -> p m i t", t=PACK)
             dst = grouped[:].rearrange("p (t m i) -> p m i t", t=PACK, i=PACK)
-            nc.scalar.copy(dst[:, lo:GROUPS], src[:, lo:GROUPS])
-
-        def round_on_vector(raw, grouped, hi):
-            src = raw[:].rearrange("p i (m h l) -> p h m i l", h=2, l=2)
-            dst = grouped[:].rearrange("p (h l m i) -> p h m i l", h=2, l=2, i=PACK)
-            nc.vector.tensor_copy(dst[:, :, 0:hi], src[:, :, 0:hi])
+            nc.scalar.copy(dst[:, lo:hi], src[:, lo - at : hi - at])
 
         def round_on_gpsimd(raw, grouped, lo, hi):
             src = raw[:].rearrange("p i (m t) -> p t m i", t=PACK)
@@ -180,14 +182,14 @@ def tile_list_kg_mul_none_kernel(
 
         tab_codes = {}
 
-        def gather_tab(n):
-            pairs = held([P, TAB_STEP], U32, "tab_pairs%d" % n)
+        def gather_tab(n, make):
+            pairs = make([P, TAB_STEP], U32, "tab_pairs%d" % n)
             lo = n * TAB_STEP
             nc.vector.tensor_copy(pairs[:], tab_win[:].bitcast(U32).indirect(part_of(list1, lo, lo + TAB_STEP)))
             return pairs
 
-        def part_tab(n, pairs):
-            parted = held([P, 2, 2 * TAB_STEP], U8, "tab_codes%d" % n)
+        def part_tab(n, pairs, make):
+            parted = make([P, 2, 2 * TAB_STEP], U8, "tab_codes%d" % n)
             nc.vector.tensor_copy(parted[:].bitcast(U16), pairs[:].bitcast(U16).rearrange("p (j d) -> p d j", d=2))
             for j0 in range(0, TAB_STEP, JC):
                 tab_codes[(n * TAB_STEP + j0) // JC] = parted[:, :, 2 * j0 : 2 * (j0 + JC)]
@@ -214,8 +216,6 @@ def tile_list_kg_mul_none_kernel(
                     )
             return bank
 
-        tab2_codes = []
-
         def project_b(b, c):
             bank = bank_tile(HB_BANKS[b][c], [P, PACK, JC])
             h, j0 = divmod(c * JC, HALF)
@@ -236,36 +236,34 @@ def tile_list_kg_mul_none_kernel(
             nc.scalar.copy(kept, by_query(bank))
             return kept
 
+        for b in range(2):
+            reorder_wb_scale(nc.gpsimd, b, held)
         grouped00 = new_grouped(0, 0, held)
-        reorder_wb_scale(nc.gpsimd, 0, held)
-        round_on_gpsimd(raw00, grouped00, 0, GROUPS)
-        reorder_wb(nc.scalar.copy, 0, held)
-        for h in range(2):
-            codes = held([P, HALF], U32, "tab2_codes%d" % h)
-            nc.vector.tensor_copy(codes[:], tab2_win[:].bitcast(U32).indirect(part_of(list2, h * HALF, (h + 1) * HALF)))
-            tab2_codes.append(codes)
-        quantise_wa(0, 0, grouped00, placed(WB0_AT))
+        round_on_gpsimd(raw00[0], grouped00, 0, GPSIMD00)
+        round_on_scalar(raw00[1], GPSIMD00, grouped00, GPSIMD00, GROUPS)
 
         hb_banks = [project_b(0, c) for c in range(CHUNKS)]
-        hb_early = held([P, HB0_EARLY, JC, PACK], F32, "hb0_early")
+        hb_early = placed(RAW00_AT)([P, HB0_EARLY, JC, PACK], F32, "hb0_early")
         hb = [copy_out(hb_banks[c], hb_early[:, c]) for c in range(HB0_EARLY)]
 
-        steps = J // TAB_STEP
-        pairs = [gather_tab(0)]
-        for n in range(steps):
-            if n + 1 < steps:
-                pairs.append(gather_tab(n + 1))
-            part_tab(n, pairs[n])
+        pairs = [gather_tab(0, held)]
+        quantise_wa(0, 0, grouped00, held)
+        part_tab(0, pairs[0], placed(RAW00_GPSIMD_AT))
+        pairs.append(gather_tab(1, placed(RAW00_GPSIMD_AT + KIB)))
+        pairs.append(gather_tab(2, placed(RAW00_GPSIMD_AT + 2 * KIB)))
+        part_tab(1, pairs[1], held)
+        pairs.append(gather_tab(3, placed(RAW00_GPSIMD_AT + 3 * KIB)))
+        part_tab(2, pairs[2], held)
+        part_tab(3, pairs[3], held)
 
         grouped01 = new_grouped(0, 1, placed(GROUPED01_AT))
-        round_on_vector(raw01, grouped01, SHARE01)
-        round_on_scalar(raw01, grouped01, SHARE01)
+        round_on_scalar(raw01[0], 0, grouped01, 0, GROUPS // 2)
+        round_on_scalar(raw01[1], GROUPS // 2, grouped01, GROUPS // 2, GROUPS)
         quantise_wa(0, 1, grouped01, held)
         hb_late = placed(RAW01_AT)([P, CHUNKS - HB0_EARLY, JC, PACK], F32, "hb0_late")
         for c in range(HB0_EARLY, CHUNKS):
             hb.append(copy_out(hb_banks[c], hb_late[:, c - HB0_EARLY]))
-        reorder_wb(nc.gpsimd.tensor_copy, 1, placed(GROUPED01_AT))
-        reorder_wb_scale(nc.gpsimd, 1, placed(GROUPED01_AT + 2 * KIB))
+        reorder_wb(nc.gpsimd.tensor_copy, 1, placed(GROUPED01_AT - KIB))
 
         h_bf16 = {}
 
@@ -278,7 +276,7 @@ def tile_list_kg_mul_none_kernel(
             tile, at = h_bf16[b, lo]
             return tile[:, lo - at : hi - at, :]
 
-        h_scale = [held([P, J], U8, "h_scale%d" % b) for b in range(2)]
+        h_scale = {1: held([P, J], U8, "h_scale1")}
         h_codes = {}
 
         def join(b, c, bank, kept):
@@ -291,28 +289,25 @@ def tile_list_kg_mul_none_kernel(
                 in_=h_cols(b, lo, hi).rearrange("p j t -> p (j t)"),
             )
 
-        split = JOINS_BEFORE_WA10 * JC
-        new_h(0, 0, split, held)
-        for c in range(JOINS_BEFORE_WA10):
+        new_h(0, 0, J, held)
+        for c in range(CHUNKS):
             join(0, c, project_a(0, c), hb[c])
 
-        grouped10 = new_grouped(1, 0, held)
-        round_on_scalar(raw10, grouped10, 0)
-        quantise_wa(1, 0, grouped10, held)
+        grouped10 = new_grouped(1, 0, placed(GROUPED01_AT + 2 * KIB))
+        round_on_gpsimd(raw10[0], grouped10, 0, GPSIMD10)
+        round_on_scalar(raw10[1], GPSIMD10, grouped10, GPSIMD10, GROUPS)
+        hb_banks = [project_b(1, c) for c in range(CHUNKS)]
         grouped11 = new_grouped(1, 1, held)
-        round_on_vector(raw11, grouped11, SHARE11)
-        round_on_scalar(raw11, grouped11, SHARE11)
-        new_h(0, split, J, placed(RAW10_AT))
-        for c in range(JOINS_BEFORE_WA10, CHUNKS):
-            join(0, c, project_a(0, c), hb[c])
-        quantise_wa(1, 1, grouped11, held)
+        round_on_scalar(raw11, 0, grouped11, 0, GROUPS)
+        quantise_wa(1, 0, grouped10, held)
+        quantise_wa(1, 1, grouped11, placed(RAW10_GPSIMD_AT))
         new_h(1, 0, J, held)
+        h_scale[0] = placed(RAW10_GPSIMD_AT + 2 * KIB)([P, J], U8, "h_scale0")
         h_codes[0] = placed(RAW11_AT)([P, J], U32, "h_codes0")
         h_codes[1] = held([P, J], U32, "h_codes1")
-        for lo, hi in ((0, HALF), (HALF, split), (split, J)):
-            quantise_h(0, lo, hi)
+        for lo in range(0, J, HALF):
+            quantise_h(0, lo, lo + HALF)
 
-        hb_banks = [project_b(1, c) for c in range(CHUNKS)]
         hb1 = placed(RAW11_AT + 4 * KIB)([P, CHUNKS, JC, PACK], F32, "hb1")
         hb = [copy_out(hb_banks[c], hb1[:, c]) for c in range(CHUNKS)]
         ha = [project_a(1, c) for c in range(HA1_LEAD)]

@@ -31,7 +31,8 @@ TAB2_ROW = 4
 WB_ROW = 8
 HB0_EARLY = 4
 GPSIMD00 = 72
-GPSIMD10 = 72
+GPSIMD10 = 32
+GPSIMD11 = 56
 SCORE_RANGES = ((0, 256), (256, 512), (512, 768), (768, 896), (896, 1024))
 HB_BANKS = ((0, 1, 2, 3, 4, 5, 6, 7), (4, 5, 6, 7, 0, 1, 2, 3))
 HA_BANKS = ((0, 1, 2, 3, 0, 1, 2, 3), HB_BANKS[1])
@@ -41,7 +42,7 @@ RAW01_AT = 0
 GROUPED01_AT = 12 * KIB
 RAW11_AT = 56 * KIB
 WB0_AT = 8 * KIB
-RAW10_GPSIMD_AT = 20 * KIB
+RAW11_GPSIMD_AT = 20 * KIB
 RAW00_GPSIMD_AT = 32 * KIB
 RAW00_AT = 40 * KIB
 HA1_LEAD = 3
@@ -145,10 +146,10 @@ def tile_list_kg_mul_none_kernel(
         move_tab_rows(0)
         raw01.append(load_wa(0, 1, GROUPS // 2, GROUPS, placed(RAW01_AT)))
         wb_raw.append(load_wb(1, placed(GROUPED01_AT + 5 * KIB)))
-        raw10 = [load_wa(1, 0, 0, GPSIMD10, placed(RAW10_GPSIMD_AT))]
+        raw10 = [load_wa(1, 0, 0, GPSIMD10, held)]
         move_tab_rows(1)
         raw10.append(load_wa(1, 0, GPSIMD10, GROUPS, held))
-        raw11 = load_wa(1, 1, 0, GROUPS, placed(RAW11_AT))
+        raw11 = [load_wa(1, 1, 0, GPSIMD11, placed(RAW11_GPSIMD_AT)), load_wa(1, 1, GPSIMD11, GROUPS, placed(RAW11_AT))]
         en_codes = held([P, 2, N], I32, "en_codes")
         nc.sync.dma_start(en_codes[:], en_words.rearrange("a p n i -> p a (n i)").bitcast(I32))
         load_scale_rows(en_scale, 0, QUAD, en_scales.rearrange("a (q e) n -> e q a n", e=4))
@@ -298,11 +299,12 @@ def tile_list_kg_mul_none_kernel(
         round_on_scalar(raw10[1], GPSIMD10, grouped10, GPSIMD10, GROUPS)
         hb_banks = [project_b(1, c) for c in range(CHUNKS)]
         grouped11 = new_grouped(1, 1, held)
-        round_on_scalar(raw11, 0, grouped11, 0, GROUPS)
-        quantise_wa(1, 0, grouped10, held)
-        quantise_wa(1, 1, grouped11, placed(RAW10_GPSIMD_AT))
+        round_on_gpsimd(raw11[0], grouped11, 0, GPSIMD11)
+        round_on_scalar(raw11[1], GPSIMD11, grouped11, GPSIMD11, GROUPS)
+        quantise_wa(1, 0, grouped10, placed(RAW11_GPSIMD_AT))
+        quantise_wa(1, 1, grouped11, held)
         new_h(1, 0, J, held)
-        h_scale[0] = placed(RAW10_GPSIMD_AT + 2 * KIB)([P, J], U8, "h_scale0")
+        h_scale[0] = placed(RAW11_GPSIMD_AT + 2 * KIB)([P, J], U8, "h_scale0")
         h_codes[0] = placed(RAW11_AT)([P, J], U32, "h_codes0")
         h_codes[1] = held([P, J], U32, "h_codes1")
         for lo in range(0, J, HALF):

@@ -30,18 +30,19 @@ TAB_STEP = 256
 TAB2_ROW = 4
 WB_ROW = 8
 HB0_EARLY = 4
-GPSIMD00 = 72
-GPSIMD10 = 32
-GPSIMD11 = 56
+GPSIMD00 = 80
+GPSIMD10 = 16
+GPSIMD11 = 48
 SCORE_RANGES = ((0, 256), (256, 512), (512, 768), (768, 896), (896, 1024))
 HB_BANKS = ((0, 1, 2, 3, 4, 5, 6, 7), (4, 5, 6, 7, 0, 1, 2, 3))
 HA_BANKS = ((0, 1, 2, 3, 0, 1, 2, 3), HB_BANKS[1])
 SCORE_BANKS = tuple(HB_BANKS[1][c] for c in (0, 2, 4, 5, 6))
+STORE_FROM = {512: 0, 768: 512, 896: 768, 1024: 896}
 KIB = 1024
 RAW01_AT = 0
 GROUPED01_AT = 12 * KIB
 RAW11_AT = 56 * KIB
-WB0_AT = 8 * KIB
+WB0_AT = 80 * KIB
 RAW11_GPSIMD_AT = 20 * KIB
 RAW00_GPSIMD_AT = 32 * KIB
 RAW00_AT = 40 * KIB
@@ -134,7 +135,7 @@ def tile_list_kg_mul_none_kernel(
         tab2_scale = held([P, J], U8, "tab2_scale")
         nc.vector.tensor_copy(tab2_scale[:], tab2_scale_win[:].indirect(list2[:]))
         gather_tab2(0, held)
-        tab_scale_picked = placed(GROUPED01_AT - KIB)([P, J], U8, "tab_scale_picked")
+        tab_scale_picked = placed(RAW00_GPSIMD_AT + 5 * KIB)([P, J], U8, "tab_scale_picked")
         nc.vector.tensor_copy(tab_scale_picked[:], tab_scale_win[:].indirect(list1[:]))
         reorder_wb(nc.scalar.copy, 0, held)
         gather_tab2(1, placed(WB0_AT))
@@ -183,17 +184,16 @@ def tile_list_kg_mul_none_kernel(
 
         tab_codes = {}
 
-        def gather_tab(n, make):
-            pairs = make([P, TAB_STEP], U32, "tab_pairs%d" % n)
-            lo = n * TAB_STEP
-            nc.vector.tensor_copy(pairs[:], tab_win[:].bitcast(U32).indirect(part_of(list1, lo, lo + TAB_STEP)))
+        def gather_tab(lo, hi, make):
+            pairs = make([P, hi - lo], U32, "tab_pairs%d" % lo)
+            nc.vector.tensor_copy(pairs[:], tab_win[:].bitcast(U32).indirect(part_of(list1, lo, hi)))
             return pairs
 
-        def part_tab(n, pairs, make):
-            parted = make([P, 2, 2 * TAB_STEP], U8, "tab_codes%d" % n)
+        def part_tab(lo, hi, pairs, make):
+            parted = make([P, 2, 2 * (hi - lo)], U8, "tab_codes%d" % lo)
             nc.vector.tensor_copy(parted[:].bitcast(U16), pairs[:].bitcast(U16).rearrange("p (j d) -> p d j", d=2))
-            for j0 in range(0, TAB_STEP, JC):
-                tab_codes[(n * TAB_STEP + j0) // JC] = parted[:, :, 2 * j0 : 2 * (j0 + JC)]
+            for j0 in range(lo, hi, JC):
+                tab_codes[j0 // JC] = parted[:, :, 2 * (j0 - lo) : 2 * (j0 - lo + JC)]
 
         def bank_tile(n, shape):
             return psum.tile(shape, F32, name="bank", tag="bank%d" % n)
@@ -247,24 +247,22 @@ def tile_list_kg_mul_none_kernel(
         hb_early = placed(RAW00_AT)([P, HB0_EARLY, JC, PACK], F32, "hb0_early")
         hb = [copy_out(hb_banks[c], hb_early[:, c]) for c in range(HB0_EARLY)]
 
-        pairs = [gather_tab(0, held)]
+        pairs = [gather_tab(0, TAB_STEP, held)]
         quantise_wa(0, 0, grouped00, held)
-        part_tab(0, pairs[0], placed(RAW00_GPSIMD_AT))
-        pairs.append(gather_tab(1, placed(RAW00_GPSIMD_AT + KIB)))
-        pairs.append(gather_tab(2, placed(RAW00_GPSIMD_AT + 2 * KIB)))
-        part_tab(1, pairs[1], held)
-        pairs.append(gather_tab(3, placed(RAW00_GPSIMD_AT + 3 * KIB)))
-        part_tab(2, pairs[2], held)
-        part_tab(3, pairs[3], held)
+        part_tab(0, TAB_STEP, pairs[0], placed(RAW00_GPSIMD_AT))
+        pairs.append(gather_tab(TAB_STEP, HALF, placed(RAW00_GPSIMD_AT + KIB)))
+        pairs.append(gather_tab(HALF, J, placed(RAW00_GPSIMD_AT + 2 * KIB)))
+        part_tab(TAB_STEP, HALF, pairs[1], held)
 
         grouped01 = new_grouped(0, 1, placed(GROUPED01_AT))
         round_on_scalar(raw01[0], 0, grouped01, 0, GROUPS // 2)
         round_on_scalar(raw01[1], GROUPS // 2, grouped01, GROUPS // 2, GROUPS)
         quantise_wa(0, 1, grouped01, held)
-        hb_late = placed(RAW01_AT)([P, CHUNKS - HB0_EARLY, JC, PACK], F32, "hb0_late")
+        part_tab(HALF, J, pairs[2], placed(RAW01_AT))
+        hb_late = placed(RAW01_AT + 2 * KIB)([P, CHUNKS - HB0_EARLY, JC, PACK], F32, "hb0_late")
         for c in range(HB0_EARLY, CHUNKS):
             hb.append(copy_out(hb_banks[c], hb_late[:, c - HB0_EARLY]))
-        reorder_wb(nc.gpsimd.tensor_copy, 1, placed(GROUPED01_AT - KIB))
+        reorder_wb(nc.gpsimd.tensor_copy, 1, placed(RAW00_GPSIMD_AT + 7 * KIB // 2))
 
         h_bf16 = {}
 
@@ -315,6 +313,7 @@ def tile_list_kg_mul_none_kernel(
         ha = [project_a(1, c) for c in range(HA1_LEAD)]
 
         out_rows = out.rearrange("(u p) j -> p u j", p=P)
+        result = held([P, 2, J], F32, "result")
 
         def finish(n):
             lo, hi = SCORE_RANGES[n]
@@ -331,9 +330,9 @@ def tile_list_kg_mul_none_kernel(
                         start=(b == 0 and u == 0),
                         stop=(b == 1 and u == 1),
                     )
-            result = held([P, 2, hi - lo], F32, "result%d" % n)
-            nc.scalar.copy(result[:], bank[:])
-            nc.sync.dma_start(out_rows[:, :, lo:hi], result[:])
+            nc.scalar.copy(result[:, :, lo:hi], bank[:])
+            if hi in STORE_FROM:
+                nc.sync.dma_start(out_rows[:, :, STORE_FROM[hi] : hi], result[:, :, STORE_FROM[hi] : hi])
 
         ends = {hi // JC: n for n, (lo, hi) in enumerate(SCORE_RANGES)}
         for c in range(CHUNKS + 1):

@@ -30,7 +30,7 @@ TAB_STEP = 256
 TAB2_ROW = 4
 WB_ROW = 8
 HB0_EARLY = 4
-GPSIMD00 = 80
+GPSIMD00 = 72
 GPSIMD10 = 16
 GPSIMD11 = 48
 SCORE_RANGES = ((0, 256), (256, 512), (512, 768), (768, 896), (896, 1024))
@@ -40,7 +40,6 @@ SCORE_BANKS = tuple(HB_BANKS[1][c] for c in (0, 2, 4, 5, 6))
 STORE_FROM = {512: 0, 768: 512, 896: 768, 1024: 896}
 KIB = 1024
 RAW01_AT = 0
-GROUPED01_AT = 12 * KIB
 RAW11_AT = 56 * KIB
 WB0_AT = 80 * KIB
 RAW11_GPSIMD_AT = 20 * KIB
@@ -146,10 +145,10 @@ def tile_list_kg_mul_none_kernel(
 
         move_tab_rows(0)
         raw01.append(load_wa(0, 1, GROUPS // 2, GROUPS, placed(RAW01_AT)))
-        wb_raw.append(load_wb(1, placed(GROUPED01_AT + 5 * KIB)))
-        raw10 = [load_wa(1, 0, 0, GPSIMD10, held)]
+        wb_raw.append(load_wb(1, held))
+        raw10 = [load_wa(1, 0, 0, GROUPS // 2, held)]
         move_tab_rows(1)
-        raw10.append(load_wa(1, 0, GPSIMD10, GROUPS, held))
+        raw10.append(load_wa(1, 0, GROUPS // 2, GROUPS, held))
         raw11 = [load_wa(1, 1, 0, GPSIMD11, placed(RAW11_GPSIMD_AT)), load_wa(1, 1, GPSIMD11, GROUPS, placed(RAW11_AT))]
         en_codes = held([P, 2, N], I32, "en_codes")
         nc.sync.dma_start(en_codes[:], en_words.rearrange("a p n i -> p a (n i)").bitcast(I32))
@@ -249,12 +248,12 @@ def tile_list_kg_mul_none_kernel(
 
         pairs = [gather_tab(0, TAB_STEP, held)]
         quantise_wa(0, 0, grouped00, held)
-        part_tab(0, TAB_STEP, pairs[0], placed(RAW00_GPSIMD_AT))
+        part_tab(0, TAB_STEP, pairs[0], placed(RAW00_GPSIMD_AT - KIB // 2))
         pairs.append(gather_tab(TAB_STEP, HALF, placed(RAW00_GPSIMD_AT + KIB)))
-        pairs.append(gather_tab(HALF, J, placed(RAW00_GPSIMD_AT + 2 * KIB)))
+        pairs.append(gather_tab(HALF, J, placed(RAW00_GPSIMD_AT + 3 * KIB)))
         part_tab(TAB_STEP, HALF, pairs[1], held)
 
-        grouped01 = new_grouped(0, 1, placed(GROUPED01_AT))
+        grouped01 = new_grouped(0, 1, held)
         round_on_scalar(raw01[0], 0, grouped01, 0, GROUPS // 2)
         round_on_scalar(raw01[1], GROUPS // 2, grouped01, GROUPS // 2, GROUPS)
         quantise_wa(0, 1, grouped01, held)
@@ -262,7 +261,7 @@ def tile_list_kg_mul_none_kernel(
         hb_late = placed(RAW01_AT + 2 * KIB)([P, CHUNKS - HB0_EARLY, JC, PACK], F32, "hb0_late")
         for c in range(HB0_EARLY, CHUNKS):
             hb.append(copy_out(hb_banks[c], hb_late[:, c - HB0_EARLY]))
-        reorder_wb(nc.gpsimd.tensor_copy, 1, placed(RAW00_GPSIMD_AT + 7 * KIB // 2))
+        reorder_wb(nc.gpsimd.tensor_copy, 1, placed(RAW00_GPSIMD_AT + 9 * KIB // 2))
 
         h_bf16 = {}
 
@@ -292,9 +291,10 @@ def tile_list_kg_mul_none_kernel(
         for c in range(CHUNKS):
             join(0, c, project_a(0, c), hb[c])
 
-        grouped10 = new_grouped(1, 0, placed(GROUPED01_AT + 2 * KIB))
+        grouped10 = new_grouped(1, 0, placed(RAW00_GPSIMD_AT + KIB // 2))
         round_on_gpsimd(raw10[0], grouped10, 0, GPSIMD10)
-        round_on_scalar(raw10[1], GPSIMD10, grouped10, GPSIMD10, GROUPS)
+        round_on_scalar(raw10[0], 0, grouped10, GPSIMD10, GROUPS // 2)
+        round_on_scalar(raw10[1], GROUPS // 2, grouped10, GROUPS // 2, GROUPS)
         hb_banks = [project_b(1, c) for c in range(CHUNKS)]
         grouped11 = new_grouped(1, 1, held)
         round_on_gpsimd(raw11[0], grouped11, 0, GPSIMD11)

@@ -30,9 +30,9 @@ TAB_STEP = 256
 TAB2_ROW = 4
 WB_ROW = 8
 HB0_EARLY = 4
-GPSIMD00 = 72
-GPSIMD10 = 16
-GPSIMD11 = 48
+GPSIMD00 = 80
+GPSIMD10 = 24
+GPSIMD11 = 40
 SCORE_RANGES = ((0, 256), (256, 512), (512, 768), (768, 896), (896, 1024))
 HB_BANKS = ((0, 1, 2, 3, 4, 5, 6, 7), (4, 5, 6, 7, 0, 1, 2, 3))
 HA_BANKS = ((0, 1, 2, 3, 0, 1, 2, 3), HB_BANKS[1])
@@ -40,6 +40,8 @@ SCORE_BANKS = tuple(HB_BANKS[1][c] for c in (0, 2, 4, 5, 6))
 STORE_FROM = {512: 0, 768: 512, 896: 768, 1024: 896}
 KIB = 1024
 RAW01_AT = 0
+RAW01_FIRST_AT = 10 * KIB
+PAIRS0_AT = 16 * KIB
 RAW11_AT = 56 * KIB
 WB0_AT = 80 * KIB
 RAW11_GPSIMD_AT = 20 * KIB
@@ -113,9 +115,9 @@ def tile_list_kg_mul_none_kernel(
         raw00 = [load_wa(0, 0, 0, GPSIMD00, placed(RAW00_GPSIMD_AT)), load_wa(0, 0, GPSIMD00, GROUPS, placed(RAW00_AT))]
         tab_win = held([P, T], I32, "tab_win")
         nc.sync.dma_start(tab_win[:], as_words(tab_words[0]))
-        raw01 = [load_wa(0, 1, 0, GROUPS // 2, held)]
+        raw01 = [load_wa(0, 1, 0, GROUPS // 2, placed(RAW01_FIRST_AT))]
 
-        wb_codes, wb_scale = {}, {}
+        wb_codes = {}
 
         def reorder_wb(copy, b, make):
             wb_codes[b] = make([P, PASS], U32, "wb_codes%d" % b)
@@ -134,7 +136,7 @@ def tile_list_kg_mul_none_kernel(
         tab2_scale = held([P, J], U8, "tab2_scale")
         nc.vector.tensor_copy(tab2_scale[:], tab2_scale_win[:].indirect(list2[:]))
         gather_tab2(0, held)
-        tab_scale_picked = placed(RAW00_GPSIMD_AT + 5 * KIB)([P, J], U8, "tab_scale_picked")
+        tab_scale_picked = placed(RAW00_GPSIMD_AT + 13 * KIB // 2)([P, J], U8, "tab_scale_picked")
         nc.vector.tensor_copy(tab_scale_picked[:], tab_scale_win[:].indirect(list1[:]))
         reorder_wb(nc.scalar.copy, 0, held)
         gather_tab2(1, placed(WB0_AT))
@@ -146,25 +148,34 @@ def tile_list_kg_mul_none_kernel(
         move_tab_rows(0)
         raw01.append(load_wa(0, 1, GROUPS // 2, GROUPS, placed(RAW01_AT)))
         wb_raw.append(load_wb(1, held))
-        raw10 = [load_wa(1, 0, 0, GROUPS // 2, held)]
+        raw10 = [load_wa(1, 0, 0, GPSIMD10, held)]
         move_tab_rows(1)
-        raw10.append(load_wa(1, 0, GROUPS // 2, GROUPS, held))
+        raw10.append(load_wa(1, 0, GPSIMD10, GROUPS, held))
         raw11 = [load_wa(1, 1, 0, GPSIMD11, placed(RAW11_GPSIMD_AT)), load_wa(1, 1, GPSIMD11, GROUPS, placed(RAW11_AT))]
         en_codes = held([P, 2, N], I32, "en_codes")
         nc.sync.dma_start(en_codes[:], en_words.rearrange("a p n i -> p a (n i)").bitcast(I32))
         load_scale_rows(en_scale, 0, QUAD, en_scales.rearrange("a (q e) n -> e q a n", e=4))
 
-        def reorder_wb_scale(engine, b, make):
-            wb_scale[b] = make([P, PASS], U8, "wb_scale%d" % b)
-            engine.tensor_copy(
-                wb_scale[b][:].rearrange("p (t c m) -> p c t m", t=PACK, m=16),
-                wb_scale_raw[:, b * PASS : (b + 1) * PASS].rearrange("p (c m t) -> p c t m", t=PACK, m=16),
-            )
+        wb_scale = held([P, R], U8, "wb_scale")
+        nc.gpsimd.tensor_copy(
+            wb_scale[:].rearrange("p (b t c m) -> p b c t m", b=2, t=PACK, m=16),
+            wb_scale_raw[:].rearrange("p (b c m t) -> p b c t m", b=2, t=PACK, m=16),
+        )
 
         def round_on_scalar(raw, at, grouped, lo, hi):
             src = raw[:].rearrange("p i (m t) -> p m i t", t=PACK)
             dst = grouped[:].rearrange("p (t m i) -> p m i t", t=PACK, i=PACK)
             nc.scalar.copy(dst[:, lo:hi], src[:, lo - at : hi - at])
+
+        def round_pair(copy, raw, at, h, grouped, lo, hi):
+            src = raw[:].rearrange("p i (m h l) -> p h m i l", h=2, l=2)[:, h]
+            dst = grouped[:].rearrange("p (l m i) -> p m i l", l=2, i=PACK)
+            copy(dst[:, lo:hi], src[:, lo - at : hi - at])
+
+        def round_pair_on_gpsimd(raw, h, grouped):
+            src = raw[:].rearrange("p i (m h l) -> p h l m i", h=2, l=2)[:, h]
+            dst = grouped[:].rearrange("p (l m i) -> p l m i", l=2, i=PACK)
+            nc.gpsimd.tensor_scalar(dst[:, :, 0 : GROUPS // 2], src, 1.0, 0.0, MULT, ADD)
 
         def round_on_gpsimd(raw, grouped, lo, hi):
             src = raw[:].rearrange("p i (m t) -> p t m i", t=PACK)
@@ -173,10 +184,15 @@ def tile_list_kg_mul_none_kernel(
 
         wa_codes, wa_scale = {}, {}
 
-        def quantise_wa(b, a, grouped, make):
+        def quantise_wa(b, a, pieces, make):
             wa_codes[b, a] = make([P, PASS], U32, "wa_codes%d%d" % (b, a))
             wa_scale[b, a] = held([P, PASS], U8, "wa_scale%d%d" % (b, a))
-            nc.vector.quantize_mx(out=wa_codes[b, a][:].bitcast(FP8X4), scales=wa_scale[b, a][:], in_=grouped[:])
+            width = PASS // len(pieces)
+            for n, piece in reversed(list(enumerate(pieces))):
+                cols = slice(n * width, (n + 1) * width)
+                nc.vector.quantize_mx(
+                    out=wa_codes[b, a][:, cols].bitcast(FP8X4), scales=wa_scale[b, a][:, cols], in_=piece[:]
+                )
 
         def new_grouped(b, a, make):
             return make([P, PASS * PACK], BF16, "wa_grouped%d%d" % (b, a))
@@ -224,7 +240,7 @@ def tile_list_kg_mul_none_kernel(
                 nc.tensor.matmul_mx(
                     out=bank[:, t, :],
                     lhsT=wb_codes[b][:, cols].bitcast(FP8X4),
-                    lhsT_scale=wb_scale[b][WB_ROW:P, cols],
+                    lhsT_scale=wb_scale[WB_ROW:P, b * PASS + t * P : b * PASS + (t + 1) * P],
                     rhs=tab2_codes[h][:, j0 : j0 + JC].bitcast(FP8X4),
                     rhs_scale=tab2_scale[TAB2_ROW:P, c * JC : (c + 1) * JC],
                     start=True,
@@ -236,8 +252,6 @@ def tile_list_kg_mul_none_kernel(
             nc.scalar.copy(kept, by_query(bank))
             return kept
 
-        for b in range(2):
-            reorder_wb_scale(nc.gpsimd, b, held)
         grouped00 = new_grouped(0, 0, held)
         round_on_gpsimd(raw00[0], grouped00, 0, GPSIMD00)
         round_on_scalar(raw00[1], GPSIMD00, grouped00, GPSIMD00, GROUPS)
@@ -246,22 +260,26 @@ def tile_list_kg_mul_none_kernel(
         hb_early = placed(RAW00_AT)([P, HB0_EARLY, JC, PACK], F32, "hb0_early")
         hb = [copy_out(hb_banks[c], hb_early[:, c]) for c in range(HB0_EARLY)]
 
-        pairs = [gather_tab(0, TAB_STEP, held)]
-        quantise_wa(0, 0, grouped00, held)
-        part_tab(0, TAB_STEP, pairs[0], placed(RAW00_GPSIMD_AT - KIB // 2))
-        pairs.append(gather_tab(TAB_STEP, HALF, placed(RAW00_GPSIMD_AT + KIB)))
-        pairs.append(gather_tab(HALF, J, placed(RAW00_GPSIMD_AT + 3 * KIB)))
+        pairs = [gather_tab(0, TAB_STEP, placed(PAIRS0_AT))]
+        quantise_wa(0, 0, [grouped00], held)
+        part_tab(0, TAB_STEP, pairs[0], placed(RAW00_GPSIMD_AT + KIB // 2))
+        pairs.append(gather_tab(TAB_STEP, HALF, placed(RAW00_GPSIMD_AT + 3 * KIB // 2)))
+        pairs.append(gather_tab(HALF, J, placed(RAW00_GPSIMD_AT + 4 * KIB)))
         part_tab(TAB_STEP, HALF, pairs[1], held)
 
-        grouped01 = new_grouped(0, 1, held)
-        round_on_scalar(raw01[0], 0, grouped01, 0, GROUPS // 2)
-        round_on_scalar(raw01[1], GROUPS // 2, grouped01, GROUPS // 2, GROUPS)
+        grouped01 = [
+            make([P, PASS * PACK // 2], BF16, "wa_grouped01_%d" % h) for h, make in enumerate((placed(RAW00_GPSIMD_AT - 3 * KIB // 2), placed(PAIRS0_AT)))
+        ]
+        round_pair(nc.scalar.copy, raw01[0], 0, 0, grouped01[0], 0, GROUPS // 2)
+        round_pair_on_gpsimd(raw01[0], 1, grouped01[1])
+        round_pair(nc.scalar.copy, raw01[1], GROUPS // 2, 1, grouped01[1], GROUPS // 2, GROUPS)
+        round_pair(nc.scalar.copy, raw01[1], GROUPS // 2, 0, grouped01[0], GROUPS // 2, GROUPS)
         quantise_wa(0, 1, grouped01, held)
-        part_tab(HALF, J, pairs[2], placed(RAW01_AT))
-        hb_late = placed(RAW01_AT + 2 * KIB)([P, CHUNKS - HB0_EARLY, JC, PACK], F32, "hb0_late")
+        part_tab(HALF, J, pairs[2], placed(RAW01_FIRST_AT))
+        hb_late = placed(RAW01_AT)([P, CHUNKS - HB0_EARLY, JC, PACK], F32, "hb0_late")
         for c in range(HB0_EARLY, CHUNKS):
             hb.append(copy_out(hb_banks[c], hb_late[:, c - HB0_EARLY]))
-        reorder_wb(nc.gpsimd.tensor_copy, 1, placed(RAW00_GPSIMD_AT + 9 * KIB // 2))
+        reorder_wb(nc.gpsimd.tensor_copy, 1, placed(RAW00_GPSIMD_AT + 11 * KIB // 2))
 
         h_bf16 = {}
 
@@ -291,16 +309,15 @@ def tile_list_kg_mul_none_kernel(
         for c in range(CHUNKS):
             join(0, c, project_a(0, c), hb[c])
 
-        grouped10 = new_grouped(1, 0, placed(RAW00_GPSIMD_AT + KIB // 2))
+        grouped10 = new_grouped(1, 0, placed(RAW00_GPSIMD_AT + 3 * KIB // 2))
         round_on_gpsimd(raw10[0], grouped10, 0, GPSIMD10)
-        round_on_scalar(raw10[0], 0, grouped10, GPSIMD10, GROUPS // 2)
-        round_on_scalar(raw10[1], GROUPS // 2, grouped10, GROUPS // 2, GROUPS)
+        round_on_scalar(raw10[1], GPSIMD10, grouped10, GPSIMD10, GROUPS)
         hb_banks = [project_b(1, c) for c in range(CHUNKS)]
         grouped11 = new_grouped(1, 1, held)
         round_on_gpsimd(raw11[0], grouped11, 0, GPSIMD11)
         round_on_scalar(raw11[1], GPSIMD11, grouped11, GPSIMD11, GROUPS)
-        quantise_wa(1, 0, grouped10, placed(RAW11_GPSIMD_AT))
-        quantise_wa(1, 1, grouped11, held)
+        quantise_wa(1, 0, [grouped10], placed(RAW11_GPSIMD_AT))
+        quantise_wa(1, 1, [grouped11], held)
         new_h(1, 0, J, held)
         h_scale[0] = placed(RAW11_GPSIMD_AT + 2 * KIB)([P, J], U8, "h_scale0")
         h_codes[0] = placed(RAW11_AT)([P, J], U32, "h_codes0")

@@ -26,27 +26,23 @@ HALF = J // 2
 JC = 128
 CHUNKS = J // JC
 GROUPS = PASS // PACK
-TAB_STEP = 256
 TAB2_ROW = 4
 WB_ROW = 8
 HB0_EARLY = 4
 GPSIMD00 = 80
-GPSIMD10 = 24
-GPSIMD11 = 40
+WA10_CUT = 32
+GPSIMD11 = 56
 SCORE_RANGES = ((0, 256), (256, 512), (512, 768), (768, 896), (896, 1024))
 HB_BANKS = ((0, 1, 2, 3, 4, 5, 6, 7), (4, 5, 6, 7, 0, 1, 2, 3))
 HA_BANKS = ((0, 1, 2, 3, 0, 1, 2, 3), HB_BANKS[1])
 SCORE_BANKS = tuple(HB_BANKS[1][c] for c in (0, 2, 4, 5, 6))
-STORE_FROM = {512: 0, 768: 512, 896: 768, 1024: 896}
+STORE_FROM = {hi: lo for lo, hi in SCORE_RANGES}
 KIB = 1024
 RAW01_AT = 0
-RAW01_FIRST_AT = 10 * KIB
-PAIRS0_AT = 16 * KIB
 RAW11_AT = 56 * KIB
 WB0_AT = 80 * KIB
 RAW11_GPSIMD_AT = 20 * KIB
-RAW00_GPSIMD_AT = 32 * KIB
-RAW00_AT = 40 * KIB
+RAW00_AT = 28 * KIB
 HA1_LEAD = 3
 
 
@@ -112,10 +108,10 @@ def tile_list_kg_mul_none_kernel(
         )
         wb_raw = [load_wb(0, placed(WB0_AT))]
         load_scale_rows(wb_scale_raw, WB_ROW, QUAD, wb_scales[0].rearrange("(q e) r -> e q r", e=4))
-        raw00 = [load_wa(0, 0, 0, GPSIMD00, placed(RAW00_GPSIMD_AT)), load_wa(0, 0, GPSIMD00, GROUPS, placed(RAW00_AT))]
+        raw00 = load_wa(0, 0, 0, GROUPS, placed(RAW00_AT))
         tab_win = held([P, T], I32, "tab_win")
         nc.sync.dma_start(tab_win[:], as_words(tab_words[0]))
-        raw01 = [load_wa(0, 1, 0, GROUPS // 2, placed(RAW01_FIRST_AT))]
+        raw01 = [load_wa(0, 1, 0, GROUPS // 2, held)]
 
         wb_codes = {}
 
@@ -136,7 +132,7 @@ def tile_list_kg_mul_none_kernel(
         tab2_scale = held([P, J], U8, "tab2_scale")
         nc.vector.tensor_copy(tab2_scale[:], tab2_scale_win[:].indirect(list2[:]))
         gather_tab2(0, held)
-        tab_scale_picked = placed(RAW00_GPSIMD_AT + 13 * KIB // 2)([P, J], U8, "tab_scale_picked")
+        tab_scale_picked = placed(RAW00_AT + 17 * KIB // 2)([P, J], U8, "tab_scale_picked")
         nc.vector.tensor_copy(tab_scale_picked[:], tab_scale_win[:].indirect(list1[:]))
         reorder_wb(nc.scalar.copy, 0, held)
         gather_tab2(1, placed(WB0_AT))
@@ -148,9 +144,9 @@ def tile_list_kg_mul_none_kernel(
         move_tab_rows(0)
         raw01.append(load_wa(0, 1, GROUPS // 2, GROUPS, placed(RAW01_AT)))
         wb_raw.append(load_wb(1, held))
-        raw10 = [load_wa(1, 0, 0, GPSIMD10, held)]
+        raw10 = [load_wa(1, 0, 0, WA10_CUT, held)]
         move_tab_rows(1)
-        raw10.append(load_wa(1, 0, GPSIMD10, GROUPS, held))
+        raw10.append(load_wa(1, 0, WA10_CUT, GROUPS, held))
         raw11 = [load_wa(1, 1, 0, GPSIMD11, placed(RAW11_GPSIMD_AT)), load_wa(1, 1, GPSIMD11, GROUPS, placed(RAW11_AT))]
         en_codes = held([P, 2, N], I32, "en_codes")
         nc.sync.dma_start(en_codes[:], en_words.rearrange("a p n i -> p a (n i)").bitcast(I32))
@@ -167,16 +163,6 @@ def tile_list_kg_mul_none_kernel(
             dst = grouped[:].rearrange("p (t m i) -> p m i t", t=PACK, i=PACK)
             nc.scalar.copy(dst[:, lo:hi], src[:, lo - at : hi - at])
 
-        def round_pair(copy, raw, at, h, grouped, lo, hi):
-            src = raw[:].rearrange("p i (m h l) -> p h m i l", h=2, l=2)[:, h]
-            dst = grouped[:].rearrange("p (l m i) -> p m i l", l=2, i=PACK)
-            copy(dst[:, lo:hi], src[:, lo - at : hi - at])
-
-        def round_pair_on_gpsimd(raw, h, grouped):
-            src = raw[:].rearrange("p i (m h l) -> p h l m i", h=2, l=2)[:, h]
-            dst = grouped[:].rearrange("p (l m i) -> p l m i", l=2, i=PACK)
-            nc.gpsimd.tensor_scalar(dst[:, :, 0 : GROUPS // 2], src, 1.0, 0.0, MULT, ADD)
-
         def round_on_gpsimd(raw, grouped, lo, hi):
             src = raw[:].rearrange("p i (m t) -> p t m i", t=PACK)
             dst = grouped[:].rearrange("p (t m i) -> p t m i", t=PACK, i=PACK)
@@ -184,15 +170,10 @@ def tile_list_kg_mul_none_kernel(
 
         wa_codes, wa_scale = {}, {}
 
-        def quantise_wa(b, a, pieces, make):
+        def quantise_wa(b, a, grouped, make):
             wa_codes[b, a] = make([P, PASS], U32, "wa_codes%d%d" % (b, a))
             wa_scale[b, a] = held([P, PASS], U8, "wa_scale%d%d" % (b, a))
-            width = PASS // len(pieces)
-            for n, piece in reversed(list(enumerate(pieces))):
-                cols = slice(n * width, (n + 1) * width)
-                nc.vector.quantize_mx(
-                    out=wa_codes[b, a][:, cols].bitcast(FP8X4), scales=wa_scale[b, a][:, cols], in_=piece[:]
-                )
+            nc.vector.quantize_mx(out=wa_codes[b, a][:].bitcast(FP8X4), scales=wa_scale[b, a][:], in_=grouped[:])
 
         def new_grouped(b, a, make):
             return make([P, PASS * PACK], BF16, "wa_grouped%d%d" % (b, a))
@@ -253,33 +234,27 @@ def tile_list_kg_mul_none_kernel(
             return kept
 
         grouped00 = new_grouped(0, 0, held)
-        round_on_gpsimd(raw00[0], grouped00, 0, GPSIMD00)
-        round_on_scalar(raw00[1], GPSIMD00, grouped00, GPSIMD00, GROUPS)
+        round_on_gpsimd(raw00, grouped00, 0, GPSIMD00)
+        round_on_scalar(raw00, 0, grouped00, GPSIMD00, GROUPS)
 
         hb_banks = [project_b(0, c) for c in range(CHUNKS)]
-        hb_early = placed(RAW00_AT)([P, HB0_EARLY, JC, PACK], F32, "hb0_early")
+        hb_early = held([P, HB0_EARLY, JC, PACK], F32, "hb0_early")
         hb = [copy_out(hb_banks[c], hb_early[:, c]) for c in range(HB0_EARLY)]
 
-        pairs = [gather_tab(0, TAB_STEP, placed(PAIRS0_AT))]
-        quantise_wa(0, 0, [grouped00], held)
-        part_tab(0, TAB_STEP, pairs[0], placed(RAW00_GPSIMD_AT + KIB // 2))
-        pairs.append(gather_tab(TAB_STEP, HALF, placed(RAW00_GPSIMD_AT + 3 * KIB // 2)))
-        pairs.append(gather_tab(HALF, J, placed(RAW00_GPSIMD_AT + 4 * KIB)))
-        part_tab(TAB_STEP, HALF, pairs[1], held)
+        pairs = [gather_tab(0, HALF, held)]
+        quantise_wa(0, 0, grouped00, held)
+        part_tab(0, HALF, pairs[0], placed(RAW00_AT))
+        pairs.append(gather_tab(HALF, J, placed(RAW00_AT + 6 * KIB)))
 
-        grouped01 = [
-            make([P, PASS * PACK // 2], BF16, "wa_grouped01_%d" % h) for h, make in enumerate((placed(RAW00_GPSIMD_AT - 3 * KIB // 2), placed(PAIRS0_AT)))
-        ]
-        round_pair(nc.scalar.copy, raw01[0], 0, 0, grouped01[0], 0, GROUPS // 2)
-        round_pair_on_gpsimd(raw01[0], 1, grouped01[1])
-        round_pair(nc.scalar.copy, raw01[1], GROUPS // 2, 1, grouped01[1], GROUPS // 2, GROUPS)
-        round_pair(nc.scalar.copy, raw01[1], GROUPS // 2, 0, grouped01[0], GROUPS // 2, GROUPS)
-        quantise_wa(0, 1, grouped01, held)
-        part_tab(HALF, J, pairs[2], placed(RAW01_FIRST_AT))
-        hb_late = placed(RAW01_AT)([P, CHUNKS - HB0_EARLY, JC, PACK], F32, "hb0_late")
+        grouped01 = new_grouped(0, 1, held)
+        round_on_scalar(raw01[0], 0, grouped01, 0, GROUPS // 2)
+        round_on_scalar(raw01[1], GROUPS // 2, grouped01, GROUPS // 2, GROUPS)
+        quantise_wa(0, 1, grouped01, placed(RAW00_AT + 2 * KIB))
+        part_tab(HALF, J, pairs[1], placed(RAW01_AT))
+        hb_late = placed(RAW01_AT + 2 * KIB)([P, CHUNKS - HB0_EARLY, JC, PACK], F32, "hb0_late")
         for c in range(HB0_EARLY, CHUNKS):
             hb.append(copy_out(hb_banks[c], hb_late[:, c - HB0_EARLY]))
-        reorder_wb(nc.gpsimd.tensor_copy, 1, placed(RAW00_GPSIMD_AT + 11 * KIB // 2))
+        reorder_wb(nc.gpsimd.tensor_copy, 1, placed(RAW00_AT + 15 * KIB // 2))
 
         h_bf16 = {}
 
@@ -309,15 +284,15 @@ def tile_list_kg_mul_none_kernel(
         for c in range(CHUNKS):
             join(0, c, project_a(0, c), hb[c])
 
-        grouped10 = new_grouped(1, 0, placed(RAW00_GPSIMD_AT + 3 * KIB // 2))
-        round_on_gpsimd(raw10[0], grouped10, 0, GPSIMD10)
-        round_on_scalar(raw10[1], GPSIMD10, grouped10, GPSIMD10, GROUPS)
+        grouped10 = new_grouped(1, 0, held)
+        round_on_scalar(raw10[0], 0, grouped10, 0, WA10_CUT)
+        round_on_scalar(raw10[1], WA10_CUT, grouped10, WA10_CUT, GROUPS)
         hb_banks = [project_b(1, c) for c in range(CHUNKS)]
         grouped11 = new_grouped(1, 1, held)
         round_on_gpsimd(raw11[0], grouped11, 0, GPSIMD11)
         round_on_scalar(raw11[1], GPSIMD11, grouped11, GPSIMD11, GROUPS)
-        quantise_wa(1, 0, [grouped10], placed(RAW11_GPSIMD_AT))
-        quantise_wa(1, 1, [grouped11], held)
+        quantise_wa(1, 0, grouped10, placed(RAW11_GPSIMD_AT))
+        quantise_wa(1, 1, grouped11, held)
         new_h(1, 0, J, held)
         h_scale[0] = placed(RAW11_GPSIMD_AT + 2 * KIB)([P, J], U8, "h_scale0")
         h_codes[0] = placed(RAW11_AT)([P, J], U32, "h_codes0")

@@ -36,7 +36,7 @@ SCORE_RANGES = ((0, 256), (256, 512), (512, 768), (768, 896), (896, 1024))
 HB_BANKS = ((0, 1, 2, 3, 4, 5, 6, 7), (4, 5, 6, 7, 0, 1, 2, 3))
 HA_BANKS = ((0, 1, 2, 3, 0, 1, 2, 3), HB_BANKS[1])
 SCORE_BANKS = tuple(HB_BANKS[1][c] for c in (0, 2, 4, 5, 6))
-STORE_FROM = {hi: lo for lo, hi in SCORE_RANGES}
+STORE_FROM = {512: 0, 768: 512, 896: 768, 1024: 896}
 KIB = 1024
 RAW01_AT = 0
 RAW11_AT = 56 * KIB
@@ -73,8 +73,11 @@ def tile_list_kg_mul_none_kernel(
         wb_scale_raw = held([P, R], U8, "wb_scale_raw")
         tab_scale = [held([P, J], U8, "tab_scale%d" % a) for a in range(2)]
         en_scale = held([P, 2, N], U8, "en_scale")
-        nc.gpsimd.memset(tab2_scale_win[:].bitcast(I32), 0)
-        nc.vector.memset(wb_scale_raw[:].bitcast(I32), 0)
+        tab2_scale = held([P, J], U8, "tab2_scale")
+        nc.vector.memset(tab2_scale_win[0:96, :].bitcast(I32), 0)
+        nc.vector.memset(tab2_scale_win[96 : P - ROWS, :].bitcast(I32), 0)
+        nc.gpsimd.memset(tab2_scale[:].bitcast(I32), 0)
+        nc.gpsimd.memset(wb_scale_raw[:].bitcast(I32), 0)
         nc.vector.memset(tab_scale_win[0 : P - 2 * ROWS, :].bitcast(I32), 0)
         for a in range(2):
             nc.vector.memset(tab_scale[a][:].bitcast(I32), 0)
@@ -99,8 +102,8 @@ def tile_list_kg_mul_none_kernel(
             return lst[:, lo // LIST_GROUP : hi // LIST_GROUP]
 
         nc.sync.dma_start(list2[:], offs2)
+        nc.sync.dma_start(tab2_scale_win[P - ROWS : P, :].bitcast(I32), tab2_scales[0].bitcast(I32))
         nc.sync.dma_start(list1[:], offs)
-        load_scale_rows(tab2_scale_win, TAB2_ROW, QUAD, tab2_scales[0].rearrange("(q e) t -> e q t", e=4))
         tab2_win = held([P, T], I32, "tab2_win")
         nc.sync.dma_start(tab2_win[:], as_words(tab2_words[0]))
         nc.sync.dma_start(
@@ -109,6 +112,9 @@ def tile_list_kg_mul_none_kernel(
         wb_raw = [load_wb(0, placed(WB0_AT))]
         load_scale_rows(wb_scale_raw, WB_ROW, QUAD, wb_scales[0].rearrange("(q e) r -> e q r", e=4))
         raw00 = load_wa(0, 0, 0, GROUPS, placed(RAW00_AT))
+        tab2_scale_picked = held([P, J], U8, "tab2_scale_picked")
+        nc.vector.tensor_copy(tab2_scale_picked[:], tab2_scale_win[:].indirect(list2[:]))
+        load_scale_rows(tab2_scale, TAB2_ROW, QUAD, [tab2_scale_picked[P - ROWS + e : P : 4, :] for e in range(4)])
         tab_win = held([P, T], I32, "tab_win")
         nc.sync.dma_start(tab_win[:], as_words(tab_words[0]))
         raw01 = [load_wa(0, 1, 0, GROUPS // 2, held)]
@@ -129,8 +135,6 @@ def tile_list_kg_mul_none_kernel(
             nc.vector.tensor_copy(codes[:], tab2_win[:].bitcast(U32).indirect(part_of(list2, h * HALF, (h + 1) * HALF)))
             tab2_codes.append(codes)
 
-        tab2_scale = held([P, J], U8, "tab2_scale")
-        nc.vector.tensor_copy(tab2_scale[:], tab2_scale_win[:].indirect(list2[:]))
         gather_tab2(0, held)
         tab_scale_picked = placed(RAW00_AT + 17 * KIB // 2)([P, J], U8, "tab_scale_picked")
         nc.vector.tensor_copy(tab_scale_picked[:], tab_scale_win[:].indirect(list1[:]))

@@ -31,7 +31,7 @@ WB_ROW = 8
 HB0_EARLY = 4
 GPSIMD00 = 80
 WA10_CUT = 32
-GPSIMD11 = 56
+GPSIMD11 = 52
 SCORE_RANGES = ((0, 256), (256, 512), (512, 768), (768, 896), (896, 1024))
 HB_BANKS = ((0, 1, 2, 3, 4, 5, 6, 7), (4, 5, 6, 7, 0, 1, 2, 3))
 HA_BANKS = ((0, 1, 2, 3, 0, 1, 2, 3), HB_BANKS[1])
@@ -301,8 +301,7 @@ def tile_list_kg_mul_none_kernel(
         h_scale[0] = placed(RAW11_GPSIMD_AT + 2 * KIB)([P, J], U8, "h_scale0")
         h_codes[0] = placed(RAW11_AT)([P, J], U32, "h_codes0")
         h_codes[1] = held([P, J], U32, "h_codes1")
-        for lo in range(0, J, HALF):
-            quantise_h(0, lo, lo + HALF)
+        quantise_h(0, 0, J)
 
         hb1 = placed(RAW11_AT + 4 * KIB)([P, CHUNKS, JC, PACK], F32, "hb1")
         hb = [copy_out(hb_banks[c], hb1[:, c]) for c in range(CHUNKS)]

from contextlib import ExitStack

import concourse.mybir as mybir

K, L, R, N, T, J = 1024, 512, 1024, 256, 2048, 1024
FLOPS = 2 * J * R * (K + L + N)

F32 = mybir.dt.float32
BF16 = mybir.dt.bfloat16
I32 = mybir.dt.int32
U32 = mybir.dt.uint32
U16 = mybir.dt.uint16
U8 = mybir.dt.uint8
FP8X4 = mybir.dt.float8_e4m3fn_x4
FP4X4 = mybir.dt.float4_e2m1fn_x4
MULT = mybir.AluOpType.mult
ADD = mybir.AluOpType.add

P = 128
PACK = 4
PASS = P * PACK
QUAD = 32
ROWS = 16
LIST_GROUP = 16
HALF = J // 2
JC = 128
CHUNKS = J // JC
GROUPS = PASS // PACK
TAB2_ROW = 4
WB_ROW = 8
HB0_EARLY = 4
GPSIMD00 = 80
WA10_CUT = 32
GPSIMD11 = 52
SCORE_RANGES = ((0, 256), (256, 512), (512, 768), (768, 896), (896, 1024))
HB_BANKS = ((0, 1, 2, 3, 4, 5, 6, 7), (4, 5, 6, 7, 0, 1, 2, 3))
HA_BANKS = ((0, 1, 2, 3, 0, 1, 2, 3), HB_BANKS[1])
SCORE_BANKS = tuple(HB_BANKS[1][c] for c in (0, 2, 4, 5, 6))
STORE_FROM = {512: 0, 768: 512, 896: 768, 1024: 896}
KIB = 1024
RAW01_AT = 0
RAW11_AT = 56 * KIB
WB0_AT = 80 * KIB
RAW11_GPSIMD_AT = 20 * KIB
RAW00_AT = 28 * KIB
HA1_LEAD = 3


def as_words(dram_pass):
    return dram_pass.rearrange("p n i -> p (n i)").bitcast(I32)


def tile_list_kg_mul_none_kernel(
    tc, tab_words, tab_scales, tab2_words, tab2_scales, wa, wb_words, wb_scales, en_words, en_scales, offs, offs2, out
):
    nc = tc.nc
    with ExitStack() as ctx:
        lists = ctx.enter_context(tc.tile_pool(name="lists", bufs=1))
        keep = ctx.enter_context(tc.tile_pool(name="keep", bufs=1))
        shared = ctx.enter_context(tc.tile_pool(name="shared", bufs=1))
        psum = ctx.enter_context(tc.psum_pool(name="psum", bufs=1))

        def held(shape, dtype, name):
            return keep.tile(shape, dtype, name=name, align_bytes=64)

        def placed(offset):
            return lambda shape, dtype, name: shared.tile(shape, dtype, name=name, offset=offset, align_bytes=64)

        list1 = lists.tile([P, J // LIST_GROUP], U16, name="list1")
        list2 = lists.tile([P, J // LIST_GROUP], U16, name="list2")
        tab_scale_win = held([P, T], U8, "tab_scale_win")
        tab2_scale_win = held([P, T], U8, "tab2_scale_win")
        wb_scale_raw = held([P, R], U8, "wb_scale_raw")
        tab_scale = [held([P, J], U8, "tab_scale%d" % a) for a in range(2)]
        en_scale = held([P, 2, N], U8, "en_scale")
        tab2_scale = held([P, J], U8, "tab2_scale")
        nc.vector.memset(tab2_scale_win[0:96, :].bitcast(I32), 0)
        nc.vector.memset(tab2_scale_win[96 : P - ROWS, :].bitcast(I32), 0)
        nc.gpsimd.memset(tab2_scale[:].bitcast(I32), 0)
        nc.gpsimd.memset(wb_scale_raw[:].bitcast(I32), 0)
        nc.vector.memset(tab_scale_win[0 : P - 2 * ROWS, :].bitcast(I32), 0)
        for a in range(2):
            nc.vector.memset(tab_scale[a][:].bitcast(I32), 0)
        nc.gpsimd.memset(en_scale[:].bitcast(I32), 0)

        def load_wa(b, a, lo, hi, make):
            raw = make([P, PACK, PACK * (hi - lo)], F32, "wa_raw%d%d_%d" % (b, a, lo))
            rows = wa[a * PASS : (a + 1) * PASS, b * PASS + PACK * lo : b * PASS + PACK * hi]
            nc.sync.dma_start(raw[:], rows.rearrange("(p i) c -> p i c", i=PACK))
            return raw

        def load_wb(b, make):
            raw = make([P, PASS], I32, "wb_raw%d" % b)
            nc.sync.dma_start(raw[:], as_words(wb_words[0])[:, b * PASS : (b + 1) * PASS])
            return raw

        def load_scale_rows(plane, first_row, step, rows):
            for e in range(4):
                nc.sync.dma_start(plane[first_row + e : P : step].bitcast(I32), rows[e].bitcast(I32))

        def part_of(lst, lo, hi):
            return lst[:, lo // LIST_GROUP : hi // LIST_GROUP]

        nc.sync.dma_start(list2[:], offs2)
        nc.sync.dma_start(tab2_scale_win[P - ROWS : P, :].bitcast(I32), tab2_scales[0].bitcast(I32))
        nc.sync.dma_start(list1[:], offs)
        tab2_win = held([P, T], I32, "tab2_win")
        nc.sync.dma_start(tab2_win[:], as_words(tab2_words[0]))
        nc.sync.dma_start(
            tab_scale_win[P - 2 * ROWS : P, :].bitcast(I32), tab_scales.rearrange("a g t -> (a g) t").bitcast(I32)
        )
        wb_raw = [load_wb(0, placed(WB0_AT))]
        load_scale_rows(wb_scale_raw, WB_ROW, QUAD, wb_scales[0].rearrange("(q e) r -> e q r", e=4))
        raw00 = load_wa(0, 0, 0, GROUPS, placed(RAW00_AT))
        tab2_scale_picked = held([P, J], U8, "tab2_scale_picked")
        nc.vector.tensor_copy(tab2_scale_picked[:], tab2_scale_win[:].indirect(list2[:]))
        load_scale_rows(tab2_scale, TAB2_ROW, QUAD, [tab2_scale_picked[P - ROWS + e : P : 4, :] for e in range(4)])
        tab_win = held([P, T], I32, "tab_win")
        nc.sync.dma_start(tab_win[:], as_words(tab_words[0]))
        raw01 = [load_wa(0, 1, 0, GROUPS // 2, held)]

        wb_codes = {}

        def reorder_wb(copy, b, make):
            wb_codes[b] = make([P, PASS], U32, "wb_codes%d" % b)
            copy(
                wb_codes[b][:].rearrange("p (t c m) -> p c t m", t=PACK, m=4),
                wb_raw[b][:].bitcast(U32).rearrange("p (c m t) -> p c t m", t=PACK, m=4),
            )

        tab2_codes = []

        def gather_tab2(h, make):
            codes = make([P, HALF], U32, "tab2_codes%d" % h)
            nc.vector.tensor_copy(codes[:], tab2_win[:].bitcast(U32).indirect(part_of(list2, h * HALF, (h + 1) * HALF)))
            tab2_codes.append(codes)

        gather_tab2(0, held)
        tab_scale_picked = placed(RAW00_AT + 17 * KIB // 2)([P, J], U8, "tab_scale_picked")
        nc.vector.tensor_copy(tab_scale_picked[:], tab_scale_win[:].indirect(list1[:]))
        reorder_wb(nc.scalar.copy, 0, held)
        gather_tab2(1, placed(WB0_AT))

        def move_tab_rows(a):
            first = P - 2 * ROWS + a * ROWS
            load_scale_rows(tab_scale[a], 0, QUAD, [tab_scale_picked[first + e : first + ROWS : 4, :] for e in range(4)])

        move_tab_rows(0)
        raw01.append(load_wa(0, 1, GROUPS // 2, GROUPS, placed(RAW01_AT)))
        wb_raw.append(load_wb(1, held))
        raw10 = [load_wa(1, 0, 0, WA10_CUT, held)]
        move_tab_rows(1)
        raw10.append(load_wa(1, 0, WA10_CUT, GROUPS, held))
        raw11 = [load_wa(1, 1, 0, GPSIMD11, placed(RAW11_GPSIMD_AT)), load_wa(1, 1, GPSIMD11, GROUPS, placed(RAW11_AT))]
        en_codes = held([P, 2, N], I32, "en_codes")
        nc.sync.dma_start(en_codes[:], en_words.rearrange("a p n i -> p a (n i)").bitcast(I32))
        load_scale_rows(en_scale, 0, QUAD, en_scales.rearrange("a (q e) n -> e q a n", e=4))

        wb_scale = held([P, R], U8, "wb_scale")
        nc.gpsimd.tensor_copy(
            wb_scale[:].rearrange("p (b t c m) -> p b c t m", b=2, t=PACK, m=16),
            wb_scale_raw[:].rearrange("p (b c m t) -> p b c t m", b=2, t=PACK, m=16),
        )

        def round_on_scalar(raw, at, grouped, lo, hi):
            src = raw[:].rearrange("p i (m t) -> p m i t", t=PACK)
            dst = grouped[:].rearrange("p (t m i) -> p m i t", t=PACK, i=PACK)
            nc.scalar.copy(dst[:, lo:hi], src[:, lo - at : hi - at])

        def round_on_gpsimd(raw, grouped, lo, hi):
            src = raw[:].rearrange("p i (m t) -> p t m i", t=PACK)
            dst = grouped[:].rearrange("p (t m i) -> p t m i", t=PACK, i=PACK)
            nc.gpsimd.tensor_scalar(dst[:, :, lo:hi], src[:, :, lo:hi], 1.0, 0.0, MULT, ADD)

        wa_codes, wa_scale = {}, {}

        def quantise_wa(b, a, grouped, make):
            wa_codes[b, a] = make([P, PASS], U32, "wa_codes%d%d" % (b, a))
            wa_scale[b, a] = held([P, PASS], U8, "wa_scale%d%d" % (b, a))
            nc.vector.quantize_mx(out=wa_codes[b, a][:].bitcast(FP8X4), scales=wa_scale[b, a][:], in_=grouped[:])

        def new_grouped(b, a, make):
            return make([P, PASS * PACK], BF16, "wa_grouped%d%d" % (b, a))

        tab_codes = {}

        def gather_tab(lo, hi, make):
            pairs = make([P, hi - lo], U32, "tab_pairs%d" % lo)
            nc.vector.tensor_copy(pairs[:], tab_win[:].bitcast(U32).indirect(part_of(list1, lo, hi)))
            return pairs

        def part_tab(lo, hi, pairs, make):
            parted = make([P, 2, 2 * (hi - lo)], U8, "tab_codes%d" % lo)
            nc.vector.tensor_copy(parted[:].bitcast(U16), pairs[:].bitcast(U16).rearrange("p (j d) -> p d j", d=2))
            for j0 in range(lo, hi, JC):
                tab_codes[j0 // JC] = parted[:, :, 2 * (j0 - lo) : 2 * (j0 - lo + JC)]

        def bank_tile(n, shape):
            return psum.tile(shape, F32, name="bank", tag="bank%d" % n)

        def by_query(bank):
            return bank[:].rearrange("p t j -> p j t")

        def project_a(b, c):
            bank = bank_tile(HA_BANKS[b][c], [P, PACK, JC])
            for a in range(2):
                for t in range(PACK):
                    cols = slice(t * P, (t + 1) * P)
                    nc.tensor.matmul_mx(
                        out=bank[:, t, :],
                        lhsT=wa_codes[b, a][:, cols].bitcast(FP8X4),
                        lhsT_scale=wa_scale[b, a][:, cols],
                        rhs=tab_codes[c][:, a, :].bitcast(FP4X4),
                        rhs_scale=tab_scale[a][:, c * JC : (c + 1) * JC],
                        start=(a == 0 and t == 0),
                        stop=(a == 1 and t == PACK - 1),
                    )
            return bank

        def project_b(b, c):
            bank = bank_tile(HB_BANKS[b][c], [P, PACK, JC])
            h, j0 = divmod(c * JC, HALF)
            for t in range(PACK):
                cols = slice(t * P, (t + 1) * P)
                nc.tensor.matmul_mx(
                    out=bank[:, t, :],
                    lhsT=wb_codes[b][:, cols].bitcast(FP8X4),
                    lhsT_scale=wb_scale[WB_ROW:P, b * PASS + t * P : b * PASS + (t + 1) * P],
                    rhs=tab2_codes[h][:, j0 : j0 + JC].bitcast(FP8X4),
                    rhs_scale=tab2_scale[TAB2_ROW:P, c * JC : (c + 1) * JC],
                    start=True,
                    stop=True,
                )
            return bank

        def copy_out(bank, kept):
            nc.scalar.copy(kept, by_query(bank))
            return kept

        grouped00 = new_grouped(0, 0, held)
        round_on_gpsimd(raw00, grouped00, 0, GPSIMD00)
        round_on_scalar(raw00, 0, grouped00, GPSIMD00, GROUPS)

        hb_banks = [project_b(0, c) for c in range(CHUNKS)]
        hb_early = held([P, HB0_EARLY, JC, PACK], F32, "hb0_early")
        hb = [copy_out(hb_banks[c], hb_early[:, c]) for c in range(HB0_EARLY)]

        pairs = [gather_tab(0, HALF, held)]
        quantise_wa(0, 0, grouped00, held)
        part_tab(0, HALF, pairs[0], placed(RAW00_AT))
        pairs.append(gather_tab(HALF, J, placed(RAW00_AT + 6 * KIB)))

        grouped01 = new_grouped(0, 1, held)
        round_on_scalar(raw01[0], 0, grouped01, 0, GROUPS // 2)
        round_on_scalar(raw01[1], GROUPS // 2, grouped01, GROUPS // 2, GROUPS)
        quantise_wa(0, 1, grouped01, placed(RAW00_AT + 2 * KIB))
        part_tab(HALF, J, pairs[1], placed(RAW01_AT))
        hb_late = placed(RAW01_AT + 2 * KIB)([P, CHUNKS - HB0_EARLY, JC, PACK], F32, "hb0_late")
        for c in range(HB0_EARLY, CHUNKS):
            hb.append(copy_out(hb_banks[c], hb_late[:, c - HB0_EARLY]))
        reorder_wb(nc.gpsimd.tensor_copy, 1, placed(RAW00_AT + 15 * KIB // 2))

        h_bf16 = {}

        def new_h(b, lo, hi, make):
            tile = make([P, hi - lo, PACK], BF16, "h_bf16_%d_%d" % (b, lo))
            for j0 in range(lo, hi, JC):
                h_bf16[b, j0] = (tile, lo)

        def h_cols(b, lo, hi):
            tile, at = h_bf16[b, lo]
            return tile[:, lo - at : hi - at, :]

        h_scale = {1: held([P, J], U8, "h_scale1")}
        h_codes = {}

        def join(b, c, bank, kept):
            nc.vector.tensor_tensor(h_cols(b, c * JC, (c + 1) * JC), by_query(bank), kept, MULT)

        def quantise_h(b, lo, hi):
            nc.vector.quantize_mx(
                out=h_codes[b][:, lo:hi].bitcast(FP8X4),
                scales=h_scale[b][:, lo:hi],
                in_=h_cols(b, lo, hi).rearrange("p j t -> p (j t)"),
            )

        new_h(0, 0, J, held)
        for c in range(CHUNKS):
            join(0, c, project_a(0, c), hb[c])

        grouped10 = new_grouped(1, 0, held)
        round_on_scalar(raw10[0], 0, grouped10, 0, WA10_CUT)
        round_on_scalar(raw10[1], WA10_CUT, grouped10, WA10_CUT, GROUPS)
        hb_banks = [project_b(1, c) for c in range(CHUNKS)]
        grouped11 = new_grouped(1, 1, held)
        round_on_gpsimd(raw11[0], grouped11, 0, GPSIMD11)
        round_on_scalar(raw11[1], GPSIMD11, grouped11, GPSIMD11, GROUPS)
        quantise_wa(1, 0, grouped10, placed(RAW11_GPSIMD_AT))
        quantise_wa(1, 1, grouped11, held)
        new_h(1, 0, J, held)
        h_scale[0] = placed(RAW11_GPSIMD_AT + 2 * KIB)([P, J], U8, "h_scale0")
        h_codes[0] = placed(RAW11_AT)([P, J], U32, "h_codes0")
        h_codes[1] = held([P, J], U32, "h_codes1")
        quantise_h(0, 0, J)

        hb1 = placed(RAW11_AT + 4 * KIB)([P, CHUNKS, JC, PACK], F32, "hb1")
        hb = [copy_out(hb_banks[c], hb1[:, c]) for c in range(CHUNKS)]
        ha = [project_a(1, c) for c in range(HA1_LEAD)]

        out_rows = out.rearrange("(u p) j -> p u j", p=P)
        result = held([P, 2, J], F32, "result")

        def finish(n):
            lo, hi = SCORE_RANGES[n]
            bank = bank_tile(SCORE_BANKS[n], [P, 2, hi - lo])
            for b in range(2):
                for u in range(2):
                    cols = slice(u * P, (u + 1) * P)
                    nc.tensor.matmul_mx(
                        out=bank[:, u, :],
                        lhsT=en_codes[:, b, cols].bitcast(FP8X4),
                        lhsT_scale=en_scale[:, b, cols],
                        rhs=h_codes[b][:, lo:hi].bitcast(FP8X4),
                        rhs_scale=h_scale[b][:, lo:hi],
                        start=(b == 0 and u == 0),
                        stop=(b == 1 and u == 1),
                    )
            nc.scalar.copy(result[:, :, lo:hi], bank[:])
            if hi in STORE_FROM:
                nc.sync.dma_start(out_rows[:, :, STORE_FROM[hi] : hi], result[:, :, STORE_FROM[hi] : hi])

        ends = {hi // JC: n for n, (lo, hi) in enumerate(SCORE_RANGES)}
        for c in range(CHUNKS + 1):
            if c + HA1_LEAD < CHUNKS:
                ha.append(project_a(1, c + HA1_LEAD))
            if c < CHUNKS:
                join(1, c, ha[c], hb[c])
            if c in ends:
                quantise_h(1, *SCORE_RANGES[ends[c]])
                finish(ends[c])
